import numpy as np
import ml_dtypes


def mxq(x, axis, fmt="e4m3"):
    dtype, down = {"e4m3": (ml_dtypes.float8_e4m3fn, 7), "e5m2": (ml_dtypes.float8_e5m2, 14)}[fmt]
    v = np.moveaxis(np.asarray(x, np.float32).astype(ml_dtypes.bfloat16).astype(np.float64), axis, -1)
    blocks = v.reshape(v.shape[:-1] + (-1, 32))
    amax = np.abs(blocks).max(-1, keepdims=True)
    byte = np.maximum(np.where(amax > 0, np.frexp(amax)[1] - 1 + 127, 0) - down, 1)
    scale = np.exp2(byte - 127.0)
    codes = (blocks / scale).astype(np.float32).astype(dtype).astype(np.float64)
    return np.moveaxis((codes * scale).reshape(v.shape), -1, axis)


WIDE = False


def mx_kscale(k):
    if not WIDE:
        return np.ones(k)
    levels = np.array([10, -10, 5, -5, 0])
    if k % 512:
        return np.exp2(np.random.permutation(np.resize(levels, k // 32))).repeat(32)
    a = np.empty((k // 512, 16))
    for p in range(k // 512):
        a[p, :8] = np.random.permutation(np.resize(levels, 8))
        for g in range(8):
            far = levels[np.abs(levels - a[p, g]) >= 10]
            a[p, g + 8] = far[np.random.randint(len(far))]
    return np.exp2(a.ravel()).repeat(32)


BF16 = ml_dtypes.bfloat16


def bf(x):
    return np.asarray(x, np.float32).astype(BF16)


def f64(x):
    return np.asarray(x).astype(np.float64)


E2M1 = np.array([0.0, 0.5, 1.0, 1.5, 2.0, 3.0, 4.0, 6.0, -0.0, -0.5, -1.0, -1.5, -2.0, -3.0, -4.0, -6.0])


def pack_weight(w, fmt):
    k, n = w.shape
    w = f64(bf(w)).reshape(k // 32, 32, n)
    amax = np.abs(w).max(1)
    if fmt == "e4m3":
        byte = np.frexp(amax)[1] - 1 + 127 - 7
    else:
        mant, ex = np.frexp(amax / 6.0)
        byte = np.where(mant > 0.5, ex, ex - 1) + 127
    byte = np.clip(np.where(amax > 0, byte, 1), 1, 254)
    scaled = (w * np.exp2(127.0 - byte)[:, None, :]).reshape(k, n).astype(np.float32)
    by_word = np.ascontiguousarray(scaled.reshape(k // 512, 128, 4, n).transpose(0, 1, 3, 2))
    if fmt == "e4m3":
        words = by_word.astype(ml_dtypes.float8_e4m3fn).view(np.uint8)
    else:
        c = by_word.astype(ml_dtypes.float4_e2m1fn).view(np.uint8) & 0xF
        words = c[..., 0::2] | (c[..., 1::2] << 4)
    return np.ascontiguousarray(words), np.ascontiguousarray(byte.astype(np.uint8).reshape(k // 512, 16, n))


def unpack_weight(words, scales, fmt):
    g, p, n, _ = words.shape
    if fmt == "e4m3":
        vals = np.ascontiguousarray(words).view(ml_dtypes.float8_e4m3fn).astype(np.float64)
    else:
        nib = np.empty((g, p, n, 4), np.uint8)
        nib[..., 0::2] = words & 0xF
        nib[..., 1::2] = words >> 4
        vals = E2M1[nib]
    vals = vals * np.repeat(np.exp2(scales.astype(np.float64) - 127.0), 8, axis=1)[..., None]
    return vals.transpose(0, 1, 3, 2).reshape(g * 512, n)
def pack4(w):
    words, scales = pack_weight(w, "e2m1")
    return words.reshape(words.shape[0], 128, -1), scales


def unpack4(words, scales):
    return unpack_weight(words.reshape(words.shape[0], 128, -1, 2), scales, "e2m1")


D, R, L = 4096, 1024, 512


def draw0():
    s = mx_kscale(D)
    t = mx_kscale(R)
    u = np.random.standard_normal((D, R)) / np.sqrt(D)
    cal = 1 + 0.1 * np.random.standard_normal(D)
    load = 0.5 + 0.5 * np.random.random(R)
    v_words, v_scales = pack4(u.T / t[:, None])
    return {"x": bf(np.random.standard_normal((D, L)) * s[:, None]),
            "g": bf(cal / s),
            "p": bf(u.T * cal / s),
            "a": bf(load * t),
            "v_words": v_words,
            "v_scales": v_scales}


def core(x, g, p, a, v_words, v_scales):
    x = f64(x)
    c = mxq(f64(p), 1, "e4m3") @ mxq(x, 0, "e4m3")
    c = c * f64(a)[:, None]
    clutter = unpack4(v_words, v_scales).T @ mxq(c, 0, "e4m3")
    return x * f64(g)[:, None] - clutter


def e4m3fn_bytes(y):
    return np.clip(np.asarray(y, np.float64), -448.0, 448.0).astype(np.float32).astype(ml_dtypes.float8_e4m3fn).view(np.uint8)


def e4m3fn_values(b):
    return np.asarray(b, np.uint8).view(ml_dtypes.float8_e4m3fn).astype(np.float64)


def setup_inputs():
    d = draw0()
    x0 = np.asarray(d['p']).astype(np.float64)
    s = (np.max(np.abs(x0), axis=(0,), keepdims=True) / 448.0).astype(np.float32)
    out = {}
    for k, v in d.items():
        if k == 'p':
            out['p_bytes'] = e4m3fn_bytes(x0 / s.astype(np.float64))
            out['p_scale'] = s
        else:
            out[k] = v
    return out


def reference(x, g, p_bytes, p_scale, a, v_words, v_scales):
    return core(x, g, e4m3fn_values(p_bytes) * p_scale.astype(np.float64), a, v_words, v_scales)

@@ -1,0 +1,347 @@
+from contextlib import ExitStack
+
+import concourse.mybir as mybir
+from concourse.masks import make_identity
+
+D, R, L = 4096, 1024, 512
+FLOPS = 4 * D * R * L
+
+F32 = mybir.dt.float32
+BF16 = mybir.dt.bfloat16
+I32 = mybir.dt.int32
+U32 = mybir.dt.uint32
+U8 = mybir.dt.uint8
+E4M3 = mybir.dt.float8_e4m3fn
+E4M3X4 = mybir.dt.float8_e4m3fn_x4
+E2M1X4 = mybir.dt.float4_e2m1fn_x4
+MULT = mybir.AluOpType.mult
+SUB = mybir.AluOpType.subtract
+COPY = mybir.ActivationFunctionType.Copy
+
+P = 128
+PACK = 4
+KP = P * PACK
+NC = D // KP
+NG = R // KP
+NT = D // P
+WIDE = 5
+STEPS = NC + 2 * (2 * PACK - WIDE)
+LAST = STEPS - 1
+
+
+def units_of(s):
+    if s < NC:
+        return [(r, s) for r in range(WIDE)]
+    r, h = WIDE + (s - NC) // 2, (s - NC) % 2
+    return [(r, 4 * h + j) for j in range(4)]
+
+
+def tile_stap_clutter_removal_s13_kernel(tc, x, g, p_bytes, p_scale, a, v_words, v_scales, out):
+    nc = tc.nc
+    with ExitStack() as ctx:
+        keep = ctx.enter_context(tc.tile_pool(name="keep", bufs=1))
+        work = ctx.enter_context(tc.tile_pool(name="work", bufs=3))
+        psum = ctx.enter_context(tc.psum_pool(name="psum", bufs=4))
+        ctx.enter_context(tc.manual_schedule())
+
+        ident = keep.tile([P, P], F32, name="ident")
+        make_identity(nc, ident[:])
+        vs = keep.tile([P, NG, D], U8, name="vs", align_bytes=64)
+        nc.vector.memset(vs[:].rearrange("p g n -> p (g n)").bitcast(I32), 0)
+        g_rows = keep.tile([P, P], F32, name="g_rows")
+        nc.vector.memset(g_rows[:], 0.0)
+
+        p_by = p_bytes.rearrange("(g m t) k -> g m t k", g=NG, t=PACK)
+        sc = keep.tile([P, D], F32, name="sc", align_bytes=64)
+        pb0, pb4, xr = {}, {}, {}
+
+        def load_scale(c):
+            ks = slice(KP * c, KP * (c + 1))
+            nc.sync.dma_start(out=sc[:, ks], in_=p_scale[:, ks].rearrange("o k -> (o k)").partition_broadcast(P))
+
+        def load_p(c0, c1):
+            t0 = keep.tile([P, PACK, KP * (c1 - c0)], U8, name="pb0_%d" % c0, align_bytes=64)
+            nc.sync.dma_start(out=t0[:], in_=p_by[0][:, :, KP * c0 : KP * c1])
+            t4 = keep.tile([P, KP * (c1 - c0)], U8, name="pb4_%d" % c0, align_bytes=64)
+            nc.sync.dma_start(out=t4[:], in_=p_by[1][:, 0, KP * c0 : KP * c1])
+            for c in range(c0, c1):
+                pb0[c] = (t0, KP * (c - c0))
+                pb4[c] = (t4, KP * (c - c0))
+
+        def load_x(c):
+            t = work.tile([P, PACK, L], BF16, name="xr_%d" % c, tag="xr", bufs=8, align_bytes=64)
+            nc.sync.dma_start(out=t[:], in_=x[KP * c : KP * (c + 1), :].rearrange("(p j) l -> p j l", j=PACK))
+            xr[c] = t
+
+        load_scale(0)
+        load_p(0, 1)
+        load_x(0)
+        load_scale(1)
+        load_p(1, 2)
+        load_x(1)
+        load_scale(2)
+        load_p(2, 4)
+        load_x(2)
+        load_scale(3)
+        load_x(3)
+        load_scale(4)
+        load_p(4, 8)
+        for c in range(4, NC):
+            load_x(c)
+            if c + 1 < NC:
+                load_scale(c + 1)
+        a_bf = keep.tile([P, NG, PACK], BF16, name="a_bf")
+        nc.sync.dma_start(out=a_bf[:], in_=a.rearrange("(g m t) -> m g t", g=NG, t=PACK))
+        g_bf = keep.tile([P, P], BF16, name="g_bf")
+        nc.sync.dma_start(out=g_bf[0:NT, :], in_=g.rearrange("(i p) -> i p", p=P))
+        pb1 = {}
+        for r in range(WIDE, 2 * PACK):
+            pb1[r] = keep.tile([P, D], U8, name="pb1_%d" % r, align_bytes=64)
+            nc.sync.dma_start(out=pb1[r][:], in_=p_by[1][:, r - PACK, :])
+        for q in range(4):
+            nc.sync.dma_start(
+                out=vs[32 * q : 32 * q + 4, :, :].bitcast(I32),
+                in_=v_scales[:, 4 * q : 4 * q + 4, :].rearrange("g q n -> q g n").bitcast(I32),
+            )
+        vw = keep.tile([P, NG, 2 * D], U8, name="vw", align_bytes=64)
+        for gg in range(NG):
+            nc.sync.dma_start(out=vw[:, gg, :].bitcast(I32), in_=v_words[gg].bitcast(I32))
+        xn = []
+        for j in range(8):
+            t = work.tile([P, 4, L], BF16, name="xn_%d" % j, tag="xr", bufs=8, align_bytes=64)
+            nc.sync.dma_start(out=t[:], in_=x[512 * j : 512 * (j + 1), :].rearrange("(i p) l -> p i l", p=P))
+            xn.append(t)
+
+        xq = keep.tile([P, NC, L], U32, name="xq", align_bytes=64)
+        xs = keep.tile([P, NC, L], U8, name="xs", align_bytes=64)
+        hq = keep.tile([P, NG, L], U32, name="hq", align_bytes=64)
+        hs = keep.tile([P, NG, L], U8, name="hs", align_bytes=64)
+        hg1 = keep.tile([P, L, PACK], BF16, name="hg1", align_bytes=64)
+        hg0 = keep.tile([P, L, PACK], BF16, name="hg0", align_bytes=64)
+        hp0 = keep.tile([P, PACK, L], BF16, name="hp0", align_bytes=64)
+        a_f = keep.tile([P, NG * PACK], F32, name="a_f")
+        g_f = keep.tile([P, NT], F32, name="g_f")
+
+        W, TR, PG, PQ, PS, XG, ACC = {}, {}, {}, {}, {}, {}, {}
+
+        def product(s, lo, hi):
+            units = units_of(s)
+            if s not in W:
+                W[s] = work.tile([P, WIDE * KP], BF16, name="w", tag="w", align_bytes=64)
+            for j in range(lo, hi):
+                r, c = units[j]
+                if r < PACK:
+                    t, off = pb0[c]
+                    src = t[:, r, off : off + KP]
+                elif r < WIDE:
+                    t, off = pb4[c]
+                    src = t[:, off : off + KP]
+                else:
+                    src = pb1[r][:, KP * c : KP * (c + 1)]
+                nc.vector.tensor_tensor(
+                    out=W[s][:, KP * j : KP * (j + 1)],
+                    in0=src.bitcast(E4M3),
+                    in1=sc[:, KP * c : KP * (c + 1)],
+                    op=MULT,
+                )
+
+        def transposes(s, b):
+            words = W[s][:].bitcast(F32)
+            tr = psum.tile([P, 2, 2, P], F32, name="tr", tag="tr", bufs=8 - WIDE)
+            for j in range(2 * b, min(2 * b + 2, len(units_of(s)))):
+                for u in range(2):
+                    nc.tensor.transpose(tr[:, j % 2, u, :], words[:, 256 * j + u : 256 * (j + 1) : 2], ident[:])
+            TR[(s, b)] = tr
+
+        def evac(s, lo, hi):
+            if s not in PG:
+                PG[s] = work.tile([P, WIDE, P, PACK], BF16, name="pg", tag="pg", align_bytes=64)
+            pw = PG[s][:].rearrange("p j m t -> p (j m t)").bitcast(F32)
+            pw = pw.rearrange("p (j m u) -> p j m u", j=WIDE, u=2)
+            b = lo // 2
+            nc.scalar.copy(
+                out=pw[:, lo:hi, :, :],
+                in_=TR[(s, b)][:, lo - 2 * b : hi - 2 * b, :, :].rearrange("p j u m -> p j m u"),
+            )
+
+        def quant_p(s, lo, hi):
+            if s not in PQ:
+                PQ[s] = work.tile([P, WIDE * P], U32, name="pq", tag="pq", align_bytes=64)
+                PS[s] = work.tile([P, WIDE * P], U8, name="ps", tag="ps", align_bytes=64)
+            nc.vector.quantize_mx(
+                out=PQ[s][:, P * lo : P * hi].bitcast(E4M3X4),
+                scales=PS[s][:, P * lo : P * hi],
+                in_=PG[s][:, lo:hi, :, :].rearrange("p j m t -> p (j m t)"),
+            )
+
+        def x_interleave(c, lo, hi):
+            if c not in XG:
+                XG[c] = work.tile([P, L, PACK], BF16, name="xg", tag="xg", align_bytes=64)
+            nc.scalar.copy(
+                out=XG[c][:, lo:hi, :].rearrange("p (c i) t -> p c t i", i=4),
+                in_=xr[c][:, :, lo:hi].rearrange("p t (c i) -> p c t i", i=4),
+            )
+
+        def quant_x(c):
+            nc.vector.quantize_mx(
+                out=xq[:, c, :].bitcast(E4M3X4), scales=xs[:, c, :], in_=XG[c][:].rearrange("p l t -> p (l t)")
+            )
+
+        def mm(s, lo, hi):
+            for j in range(lo, min(hi, len(units_of(s)))):
+                r, c = units_of(s)[j]
+                if c == 0:
+                    ACC[r] = psum.tile([P, L], F32, name="acc", tag="acc", bufs=WIDE)
+                nc.tensor.matmul_mx(
+                    out=ACC[r][:],
+                    lhsT=PQ[s][:, P * j : P * (j + 1)].bitcast(E4M3X4),
+                    lhsT_scale=PS[s][:, P * j : P * (j + 1)],
+                    rhs=xq[:, c, :].bitcast(E4M3X4),
+                    rhs_scale=xs[:, c, :],
+                    start=(c == 0),
+                    stop=(c == NC - 1),
+                )
+
+        def quant_h(gg, src):
+            nc.vector.quantize_mx(
+                out=hq[:, gg, :].bitcast(E4M3X4), scales=hs[:, gg, :], in_=src[:].rearrange("p l t -> p (l t)")
+            )
+
+        def h0_evac(t):
+            nc.scalar.activation(out=hp0[:, t, :], in_=ACC[t][:], func=COPY, scale=a_f[:, t : t + 1])
+
+        def h0_interleave(lo, hi):
+            nc.scalar.copy(
+                out=hg0[:, lo:hi, :].rearrange("p (c i) t -> p c t i", i=4),
+                in_=hp0[:, :, lo:hi].rearrange("p t (c i) -> p c t i", i=4),
+            )
+
+        def h1_scalar(t, lo, hi):
+            r = PACK + t
+            nc.scalar.activation(out=hg1[:, lo:hi, t], in_=ACC[r][:, lo:hi], func=COPY, scale=a_f[:, r : r + 1])
+
+        def h1_vector(t, lo, hi):
+            r = PACK + t
+            nc.vector.tensor_scalar(
+                out=hg1[:, lo:hi, t], in0=ACC[r][:, lo:hi], scalar1=a_f[:, r : r + 1], scalar2=None, op0=MULT
+            )
+
+        for s in range(STEPS):
+            wide = s < NC
+            product(s, 0, 2)
+            transposes(s, 0)
+            if s == NC + 2:
+                h0_evac(0)
+            if s >= 1:
+                n = len(units_of(s - 1))
+                evac(s - 1, 4 if n > 4 else 2, n)
+            if s == NC + 2:
+                h0_evac(1)
+            if s == NC + 3:
+                h0_evac(2)
+                h0_evac(3)
+            if wide:
+                x_interleave(s, 0, 256)
+            evac_late = s == LAST
+            if evac_late:
+                evac(s, 0, 1)
+                evac(s, 1, 2)
+            else:
+                evac(s, 0, 2)
+            if wide:
+                x_interleave(s, 256, 512)
+            if s == NC + 2:
+                h1_scalar(0, 0, 256)
+            if s == NC + 3:
+                h1_scalar(0, 256, 512)
+            if s == NC + 4:
+                h0_interleave(0, 512)
+            if s == NC + 5:
+                h1_scalar(1, 0, 512)
+            if s >= 2:
+                quant_p(s - 2, 0, 4)
+                if s - 2 < NC:
+                    quant_p(s - 2, 4, 5)
+                mm(s - 2, 0, 2)
+            product(s, 2, 4)
+            transposes(s, 1)
+            if wide:
+                evac(s, 2, 4)
+            if s >= 2:
+                mm(s - 2, 2, 4)
+            if wide:
+                product(s, 4, 5)
+                transposes(s, 2)
+                if s >= 2:
+                    mm(s - 2, 4, 5)
+            elif s - 2 < NC:
+                mm(s - 2, 4, 5)
+            if 1 <= s <= NC:
+                quant_x(s - 1)
+            if s == NC + 1:
+                nc.scalar.copy(out=a_f[:], in_=a_bf[:].rearrange("p g t -> p (g t)"))
+                nc.vector.tensor_copy(out=g_rows[0:NT, :], in_=g_bf[0:NT, :])
+        evac(LAST, 2, 3)
+        evac(LAST, 3, 4)
+        quant_p(LAST - 1, 0, 4)
+        mm(LAST - 1, 0, 4)
+        for j in range(2):
+            quant_p(LAST, j, j + 1)
+            mm(LAST, j, j + 1)
+        h1_scalar(2, 256, L)
+        quant_h(0, hg0)
+        h1_vector(2, 0, 256)
+        for j in range(2, 4):
+            quant_p(LAST, j, j + 1)
+            mm(LAST, j, j + 1)
+        h1_scalar(3, 256, L)
+        h1_vector(3, 0, 256)
+        quant_h(1, hg1)
+
+        Y = {}
+
+        def y_pass(i, gg):
+            if gg == 0:
+                tr = i % 8 < 8 - WIDE
+                Y[i] = psum.tile([P, L], F32, name="y", tag="tr" if tr else "acc", bufs=8 - WIDE if tr else WIDE)
+            nc.tensor.matmul_mx(
+                out=Y[i][:],
+                lhsT=vw[:, gg, 256 * i : 256 * (i + 1)].bitcast(E2M1X4),
+                lhsT_scale=vs[:, gg, P * i : P * (i + 1)],
+                rhs=hq[:, gg, :].bitcast(E4M3X4),
+                rhs_scale=hs[:, gg, :],
+                start=(gg == 0),
+                stop=(gg == NG - 1),
+            )
+
+        gt = psum.tile([P, P], F32, name="gt", tag="tr", bufs=8 - WIDE)
+        nc.tensor.transpose(gt[:], g_rows[:], ident[:])
+        nc.scalar.copy(out=g_f[:], in_=gt[:, 0:NT])
+
+        groups = [(0, 1), (1, 2)] + [(i, i + 2) for i in range(2, NT - 2, 2)] + [(NT - 2, NT - 1), (NT - 1, NT)]
+        first, end, o = {}, {}, None
+        for lo, hi in groups:
+            for i in range(lo, hi):
+                first[i], end[i] = lo, hi
+
+        for i in range(7):
+            y_pass(i, 0)
+        for i in range(NT):
+            y_pass(i, 1)
+            if i >= 1 and i + 6 < NT:
+                y_pass(i + 6, 0)
+            if i == first[i]:
+                o = work.tile([P, 2, L], F32, name="o", tag="o", bufs=6, align_bytes=64)
+            xi, gi, oi = xn[i // 4][:, i % 4, :], g_f[:, i : i + 1], o[:, i - first[i], :]
+            if i % 4 == 3 and i < NT - 4:
+                gx = work.tile([P, L], F32, name="gx", tag="gx", bufs=2)
+                ys = work.tile([P, L], F32, name="ys", tag="ys", bufs=2)
+                nc.scalar.activation(out=gx[:], in_=xi, func=COPY, scale=gi)
+                nc.scalar.copy(out=ys[:], in_=Y[i][:])
+                nc.gpsimd.tensor_tensor(out=oi, in0=gx[:], in1=ys[:], op=SUB)
+            else:
+                nc.vector.scalar_tensor_tensor(out=oi, in0=xi, scalar=gi, in1=Y[i][:], op0=MULT, op1=SUB)
+            if i == end[i] - 1:
+                nc.sync.dma_start(
+                    out=out[P * first[i] : P * end[i], :].rearrange("(i p) l -> p i l", p=P), in_=o[:, 0 : end[i] - first[i], :]
+                )

@@ -24,16 +24,18 @@ KP = P * PACK
 NC = D // KP
 NG = R // KP
 NT = D // P
-WIDE = 5
-STEPS = NC + 2 * (2 * PACK - WIDE)
+PAIRS = 3
+SWEEP = PAIRS * NC
+STEPS = SWEEP + NC
 LAST = STEPS - 1
+LAG = 3
+H_SPLIT = 320
 
 
-def units_of(s):
-    if s < NC:
-        return [(r, s) for r in range(WIDE)]
-    r, h = WIDE + (s - NC) // 2, (s - NC) % 2
-    return [(r, 4 * h + j) for j in range(4)]
+def step_of(n):
+    if n < SWEEP:
+        return n % PAIRS, n // PAIRS
+    return PAIRS, n - SWEEP
 
 
 def tile_stap_clutter_removal_s13_kernel(tc, x, g, p_bytes, p_scale, a, v_words, v_scales, out):
@@ -41,63 +43,54 @@ def tile_stap_clutter_removal_s13_kernel(tc, x, g, p_bytes, p_scale, a, v_words,
     with ExitStack() as ctx:
         keep = ctx.enter_context(tc.tile_pool(name="keep", bufs=1))
         work = ctx.enter_context(tc.tile_pool(name="work", bufs=3))
-        psum = ctx.enter_context(tc.psum_pool(name="psum", bufs=4))
+        psum = ctx.enter_context(tc.psum_pool(name="psum", bufs=1))
         ctx.enter_context(tc.manual_schedule())
+
+        def bank(b, shape):
+            return psum.tile(shape, F32, name="bank%d" % b, tag="bank%d" % b)
 
         ident = keep.tile([P, P], F32, name="ident")
         make_identity(nc, ident[:])
+        g_rows = keep.tile([P, P], F32, name="g_rows")
+        nc.gpsimd.memset(g_rows[:], 0.0)
         vs = keep.tile([P, NG, D], U8, name="vs", align_bytes=64)
         nc.vector.memset(vs[:].rearrange("p g n -> p (g n)").bitcast(I32), 0)
-        g_rows = keep.tile([P, P], F32, name="g_rows")
-        nc.vector.memset(g_rows[:], 0.0)
 
         p_by = p_bytes.rearrange("(g m t) k -> g m t k", g=NG, t=PACK)
-        sc = keep.tile([P, D], F32, name="sc", align_bytes=64)
-        pb0, pb4, xr = {}, {}, {}
+        PB, xr = {}, {}
 
-        def load_scale(c):
-            ks = slice(KP * c, KP * (c + 1))
-            nc.sync.dma_start(out=sc[:, ks], in_=p_scale[:, ks].rearrange("o k -> (o k)").partition_broadcast(P))
-
-        def load_p(c0, c1):
-            t0 = keep.tile([P, PACK, KP * (c1 - c0)], U8, name="pb0_%d" % c0, align_bytes=64)
-            nc.sync.dma_start(out=t0[:], in_=p_by[0][:, :, KP * c0 : KP * c1])
-            t4 = keep.tile([P, KP * (c1 - c0)], U8, name="pb4_%d" % c0, align_bytes=64)
-            nc.sync.dma_start(out=t4[:], in_=p_by[1][:, 0, KP * c0 : KP * c1])
-            for c in range(c0, c1):
-                pb0[c] = (t0, KP * (c - c0))
-                pb4[c] = (t4, KP * (c - c0))
+        def load_p(c, j0, j1):
+            gg, t0 = j0 // 2, 2 * (j0 % 2)
+            rows = 2 * (j1 - j0)
+            t = keep.tile([P, rows, KP], U8, name="pb_%d_%d" % (c, j0), align_bytes=64)
+            nc.sync.dma_start(out=t[:], in_=p_by[gg][:, t0 : t0 + rows, KP * c : KP * (c + 1)])
+            for j in range(j0, j1):
+                PB[(j, c)] = t[:, 2 * (j - j0) : 2 * (j - j0) + 2, :].rearrange("p r k -> p (r k)")
 
         def load_x(c):
             t = work.tile([P, PACK, L], BF16, name="xr_%d" % c, tag="xr", bufs=8, align_bytes=64)
             nc.sync.dma_start(out=t[:], in_=x[KP * c : KP * (c + 1), :].rearrange("(p j) l -> p j l", j=PACK))
             xr[c] = t
 
-        load_scale(0)
-        load_p(0, 1)
+        s4 = keep.tile([P, NC, 8], F32, name="s4")
+        a_bf = keep.tile([P, NG, 16], BF16, name="a_bf")
+        load_p(0, 0, 1)
+        nc.scalar.dma_start(out=s4[:, :, 0:PACK], in_=p_scale.rearrange("o (c p t) -> p (o c) t", p=P, t=PACK))
+        nc.scalar.dma_start(out=a_bf[:, :, 0:PACK], in_=a.rearrange("(g m t) -> m g t", g=NG, t=PACK))
+        load_p(0, 1, 2)
+        load_p(0, 2, 3)
         load_x(0)
-        load_scale(1)
-        load_p(1, 2)
-        load_x(1)
-        load_scale(2)
-        load_p(2, 4)
-        load_x(2)
-        load_scale(3)
-        load_x(3)
-        load_scale(4)
-        load_p(4, 8)
-        for c in range(4, NC):
+        for c in range(1, NC):
+            load_p(c, 0, 2)
+            load_p(c, 2, 3)
             load_x(c)
-            if c + 1 < NC:
-                load_scale(c + 1)
-        a_bf = keep.tile([P, NG, PACK], BF16, name="a_bf")
-        nc.sync.dma_start(out=a_bf[:], in_=a.rearrange("(g m t) -> m g t", g=NG, t=PACK))
+        pb_last = keep.tile([P, NC, 2, KP], U8, name="pb_last", align_bytes=64)
+        for t in range(2):
+            nc.sync.dma_start(out=pb_last[:, :, t, :], in_=p_by[1][:, 2 + t, :].rearrange("m (c k) -> m c k", k=KP))
+        for c in range(NC):
+            PB[(PAIRS, c)] = pb_last[:, c, :, :].rearrange("p r k -> p (r k)")
         g_bf = keep.tile([P, P], BF16, name="g_bf")
         nc.sync.dma_start(out=g_bf[0:NT, :], in_=g.rearrange("(i p) -> i p", p=P))
-        pb1 = {}
-        for r in range(WIDE, 2 * PACK):
-            pb1[r] = keep.tile([P, D], U8, name="pb1_%d" % r, align_bytes=64)
-            nc.sync.dma_start(out=pb1[r][:], in_=p_by[1][:, r - PACK, :])
         for q in range(4):
             nc.sync.dma_start(
                 out=vs[32 * q : 32 * q + 4, :, :].bitcast(I32),
@@ -106,204 +99,161 @@ def tile_stap_clutter_removal_s13_kernel(tc, x, g, p_bytes, p_scale, a, v_words,
         vw = keep.tile([P, NG, 2 * D], U8, name="vw", align_bytes=64)
         for gg in range(NG):
             nc.sync.dma_start(out=vw[:, gg, :].bitcast(I32), in_=v_words[gg].bitcast(I32))
-        xn = []
-        for j in range(8):
-            t = work.tile([P, 4, L], BF16, name="xn_%d" % j, tag="xr", bufs=8, align_bytes=64)
-            nc.sync.dma_start(out=t[:], in_=x[512 * j : 512 * (j + 1), :].rearrange("(i p) l -> p i l", p=P))
-            xn.append(t)
 
         xq = keep.tile([P, NC, L], U32, name="xq", align_bytes=64)
         xs = keep.tile([P, NC, L], U8, name="xs", align_bytes=64)
         hq = keep.tile([P, NG, L], U32, name="hq", align_bytes=64)
         hs = keep.tile([P, NG, L], U8, name="hs", align_bytes=64)
-        hg1 = keep.tile([P, L, PACK], BF16, name="hg1", align_bytes=64)
-        hg0 = keep.tile([P, L, PACK], BF16, name="hg0", align_bytes=64)
-        hp0 = keep.tile([P, PACK, L], BF16, name="hp0", align_bytes=64)
-        a_f = keep.tile([P, NG * PACK], F32, name="a_f")
+        hp = [keep.tile([P, PACK, L], BF16, name="hp%d" % gg, align_bytes=64) for gg in range(NG)]
+        hg = [keep.tile([P, L, PACK], BF16, name="hg%d" % gg, align_bytes=64) for gg in range(NG)]
+        a_f = keep.tile([P, NG, PACK], F32, name="a_f")
         g_f = keep.tile([P, NT], F32, name="g_f")
 
-        W, TR, PG, PQ, PS, XG, ACC = {}, {}, {}, {}, {}, {}, {}
+        W, TR, PG, PQ, PS, XG, ACC, xn = {}, {}, {}, {}, {}, {}, {}, {}
 
-        def product(s, lo, hi):
-            units = units_of(s)
-            if s not in W:
-                W[s] = work.tile([P, WIDE * KP], BF16, name="w", tag="w", align_bytes=64)
-            for j in range(lo, hi):
-                r, c = units[j]
-                if r < PACK:
-                    t, off = pb0[c]
-                    src = t[:, r, off : off + KP]
-                elif r < WIDE:
-                    t, off = pb4[c]
-                    src = t[:, off : off + KP]
-                else:
-                    src = pb1[r][:, KP * c : KP * (c + 1)]
-                nc.vector.tensor_tensor(
-                    out=W[s][:, KP * j : KP * (j + 1)],
-                    in0=src.bitcast(E4M3),
-                    in1=sc[:, KP * c : KP * (c + 1)],
-                    op=MULT,
-                )
+        def load_xn(j):
+            xn[j] = work.tile([P, PACK, L], BF16, name="xn_%d" % j, tag="xr", bufs=8, align_bytes=64)
+            nc.sync.dma_start(out=xn[j][:], in_=x[KP * j : KP * (j + 1), :].rearrange("(i p) l -> p i l", p=P))
 
-        def transposes(s, b):
-            words = W[s][:].bitcast(F32)
-            tr = psum.tile([P, 2, 2, P], F32, name="tr", tag="tr", bufs=8 - WIDE)
-            for j in range(2 * b, min(2 * b + 2, len(units_of(s)))):
+        def widen(n):
+            W[n] = work.tile([P, 2 * KP], BF16, name="w", tag="w", bufs=5, align_bytes=64)
+            src = PB[step_of(n)].bitcast(E4M3)
+            if n < 2:
+                nc.vector.tensor_copy(out=W[n][:], in_=src)
+            else:
+                nc.scalar.copy(out=W[n][:], in_=src)
+
+        def transposes(n):
+            words = W[n][:].bitcast(F32)
+            TR[n] = bank(6 + n % 2, [P, 2, 2, P])
+            for j in range(2):
                 for u in range(2):
-                    nc.tensor.transpose(tr[:, j % 2, u, :], words[:, 256 * j + u : 256 * (j + 1) : 2], ident[:])
-            TR[(s, b)] = tr
+                    nc.tensor.transpose(TR[n][:, u, j, :], words[:, 256 * j + u : 256 * (j + 1) : 2], ident[:])
 
-        def evac(s, lo, hi):
-            if s not in PG:
-                PG[s] = work.tile([P, WIDE, P, PACK], BF16, name="pg", tag="pg", align_bytes=64)
-            pw = PG[s][:].rearrange("p j m t -> p (j m t)").bitcast(F32)
-            pw = pw.rearrange("p (j m u) -> p j m u", j=WIDE, u=2)
-            b = lo // 2
-            nc.scalar.copy(
-                out=pw[:, lo:hi, :, :],
-                in_=TR[(s, b)][:, lo - 2 * b : hi - 2 * b, :, :].rearrange("p j u m -> p j m u"),
+        def product(n, lo, hi):
+            c = step_of(n)[1]
+            if n not in PG:
+                PG[n] = work.tile([P, 2 * P, PACK], BF16, name="pg", tag="pg", align_bytes=64)
+            turned = TR[n][:].rearrange("p u j m -> p (u j m)").bitcast(BF16)
+            turned = turned.rearrange("p (u m e) -> p m u e", u=2, e=2)
+            nc.vector.tensor_tensor(
+                out=PG[n][:, P * lo : P * hi, :].rearrange("p m (u e) -> p m u e", u=2),
+                in0=turned[:, P * lo : P * hi, :, :],
+                in1=s4[:, c : c + 1, 0:PACK].to_broadcast([P, P * (hi - lo), PACK]),
+                op=MULT,
             )
 
-        def quant_p(s, lo, hi):
-            if s not in PQ:
-                PQ[s] = work.tile([P, WIDE * P], U32, name="pq", tag="pq", align_bytes=64)
-                PS[s] = work.tile([P, WIDE * P], U8, name="ps", tag="ps", align_bytes=64)
+        def quant_p(n, lo, hi):
+            if n not in PQ:
+                PQ[n] = work.tile([P, 2 * P], U32, name="pq", tag="pq", bufs=6, align_bytes=64)
+                PS[n] = work.tile([P, 2 * P], U8, name="ps", tag="ps", bufs=6, align_bytes=64)
             nc.vector.quantize_mx(
-                out=PQ[s][:, P * lo : P * hi].bitcast(E4M3X4),
-                scales=PS[s][:, P * lo : P * hi],
-                in_=PG[s][:, lo:hi, :, :].rearrange("p j m t -> p (j m t)"),
+                out=PQ[n][:, P * lo : P * hi].bitcast(E4M3X4),
+                scales=PS[n][:, P * lo : P * hi],
+                in_=PG[n][:, P * lo : P * hi, :].rearrange("p m t -> p (m t)"),
             )
 
-        def x_interleave(c, lo, hi):
-            if c not in XG:
-                XG[c] = work.tile([P, L, PACK], BF16, name="xg", tag="xg", align_bytes=64)
-            nc.scalar.copy(
-                out=XG[c][:, lo:hi, :].rearrange("p (c i) t -> p c t i", i=4),
-                in_=xr[c][:, :, lo:hi].rearrange("p t (c i) -> p c t i", i=4),
+        def interleave(engine_copy, dst, src, lo, hi):
+            engine_copy(
+                out=dst[:, lo:hi, :].rearrange("p (c i) t -> p c t i", i=4),
+                in_=src[:, :, lo:hi].rearrange("p t (c i) -> p c t i", i=4),
             )
+
+        def x_interleave(c, h):
+            if h == 0:
+                XG[c] = work.tile([P, L, PACK], BF16, name="xg", tag="xg", align_bytes=64)
+            interleave(nc.scalar.copy, XG[c], xr[c], 256 * h, 256 * (h + 1))
 
         def quant_x(c):
             nc.vector.quantize_mx(
                 out=xq[:, c, :].bitcast(E4M3X4), scales=xs[:, c, :], in_=XG[c][:].rearrange("p l t -> p (l t)")
             )
 
-        def mm(s, lo, hi):
-            for j in range(lo, min(hi, len(units_of(s)))):
-                r, c = units_of(s)[j]
+        def mm(n, lo, hi):
+            pair, c = step_of(n)
+            for j in range(lo, hi):
+                r = 2 * pair + j
                 if c == 0:
-                    ACC[r] = psum.tile([P, L], F32, name="acc", tag="acc", bufs=WIDE)
+                    ACC[r] = bank(r % 6, [P, L])
                 nc.tensor.matmul_mx(
                     out=ACC[r][:],
-                    lhsT=PQ[s][:, P * j : P * (j + 1)].bitcast(E4M3X4),
-                    lhsT_scale=PS[s][:, P * j : P * (j + 1)],
+                    lhsT=PQ[n][:, P * j : P * (j + 1)].bitcast(E4M3X4),
+                    lhsT_scale=PS[n][:, P * j : P * (j + 1)],
                     rhs=xq[:, c, :].bitcast(E4M3X4),
                     rhs_scale=xs[:, c, :],
                     start=(c == 0),
                     stop=(c == NC - 1),
                 )
 
-        def quant_h(gg, src):
+        def quant_h(gg):
             nc.vector.quantize_mx(
-                out=hq[:, gg, :].bitcast(E4M3X4), scales=hs[:, gg, :], in_=src[:].rearrange("p l t -> p (l t)")
+                out=hq[:, gg, :].bitcast(E4M3X4), scales=hs[:, gg, :], in_=hg[gg][:].rearrange("p l t -> p (l t)")
             )
 
-        def h0_evac(t):
-            nc.scalar.activation(out=hp0[:, t, :], in_=ACC[t][:], func=COPY, scale=a_f[:, t : t + 1])
+        def h_scalar(r):
+            gg, t = r // PACK, r % PACK
+            nc.scalar.activation(out=hp[gg][:, t, :], in_=ACC[r][:], func=COPY, scale=a_f[:, gg, t : t + 1])
 
-        def h0_interleave(lo, hi):
-            nc.scalar.copy(
-                out=hg0[:, lo:hi, :].rearrange("p (c i) t -> p c t i", i=4),
-                in_=hp0[:, :, lo:hi].rearrange("p t (c i) -> p c t i", i=4),
-            )
-
-        def h1_scalar(t, lo, hi):
-            r = PACK + t
-            nc.scalar.activation(out=hg1[:, lo:hi, t], in_=ACC[r][:, lo:hi], func=COPY, scale=a_f[:, r : r + 1])
-
-        def h1_vector(t, lo, hi):
-            r = PACK + t
+        def h_vector(r):
+            gg, t = r // PACK, r % PACK
             nc.vector.tensor_scalar(
-                out=hg1[:, lo:hi, t], in0=ACC[r][:, lo:hi], scalar1=a_f[:, r : r + 1], scalar2=None, op0=MULT
+                out=hp[gg][:, t, :], in0=ACC[r][:], scalar1=a_f[:, gg, t : t + 1], scalar2=None, op0=MULT
             )
 
-        for s in range(STEPS):
-            wide = s < NC
-            product(s, 0, 2)
-            transposes(s, 0)
-            if s == NC + 2:
-                h0_evac(0)
-            if s >= 1:
-                n = len(units_of(s - 1))
-                evac(s - 1, 4 if n > 4 else 2, n)
-            if s == NC + 2:
-                h0_evac(1)
-            if s == NC + 3:
-                h0_evac(2)
-                h0_evac(3)
-            if wide:
-                x_interleave(s, 0, 256)
-            evac_late = s == LAST
-            if evac_late:
-                evac(s, 0, 1)
-                evac(s, 1, 2)
+        nc.scalar.activation(out=a_f[:], in_=a_bf[:, :, 0:PACK], func=COPY)
+        widen(0)
+        widen(1)
+        transposes(0)
+        for n in range(STEPS):
+            if n + 2 < STEPS:
+                widen(n + 2)
+            if n < SWEEP and n % PAIRS < 2:
+                x_interleave(n // PAIRS, n % PAIRS)
+            if n == SWEEP - 1:
+                for j in range(NC):
+                    load_xn(j)
+            if n + 1 < STEPS:
+                transposes(n + 1)
+            if n < LAST:
+                product(n, 0, 2)
             else:
-                evac(s, 0, 2)
-            if wide:
-                x_interleave(s, 256, 512)
-            if s == NC + 2:
-                h1_scalar(0, 0, 256)
-            if s == NC + 3:
-                h1_scalar(0, 256, 512)
-            if s == NC + 4:
-                h0_interleave(0, 512)
-            if s == NC + 5:
-                h1_scalar(1, 0, 512)
-            if s >= 2:
-                quant_p(s - 2, 0, 4)
-                if s - 2 < NC:
-                    quant_p(s - 2, 4, 5)
-                mm(s - 2, 0, 2)
-            product(s, 2, 4)
-            transposes(s, 1)
-            if wide:
-                evac(s, 2, 4)
-            if s >= 2:
-                mm(s - 2, 2, 4)
-            if wide:
-                product(s, 4, 5)
-                transposes(s, 2)
-                if s >= 2:
-                    mm(s - 2, 4, 5)
-            elif s - 2 < NC:
-                mm(s - 2, 4, 5)
-            if 1 <= s <= NC:
-                quant_x(s - 1)
-            if s == NC + 1:
-                nc.scalar.copy(out=a_f[:], in_=a_bf[:].rearrange("p g t -> p (g t)"))
-                nc.vector.tensor_copy(out=g_rows[0:NT, :], in_=g_bf[0:NT, :])
-        evac(LAST, 2, 3)
-        evac(LAST, 3, 4)
-        quant_p(LAST - 1, 0, 4)
-        mm(LAST - 1, 0, 4)
-        for j in range(2):
-            quant_p(LAST, j, j + 1)
-            mm(LAST, j, j + 1)
-        h1_scalar(2, 256, L)
-        quant_h(0, hg0)
-        h1_vector(2, 0, 256)
-        for j in range(2, 4):
-            quant_p(LAST, j, j + 1)
-            mm(LAST, j, j + 1)
-        h1_scalar(3, 256, L)
-        h1_vector(3, 0, 256)
-        quant_h(1, hg1)
+                product(n, 0, 1)
+            if n >= 1:
+                quant_p(n - 1, 0, 2)
+            if n < SWEEP and n % PAIRS == 2:
+                quant_x(n // PAIRS)
+            if n >= LAG:
+                mm(n - LAG, 0, 2)
+            done = n - LAG - (SWEEP - PAIRS)
+            if 0 <= done < PAIRS:
+                h_scalar(2 * done)
+                h_scalar(2 * done + 1)
+            if done in (PAIRS, PAIRS + 1):
+                interleave(nc.scalar.copy, hg[0], hp[0], 256 * (done - PAIRS), 256 * (done - PAIRS + 1))
+            if done == PAIRS + 2:
+                nc.scalar.copy(out=g_rows[0:NT, :], in_=g_bf[0:NT, :])
+                gt = bank(2, [P, P])
+                nc.tensor.transpose(gt[:], g_rows[:], ident[:])
+                nc.scalar.copy(out=g_f[:], in_=gt[:, 0:NT])
+        for n in range(STEPS - LAG, LAST):
+            mm(n, 0, 2)
+        product(LAST, 1, 2)
+        quant_p(LAST, 0, 1)
+        mm(LAST, 0, 1)
+        quant_p(LAST, 1, 2)
+        mm(LAST, 1, 2)
+        quant_h(0)
+        h_scalar(6)
+        h_vector(7)
+        interleave(nc.vector.tensor_copy, hg[1], hp[1], 0, H_SPLIT)
+        interleave(nc.scalar.copy, hg[1], hp[1], H_SPLIT, L)
+        quant_h(1)
 
         Y = {}
 
         def y_pass(i, gg):
             if gg == 0:
-                tr = i % 8 < 8 - WIDE
-                Y[i] = psum.tile([P, L], F32, name="y", tag="tr" if tr else "acc", bufs=8 - WIDE if tr else WIDE)
+                Y[i] = bank((i + 2) % 8, [P, L])
             nc.tensor.matmul_mx(
                 out=Y[i][:],
                 lhsT=vw[:, gg, 256 * i : 256 * (i + 1)].bitcast(E2M1X4),
@@ -314,21 +264,17 @@ def tile_stap_clutter_removal_s13_kernel(tc, x, g, p_bytes, p_scale, a, v_words,
                 stop=(gg == NG - 1),
             )
 
-        gt = psum.tile([P, P], F32, name="gt", tag="tr", bufs=8 - WIDE)
-        nc.tensor.transpose(gt[:], g_rows[:], ident[:])
-        nc.scalar.copy(out=g_f[:], in_=gt[:, 0:NT])
-
         groups = [(0, 1), (1, 2)] + [(i, i + 2) for i in range(2, NT - 2, 2)] + [(NT - 2, NT - 1), (NT - 1, NT)]
         first, end, o = {}, {}, None
         for lo, hi in groups:
             for i in range(lo, hi):
                 first[i], end[i] = lo, hi
 
-        for i in range(7):
+        for i in range(6):
             y_pass(i, 0)
         for i in range(NT):
             y_pass(i, 1)
-            if i >= 1 and i + 6 < NT:
+            if i + 6 < NT:
                 y_pass(i + 6, 0)
             if i == first[i]:
                 o = work.tile([P, 2, L], F32, name="o", tag="o", bufs=6, align_bytes=64)

@@ -28,7 +28,11 @@ PAIRS = 3
 SWEEP = PAIRS * NC
 STEPS = SWEEP + NC
 LAST = STEPS - 1
-LAG = 3
+AHEAD = 5
+G_COLS = 256
+S_ROUNDS = (2, 4, 6)
+EARLY = 2
+ADD = mybir.AluOpType.add
 H_SPLIT = 320
 
 
@@ -74,12 +78,16 @@ def tile_stap_clutter_removal_s13_kernel(tc, x, g, p_bytes, p_scale, a, v_words,
 
         s4 = keep.tile([P, NC, 8], F32, name="s4")
         a_bf = keep.tile([P, NG, 16], BF16, name="a_bf")
-        load_p(0, 0, 1)
+        g_bf = keep.tile([P, P], BF16, name="g_bf")
+        pb_first = [keep.tile([P, KP], U8, name="pb_first%d" % j, align_bytes=64) for j in range(2)]
+        for j in range(2):
+            nc.sync.dma_start(out=pb_first[j][:], in_=p_by[0][:, j, 0:KP])
         nc.scalar.dma_start(out=s4[:, :, 0:PACK], in_=p_scale.rearrange("o (c p t) -> p (o c) t", p=P, t=PACK))
         nc.scalar.dma_start(out=a_bf[:, :, 0:PACK], in_=a.rearrange("(g m t) -> m g t", g=NG, t=PACK))
+        nc.scalar.dma_start(out=g_bf[0:NT, :], in_=g.rearrange("(i p) -> i p", p=P))
         load_p(0, 1, 2)
-        load_p(0, 2, 3)
         load_x(0)
+        load_p(0, 2, 3)
         for c in range(1, NC):
             load_p(c, 0, 2)
             load_p(c, 2, 3)
@@ -89,8 +97,6 @@ def tile_stap_clutter_removal_s13_kernel(tc, x, g, p_bytes, p_scale, a, v_words,
             nc.sync.dma_start(out=pb_last[:, :, t, :], in_=p_by[1][:, 2 + t, :].rearrange("m (c k) -> m c k", k=KP))
         for c in range(NC):
             PB[(PAIRS, c)] = pb_last[:, c, :, :].rearrange("p r k -> p (r k)")
-        g_bf = keep.tile([P, P], BF16, name="g_bf")
-        nc.sync.dma_start(out=g_bf[0:NT, :], in_=g.rearrange("(i p) -> i p", p=P))
         for q in range(4):
             nc.sync.dma_start(
                 out=vs[32 * q : 32 * q + 4, :, :].bitcast(I32),
@@ -109,39 +115,52 @@ def tile_stap_clutter_removal_s13_kernel(tc, x, g, p_bytes, p_scale, a, v_words,
         a_f = keep.tile([P, NG, PACK], F32, name="a_f")
         g_f = keep.tile([P, NT], F32, name="g_f")
 
-        W, TR, PG, PQ, PS, XG, ACC, xn = {}, {}, {}, {}, {}, {}, {}, {}
+        W, TR, PG, PQ, PS, XG, XS, ACC, xn = {}, {}, {}, {}, {}, {}, {}, {}, {}
 
         def load_xn(j):
             xn[j] = work.tile([P, PACK, L], BF16, name="xn_%d" % j, tag="xr", bufs=8, align_bytes=64)
             nc.sync.dma_start(out=xn[j][:], in_=x[KP * j : KP * (j + 1), :].rearrange("(i p) l -> p i l", p=P))
 
         def widen(n):
-            W[n] = work.tile([P, 2 * KP], BF16, name="w", tag="w", bufs=5, align_bytes=64)
-            src = PB[step_of(n)].bitcast(E4M3)
-            if n < 2:
-                nc.vector.tensor_copy(out=W[n][:], in_=src)
-            else:
-                nc.scalar.copy(out=W[n][:], in_=src)
+            W[n] = work.tile([P, 2 * KP], BF16, name="w", tag="w", bufs=AHEAD + 3, align_bytes=64)
+            nc.scalar.copy(out=W[n][:], in_=PB[step_of(n)].bitcast(E4M3))
+
+        def turn(dst, words, j):
+            for u in range(2):
+                nc.tensor.transpose(dst[:, u, j, :], words[:, 256 * j + u : 256 * (j + 1) : 2], ident[:])
 
         def transposes(n):
-            words = W[n][:].bitcast(F32)
             TR[n] = bank(6 + n % 2, [P, 2, 2, P])
             for j in range(2):
-                for u in range(2):
-                    nc.tensor.transpose(TR[n][:, u, j, :], words[:, 256 * j + u : 256 * (j + 1) : 2], ident[:])
+                turn(TR[n], W[n][:].bitcast(F32), j)
 
-        def product(n, lo, hi):
+        def new_pg(n):
+            PG[n] = work.tile([P, 2 * P, PACK], BF16, name="pg", tag="pg", bufs=4, align_bytes=64)
+
+        def halves(tr):
+            turned = tr[:].rearrange("p u j m -> p (u j m)").bitcast(BF16)
+            return turned.rearrange("p (u m e) -> p m u e", u=2, e=2)
+
+        def product(n, lo, hi, tr=None):
             c = step_of(n)[1]
-            if n not in PG:
-                PG[n] = work.tile([P, 2 * P, PACK], BF16, name="pg", tag="pg", align_bytes=64)
-            turned = TR[n][:].rearrange("p u j m -> p (u j m)").bitcast(BF16)
-            turned = turned.rearrange("p (u m e) -> p m u e", u=2, e=2)
+            if lo == 0:
+                new_pg(n)
             nc.vector.tensor_tensor(
                 out=PG[n][:, P * lo : P * hi, :].rearrange("p m (u e) -> p m u e", u=2),
-                in0=turned[:, P * lo : P * hi, :, :],
+                in0=halves(TR[n] if tr is None else tr)[:, P * lo : P * hi, :, :],
                 in1=s4[:, c : c + 1, 0:PACK].to_broadcast([P, P * (hi - lo), PACK]),
                 op=MULT,
             )
+
+        def product_scalar(n):
+            c = step_of(n)[1]
+            new_pg(n)
+            planes = work.tile([P, PACK, 2 * P], BF16, name="planes", tag="planes", bufs=1, align_bytes=64)
+            for t in range(PACK):
+                nc.scalar.activation(
+                    out=planes[:, t, :], in_=halves(TR[n])[:, :, t // 2, t % 2], func=COPY, scale=s4[:, c, t : t + 1]
+                )
+            interleave(nc.scalar.copy, PG[n], planes, 0, 2 * P)
 
         def quant_p(n, lo, hi):
             if n not in PQ:
@@ -159,15 +178,22 @@ def tile_stap_clutter_removal_s13_kernel(tc, x, g, p_bytes, p_scale, a, v_words,
                 in_=src[:, :, lo:hi].rearrange("p t (c i) -> p c t i", i=4),
             )
 
-        def x_interleave(c, h):
-            if h == 0:
-                XG[c] = work.tile([P, L, PACK], BF16, name="xg", tag="xg", align_bytes=64)
-            interleave(nc.scalar.copy, XG[c], xr[c], 256 * h, 256 * (h + 1))
+        def gpsimd_copy(out, in_):
+            nc.gpsimd.tensor_scalar(out=out, in0=in_, scalar1=1.0, scalar2=0.0, op0=MULT, op1=ADD)
+
+        def x_gpsimd(c):
+            XG[c] = work.tile([P, G_COLS, PACK], BF16, name="xg", tag="xg", bufs=1, align_bytes=64)
+            interleave(gpsimd_copy, XG[c], xr[c][:, :, 0:G_COLS], 0, G_COLS)
+
+        def x_scalar(c):
+            XS[c] = work.tile([P, L - G_COLS, PACK], BF16, name="xsc", tag="xsc", bufs=2, align_bytes=64)
+            interleave(nc.scalar.copy, XS[c], xr[c][:, :, G_COLS:L], 0, L - G_COLS)
 
         def quant_x(c):
-            nc.vector.quantize_mx(
-                out=xq[:, c, :].bitcast(E4M3X4), scales=xs[:, c, :], in_=XG[c][:].rearrange("p l t -> p (l t)")
-            )
+            for src, lo, hi in ((XS[c], G_COLS, L), (XG[c], 0, G_COLS)):
+                nc.vector.quantize_mx(
+                    out=xq[:, c, lo:hi].bitcast(E4M3X4), scales=xs[:, c, lo:hi], in_=src[:].rearrange("p l t -> p (l t)")
+                )
 
         def mm(n, lo, hi):
             pair, c = step_of(n)
@@ -201,42 +227,78 @@ def tile_stap_clutter_removal_s13_kernel(tc, x, g, p_bytes, p_scale, a, v_words,
             )
 
         nc.scalar.activation(out=a_f[:], in_=a_bf[:, :, 0:PACK], func=COPY)
-        widen(0)
+        nc.scalar.copy(out=g_rows[0:NT, :], in_=g_bf[0:NT, :])
+        gt = bank(2, [P, P])
+        nc.tensor.transpose(gt[:], g_rows[:], ident[:])
+        W[0] = work.tile([P, 2 * KP], BF16, name="w", tag="w", bufs=AHEAD + 3, align_bytes=64)
+        first_tr = [bank(6, [P, 2, 2, P]), bank(0, [P, 2, 2, P])]
+        for j in range(2):
+            nc.vector.tensor_copy(out=W[0][:, KP * j : KP * (j + 1)], in_=pb_first[j][:].bitcast(E4M3))
+            turn(first_tr[j], W[0][:].bitcast(F32), j)
         widen(1)
-        transposes(0)
-        for n in range(STEPS):
-            if n + 2 < STEPS:
-                widen(n + 2)
-            if n < SWEEP and n % PAIRS < 2:
-                x_interleave(n // PAIRS, n % PAIRS)
-            if n == SWEEP - 1:
-                for j in range(NC):
-                    load_xn(j)
-            if n + 1 < STEPS:
-                transposes(n + 1)
+        nc.scalar.copy(out=g_f[:], in_=gt[:, 0:NT])
+        transposes(1)
+        widen(2)
+        x_scalar(0)
+        x_gpsimd(0)
+        for j in range(2):
+            product(0, j, j + 1, first_tr[j])
+        transposes(2)
+        product(1, 0, 2)
+        widen(3)
+        transposes(3)
+        quant_p(0, 0, 2)
+        quant_x(0)
+        widened = 4
+
+        def widen_to(n, widened):
+            for m in range(widened, min(STEPS, n + 1)):
+                widen(m)
+            return max(widened, min(STEPS, n + 1))
+
+        for r in range(1, NC):
+            n = PAIRS * r
+            x_gpsimd(r)
+            widened = widen_to(n + 1, widened)
+            x_scalar(r)
+            widened = widen_to(n + AHEAD, widened)
+            if r > 1:
+                mm(n - 4, 0, 2)
+            product(n - 1, 0, 2)
+            transposes(n + 1)
+            mm(n - 3, 0, 2)
+            product(n, 0, 2)
+            if r in S_ROUNDS:
+                product_scalar(n + 1)
+            transposes(n + 2)
+            quant_p(n - 2, 0, 2)
+            quant_p(n - 1, 0, 2)
+            mm(n - 2, 0, 2)
+            if r not in S_ROUNDS:
+                product(n + 1, 0, 2)
+            transposes(n + 3)
+            quant_p(n, 0, 2)
+            quant_x(r)
+        for j in range(NC):
+            load_xn(j)
+        mm(SWEEP - 4, 0, 2)
+        mm(SWEEP - 3, 0, 2)
+        for n in range(SWEEP - 1, STEPS):
+            widened = widen_to(n + AHEAD, widened)
             if n < LAST:
                 product(n, 0, 2)
             else:
                 product(n, 0, 1)
-            if n >= 1:
-                quant_p(n - 1, 0, 2)
-            if n < SWEEP and n % PAIRS == 2:
-                quant_x(n // PAIRS)
-            if n >= LAG:
-                mm(n - LAG, 0, 2)
-            done = n - LAG - (SWEEP - PAIRS)
+            if n + 2 < STEPS:
+                transposes(n + 2)
+            quant_p(n - 1, 0, 2)
+            done = n - (SWEEP - 1)
             if 0 <= done < PAIRS:
                 h_scalar(2 * done)
                 h_scalar(2 * done + 1)
             if done in (PAIRS, PAIRS + 1):
                 interleave(nc.scalar.copy, hg[0], hp[0], 256 * (done - PAIRS), 256 * (done - PAIRS + 1))
-            if done == PAIRS + 2:
-                nc.scalar.copy(out=g_rows[0:NT, :], in_=g_bf[0:NT, :])
-                gt = bank(2, [P, P])
-                nc.tensor.transpose(gt[:], g_rows[:], ident[:])
-                nc.scalar.copy(out=g_f[:], in_=gt[:, 0:NT])
-        for n in range(STEPS - LAG, LAST):
-            mm(n, 0, 2)
+            mm(n - 1, 0, 2)
         product(LAST, 1, 2)
         quant_p(LAST, 0, 1)
         mm(LAST, 0, 1)
@@ -251,9 +313,9 @@ def tile_stap_clutter_removal_s13_kernel(tc, x, g, p_bytes, p_scale, a, v_words,
 
         Y = {}
 
-        def y_pass(i, gg):
+        def y_pass(k, i, gg):
             if gg == 0:
-                Y[i] = bank((i + 2) % 8, [P, L])
+                Y[i] = bank((k + 2) % 8, [P, L])
             nc.tensor.matmul_mx(
                 out=Y[i][:],
                 lhsT=vw[:, gg, 256 * i : 256 * (i + 1)].bitcast(E2M1X4),
@@ -264,22 +326,28 @@ def tile_stap_clutter_removal_s13_kernel(tc, x, g, p_bytes, p_scale, a, v_words,
                 stop=(gg == NG - 1),
             )
 
-        groups = [(0, 1), (1, 2)] + [(i, i + 2) for i in range(2, NT - 2, 2)] + [(NT - 2, NT - 1), (NT - 1, NT)]
-        first, end, o = {}, {}, None
+        groups = [(i, i + 1) for i in range(4)] + [(i, i + 2) for i in range(4, NT - 2, 2)] + [(NT - 2, NT - 1), (NT - 1, NT)]
+        shared = [i for i in range(9, NT - 4, 4)]
+        order = sorted(range(NT), key=lambda i: i - EARLY - 0.5 if i in shared else i)
+        first, O, left = {}, {}, {}
         for lo, hi in groups:
+            left[lo] = hi - lo
             for i in range(lo, hi):
-                first[i], end[i] = lo, hi
+                first[i] = lo
+        size = dict(left)
 
-        for i in range(6):
-            y_pass(i, 0)
-        for i in range(NT):
-            y_pass(i, 1)
-            if i + 6 < NT:
-                y_pass(i + 6, 0)
-            if i == first[i]:
-                o = work.tile([P, 2, L], F32, name="o", tag="o", bufs=6, align_bytes=64)
-            xi, gi, oi = xn[i // 4][:, i % 4, :], g_f[:, i : i + 1], o[:, i - first[i], :]
-            if i % 4 == 3 and i < NT - 4:
+        for k in range(8):
+            y_pass(k, order[k], 0)
+        for k in range(NT):
+            i = order[k]
+            y_pass(k, i, 1)
+            if 8 <= k + 6 < NT:
+                y_pass(k + 6, order[k + 6], 0)
+            lo = first[i]
+            if lo not in O:
+                O[lo] = work.tile([P, 2, L], F32, name="o", tag="o", bufs=7, align_bytes=64)
+            xi, gi, oi = xn[i // 4][:, i % 4, :], g_f[:, i : i + 1], O[lo][:, i - lo, :]
+            if i in shared:
                 gx = work.tile([P, L], F32, name="gx", tag="gx", bufs=2)
                 ys = work.tile([P, L], F32, name="ys", tag="ys", bufs=2)
                 nc.scalar.activation(out=gx[:], in_=xi, func=COPY, scale=gi)
@@ -287,7 +355,8 @@ def tile_stap_clutter_removal_s13_kernel(tc, x, g, p_bytes, p_scale, a, v_words,
                 nc.gpsimd.tensor_tensor(out=oi, in0=gx[:], in1=ys[:], op=SUB)
             else:
                 nc.vector.scalar_tensor_tensor(out=oi, in0=xi, scalar=gi, in1=Y[i][:], op0=MULT, op1=SUB)
-            if i == end[i] - 1:
+            left[lo] = left[lo] - 1
+            if left[lo] == 0:
                 nc.sync.dma_start(
-                    out=out[P * first[i] : P * end[i], :].rearrange("(i p) l -> p i l", p=P), in_=o[:, 0 : end[i] - first[i], :]
+                    out=out[P * lo : P * (lo + size[lo]), :].rearrange("(i p) l -> p i l", p=P), in_=O[lo][:, 0 : size[lo], :]
                 )

@@ -32,8 +32,15 @@ AHEAD = 5
 G_COLS = 256
 S_ROUNDS = (2, 4, 6)
 EARLY = 2
+FREED = STEPS - 4
+S_LATE = STEPS - 4
+V_FIRST = 256
+S_AT = 3
+S_LAG = 2
+LEAD = 5
+Y_BANKS = (6, 7, 2, 3, 4, 5, 0, 1)
 ADD = mybir.AluOpType.add
-H_SPLIT = 320
+H_SPLIT = 352
 
 
 def step_of(n):
@@ -130,12 +137,12 @@ def tile_stap_clutter_removal_s13_kernel(tc, x, g, p_bytes, p_scale, a, v_words,
                 nc.tensor.transpose(dst[:, u, j, :], words[:, 256 * j + u : 256 * (j + 1) : 2], ident[:])
 
         def transposes(n):
-            TR[n] = bank(6 + n % 2, [P, 2, 2, P])
+            TR[n] = bank(6 + n % 2 if n < FREED else n - FREED + 2, [P, 2, 2, P])
             for j in range(2):
                 turn(TR[n], W[n][:].bitcast(F32), j)
 
         def new_pg(n):
-            PG[n] = work.tile([P, 2 * P, PACK], BF16, name="pg", tag="pg", bufs=4, align_bytes=64)
+            PG[n] = work.tile([P, 2 * P, PACK], BF16, name="pg", tag="pg", bufs=5, align_bytes=64)
 
         def halves(tr):
             turned = tr[:].rearrange("p u j m -> p (u j m)").bitcast(BF16)
@@ -183,7 +190,7 @@ def tile_stap_clutter_removal_s13_kernel(tc, x, g, p_bytes, p_scale, a, v_words,
 
         def x_gpsimd(c):
             XG[c] = work.tile([P, G_COLS, PACK], BF16, name="xg", tag="xg", bufs=1, align_bytes=64)
-            interleave(gpsimd_copy, XG[c], xr[c][:, :, 0:G_COLS], 0, G_COLS)
+            gpsimd_copy(XG[c][:], xr[c][:, :, 0:G_COLS].rearrange("p t l -> p l t"))
 
         def x_scalar(c):
             XS[c] = work.tile([P, L - G_COLS, PACK], BF16, name="xsc", tag="xsc", bufs=2, align_bytes=64)
@@ -211,19 +218,21 @@ def tile_stap_clutter_removal_s13_kernel(tc, x, g, p_bytes, p_scale, a, v_words,
                     stop=(c == NC - 1),
                 )
 
-        def quant_h(gg):
+        def quant_h(gg, lo, hi):
             nc.vector.quantize_mx(
-                out=hq[:, gg, :].bitcast(E4M3X4), scales=hs[:, gg, :], in_=hg[gg][:].rearrange("p l t -> p (l t)")
+                out=hq[:, gg, lo:hi].bitcast(E4M3X4),
+                scales=hs[:, gg, lo:hi],
+                in_=hg[gg][:, lo:hi, :].rearrange("p l t -> p (l t)"),
             )
 
         def h_scalar(r):
             gg, t = r // PACK, r % PACK
             nc.scalar.activation(out=hp[gg][:, t, :], in_=ACC[r][:], func=COPY, scale=a_f[:, gg, t : t + 1])
 
-        def h_vector(r):
+        def h_vector(r, lo, hi):
             gg, t = r // PACK, r % PACK
             nc.vector.tensor_scalar(
-                out=hp[gg][:, t, :], in0=ACC[r][:], scalar1=a_f[:, gg, t : t + 1], scalar2=None, op0=MULT
+                out=hp[gg][:, t, lo:hi], in0=ACC[r][:, lo:hi], scalar1=a_f[:, gg, t : t + 1], scalar2=None, op0=MULT
             )
 
         nc.scalar.activation(out=a_f[:], in_=a_bf[:, :, 0:PACK], func=COPY)
@@ -283,39 +292,51 @@ def tile_stap_clutter_removal_s13_kernel(tc, x, g, p_bytes, p_scale, a, v_words,
             load_xn(j)
         mm(SWEEP - 4, 0, 2)
         mm(SWEEP - 3, 0, 2)
+        before = SWEEP - 2
         for n in range(SWEEP - 1, STEPS):
             widened = widen_to(n + AHEAD, widened)
-            if n < LAST:
-                product(n, 0, 2)
-            else:
-                product(n, 0, 1)
-            if n + 2 < STEPS:
+            if n != S_LATE:
+                product(n, 0, 2 if n < LAST else 1)
+            if n + 2 < FREED:
                 transposes(n + 2)
-            quant_p(n - 1, 0, 2)
+            if n + 2 in (FREED - 1, FREED + 1):
+                transposes(n + 3)
+                transposes(n + 4)
             done = n - (SWEEP - 1)
             if 0 <= done < PAIRS:
                 h_scalar(2 * done)
                 h_scalar(2 * done + 1)
-            if done in (PAIRS, PAIRS + 1):
-                interleave(nc.scalar.copy, hg[0], hp[0], 256 * (done - PAIRS), 256 * (done - PAIRS + 1))
-            mm(n - 1, 0, 2)
+            if done == S_AT:
+                product_scalar(S_LATE)
+            if done in (S_AT, S_AT + 1):
+                interleave(nc.scalar.copy, hg[0], hp[0], 256 * (done - S_AT), 256 * (done - S_AT + 1))
+            if n != S_LATE:
+                quant_p(before, 0, 2)
+                mm(before, 0, 2)
+                before = n
+            if n == S_LATE + S_LAG:
+                quant_p(S_LATE, 0, 2)
+                mm(S_LATE, 0, 2)
         product(LAST, 1, 2)
         quant_p(LAST, 0, 1)
         mm(LAST, 0, 1)
         quant_p(LAST, 1, 2)
         mm(LAST, 1, 2)
-        quant_h(0)
+        quant_h(0, 0, L)
         h_scalar(6)
-        h_vector(7)
-        interleave(nc.vector.tensor_copy, hg[1], hp[1], 0, H_SPLIT)
+        h_vector(7, 0, V_FIRST)
+        h_vector(7, V_FIRST, L)
+        interleave(nc.vector.tensor_copy, hg[1], hp[1], 0, V_FIRST)
         interleave(nc.scalar.copy, hg[1], hp[1], H_SPLIT, L)
-        quant_h(1)
+        interleave(nc.vector.tensor_copy, hg[1], hp[1], V_FIRST, H_SPLIT)
+        quant_h(1, 0, V_FIRST)
+        quant_h(1, V_FIRST, L)
 
         Y = {}
 
         def y_pass(k, i, gg):
             if gg == 0:
-                Y[i] = bank((k + 2) % 8, [P, L])
+                Y[i] = bank(Y_BANKS[k % 8], [P, L])
             nc.tensor.matmul_mx(
                 out=Y[i][:],
                 lhsT=vw[:, gg, 256 * i : 256 * (i + 1)].bitcast(E2M1X4),
@@ -341,8 +362,8 @@ def tile_stap_clutter_removal_s13_kernel(tc, x, g, p_bytes, p_scale, a, v_words,
         for k in range(NT):
             i = order[k]
             y_pass(k, i, 1)
-            if 8 <= k + 6 < NT:
-                y_pass(k + 6, order[k + 6], 0)
+            if 8 <= k + LEAD < NT:
+                y_pass(k + LEAD, order[k + LEAD], 0)
             lo = first[i]
             if lo not in O:
                 O[lo] = work.tile([P, 2, L], F32, name="o", tag="o", bufs=7, align_bytes=64)

@@ -31,7 +31,8 @@ LAST = STEPS - 1
 AHEAD = 5
 G_COLS = 256
 S_ROUNDS = (2, 4, 6)
-EARLY = 2
+EARLY = 3
+X_PARTS = ((0, 0, 0, 256), (1, 256, 256, 512))
 FREED = STEPS - 4
 S_LATE = STEPS - 4
 V_FIRST = 256
@@ -197,9 +198,11 @@ def tile_stap_clutter_removal_s13_kernel(tc, x, g, p_bytes, p_scale, a, v_words,
             interleave(nc.scalar.copy, XS[c], xr[c][:, :, G_COLS:L], 0, L - G_COLS)
 
         def quant_x(c):
-            for src, lo, hi in ((XS[c], G_COLS, L), (XG[c], 0, G_COLS)):
+            for src, base, lo, hi in X_PARTS:
                 nc.vector.quantize_mx(
-                    out=xq[:, c, lo:hi].bitcast(E4M3X4), scales=xs[:, c, lo:hi], in_=src[:].rearrange("p l t -> p (l t)")
+                    out=xq[:, c, lo:hi].bitcast(E4M3X4),
+                    scales=xs[:, c, lo:hi],
+                    in_=(XG, XS)[src][c][:, lo - base : hi - base, :].rearrange("p l t -> p (l t)"),
                 )
 
         def mm(n, lo, hi):

@@ -32,6 +32,7 @@ AHEAD = 5
 G_COLS = 256
 S_ROUNDS = (2, 4, 6)
 EARLY = 3
+W0, W1, W2, W3 = 4, 3, 2, 1
 X_PARTS = ((0, 0, 0, 256), (1, 256, 256, 512))
 FREED = STEPS - 4
 S_LATE = STEPS - 4
@@ -65,9 +66,18 @@ def tile_stap_clutter_removal_s13_kernel(tc, x, g, p_bytes, p_scale, a, v_words,
         make_identity(nc, ident[:])
         g_rows = keep.tile([P, P], F32, name="g_rows")
         nc.gpsimd.memset(g_rows[:], 0.0)
+        warm = keep.tile([P, L], BF16, name="warm")
+        nc.vector.memset(warm[:], 0.0)
         vs = keep.tile([P, NG, D], U8, name="vs", align_bytes=64)
         nc.vector.memset(vs[:].rearrange("p g n -> p (g n)").bitcast(I32), 0)
 
+
+        def warm_up(count):
+            wb = bank(5, [P, L])
+            for i in range(count):
+                nc.tensor.matmul(out=wb[:], lhsT=warm[:, 0:P], rhs=warm[:], start=True, stop=True)
+
+        warm_up(W0)
         p_by = p_bytes.rearrange("(g m t) k -> g m t k", g=NG, t=PACK)
         PB, xr = {}, {}
 
@@ -250,15 +260,18 @@ def tile_stap_clutter_removal_s13_kernel(tc, x, g, p_bytes, p_scale, a, v_words,
         widen(1)
         nc.scalar.copy(out=g_f[:], in_=gt[:, 0:NT])
         transposes(1)
+        warm_up(W1)
         widen(2)
         x_scalar(0)
         x_gpsimd(0)
         for j in range(2):
             product(0, j, j + 1, first_tr[j])
         transposes(2)
+        warm_up(W2)
         product(1, 0, 2)
         widen(3)
         transposes(3)
+        warm_up(W3)
         quant_p(0, 0, 2)
         quant_x(0)
         widened = 4

@@ -28,19 +28,15 @@ PAIRS = 3
 SWEEP = PAIRS * NC
 STEPS = SWEEP + NC
 LAST = STEPS - 1
-AHEAD = 5
-G_COLS = 256
+AHEAD = 7
+W_BUFS = 11
+G_COLS = 288
 S_ROUNDS = (2, 4, 6)
 EARLY = 3
 W0, W1, W2, W3 = 4, 3, 2, 1
-X_PARTS = ((0, 0, 0, 256), (1, 256, 256, 512))
-FREED = STEPS - 4
-S_LATE = STEPS - 4
 V_FIRST = 256
-S_AT = 3
-S_LAG = 2
-LEAD = 5
-Y_BANKS = (6, 7, 2, 3, 4, 5, 0, 1)
+LEAD = 3
+Y_BANKS = (0, 1, 4, 6, 5, 7, 2, 3)
 ADD = mybir.AluOpType.add
 H_SPLIT = 352
 
@@ -140,20 +136,30 @@ def tile_stap_clutter_removal_s13_kernel(tc, x, g, p_bytes, p_scale, a, v_words,
             nc.sync.dma_start(out=xn[j][:], in_=x[KP * j : KP * (j + 1), :].rearrange("(i p) l -> p i l", p=P))
 
         def widen(n):
-            W[n] = work.tile([P, 2 * KP], BF16, name="w", tag="w", bufs=AHEAD + 3, align_bytes=64)
+            W[n] = work.tile([P, 2 * KP], BF16, name="w", tag="w", bufs=W_BUFS, align_bytes=64)
             nc.scalar.copy(out=W[n][:], in_=PB[step_of(n)].bitcast(E4M3))
 
         def turn(dst, words, j):
             for u in range(2):
                 nc.tensor.transpose(dst[:, u, j, :], words[:, 256 * j + u : 256 * (j + 1) : 2], ident[:])
 
-        def transposes(n):
-            TR[n] = bank(6 + n % 2 if n < FREED else n - FREED + 2, [P, 2, 2, P])
+        def transposes(n, b=None):
+            TR[n] = bank(6 + n % 2 if b is None else b, [P, 2, 2, P])
             for j in range(2):
                 turn(TR[n], W[n][:].bitcast(F32), j)
 
-        def new_pg(n):
-            PG[n] = work.tile([P, 2 * P, PACK], BF16, name="pg", tag="pg", bufs=5, align_bytes=64)
+        def place(n):
+            if n < SWEEP:
+                head = n - 1 if n % PAIRS == 2 else n
+            else:
+                head = n - n % 2
+            return head, 2 * P * (n - head)
+
+        def grouped(n):
+            head, col = place(n)
+            if head not in PG:
+                PG[head] = work.tile([P, 4 * P, PACK], BF16, name="pg", tag="pg", bufs=4, align_bytes=64)
+            return PG[head][:, col : col + 2 * P, :]
 
         def halves(tr):
             turned = tr[:].rearrange("p u j m -> p (u j m)").bitcast(BF16)
@@ -161,10 +167,8 @@ def tile_stap_clutter_removal_s13_kernel(tc, x, g, p_bytes, p_scale, a, v_words,
 
         def product(n, lo, hi, tr=None):
             c = step_of(n)[1]
-            if lo == 0:
-                new_pg(n)
             nc.vector.tensor_tensor(
-                out=PG[n][:, P * lo : P * hi, :].rearrange("p m (u e) -> p m u e", u=2),
+                out=grouped(n)[:, P * lo : P * hi, :].rearrange("p m (u e) -> p m u e", u=2),
                 in0=halves(TR[n] if tr is None else tr)[:, P * lo : P * hi, :, :],
                 in1=s4[:, c : c + 1, 0:PACK].to_broadcast([P, P * (hi - lo), PACK]),
                 op=MULT,
@@ -172,18 +176,17 @@ def tile_stap_clutter_removal_s13_kernel(tc, x, g, p_bytes, p_scale, a, v_words,
 
         def product_scalar(n):
             c = step_of(n)[1]
-            new_pg(n)
             planes = work.tile([P, PACK, 2 * P], BF16, name="planes", tag="planes", bufs=1, align_bytes=64)
             for t in range(PACK):
                 nc.scalar.activation(
                     out=planes[:, t, :], in_=halves(TR[n])[:, :, t // 2, t % 2], func=COPY, scale=s4[:, c, t : t + 1]
                 )
-            interleave(nc.scalar.copy, PG[n], planes, 0, 2 * P)
+            return planes
 
         def quant_p(n, lo, hi):
             if n not in PQ:
-                PQ[n] = work.tile([P, 2 * P], U32, name="pq", tag="pq", bufs=6, align_bytes=64)
-                PS[n] = work.tile([P, 2 * P], U8, name="ps", tag="ps", bufs=6, align_bytes=64)
+                PQ[n] = work.tile([P, 4 * P], U32, name="pq", tag="pq", bufs=4, align_bytes=64)
+                PS[n] = work.tile([P, 4 * P], U8, name="ps", tag="ps", bufs=4, align_bytes=64)
             nc.vector.quantize_mx(
                 out=PQ[n][:, P * lo : P * hi].bitcast(E4M3X4),
                 scales=PS[n][:, P * lo : P * hi],
@@ -199,32 +202,27 @@ def tile_stap_clutter_removal_s13_kernel(tc, x, g, p_bytes, p_scale, a, v_words,
         def gpsimd_copy(out, in_):
             nc.gpsimd.tensor_scalar(out=out, in0=in_, scalar1=1.0, scalar2=0.0, op0=MULT, op1=ADD)
 
-        def x_gpsimd(c):
-            XG[c] = work.tile([P, G_COLS, PACK], BF16, name="xg", tag="xg", bufs=1, align_bytes=64)
-            gpsimd_copy(XG[c][:], xr[c][:, :, 0:G_COLS].rearrange("p t l -> p l t"))
-
-        def x_scalar(c):
-            XS[c] = work.tile([P, L - G_COLS, PACK], BF16, name="xsc", tag="xsc", bufs=2, align_bytes=64)
-            interleave(nc.scalar.copy, XS[c], xr[c][:, :, G_COLS:L], 0, L - G_COLS)
+        def x_interleave(c):
+            XG[c] = work.tile([P, L, PACK], BF16, name="xg", tag="xg", bufs=1, align_bytes=64)
+            gpsimd_copy(XG[c][:, 0:G_COLS, :], xr[c][:, :, 0:G_COLS].rearrange("p t l -> p l t"))
+            interleave(nc.scalar.copy, XG[c], xr[c], G_COLS, L)
 
         def quant_x(c):
-            for src, base, lo, hi in X_PARTS:
-                nc.vector.quantize_mx(
-                    out=xq[:, c, lo:hi].bitcast(E4M3X4),
-                    scales=xs[:, c, lo:hi],
-                    in_=(XG, XS)[src][c][:, lo - base : hi - base, :].rearrange("p l t -> p (l t)"),
-                )
+            nc.vector.quantize_mx(
+                out=xq[:, c, :].bitcast(E4M3X4), scales=xs[:, c, :], in_=XG[c][:].rearrange("p l t -> p (l t)")
+            )
 
         def mm(n, lo, hi):
             pair, c = step_of(n)
+            head, col = place(n)
             for j in range(lo, hi):
                 r = 2 * pair + j
                 if c == 0:
-                    ACC[r] = bank(r % 6, [P, L])
+                    ACC[r] = bank(r if r < 6 else r - PACK, [P, L])
                 nc.tensor.matmul_mx(
                     out=ACC[r][:],
-                    lhsT=PQ[n][:, P * j : P * (j + 1)].bitcast(E4M3X4),
-                    lhsT_scale=PS[n][:, P * j : P * (j + 1)],
+                    lhsT=PQ[head][:, col + P * j : col + P * (j + 1)].bitcast(E4M3X4),
+                    lhsT_scale=PS[head][:, col + P * j : col + P * (j + 1)],
                     rhs=xq[:, c, :].bitcast(E4M3X4),
                     rhs_scale=xs[:, c, :],
                     start=(c == 0),
@@ -252,7 +250,7 @@ def tile_stap_clutter_removal_s13_kernel(tc, x, g, p_bytes, p_scale, a, v_words,
         nc.scalar.copy(out=g_rows[0:NT, :], in_=g_bf[0:NT, :])
         gt = bank(2, [P, P])
         nc.tensor.transpose(gt[:], g_rows[:], ident[:])
-        W[0] = work.tile([P, 2 * KP], BF16, name="w", tag="w", bufs=AHEAD + 3, align_bytes=64)
+        W[0] = work.tile([P, 2 * KP], BF16, name="w", tag="w", bufs=W_BUFS, align_bytes=64)
         first_tr = [bank(6, [P, 2, 2, P]), bank(0, [P, 2, 2, P])]
         for j in range(2):
             nc.vector.tensor_copy(out=W[0][:, KP * j : KP * (j + 1)], in_=pb_first[j][:].bitcast(E4M3))
@@ -261,9 +259,8 @@ def tile_stap_clutter_removal_s13_kernel(tc, x, g, p_bytes, p_scale, a, v_words,
         nc.scalar.copy(out=g_f[:], in_=gt[:, 0:NT])
         transposes(1)
         warm_up(W1)
+        x_interleave(0)
         widen(2)
-        x_scalar(0)
-        x_gpsimd(0)
         for j in range(2):
             product(0, j, j + 1, first_tr[j])
         transposes(2)
@@ -283,10 +280,9 @@ def tile_stap_clutter_removal_s13_kernel(tc, x, g, p_bytes, p_scale, a, v_words,
 
         for r in range(1, NC):
             n = PAIRS * r
-            x_gpsimd(r)
             widened = widen_to(n + 1, widened)
-            x_scalar(r)
-            widened = widen_to(n + AHEAD, widened)
+            x_interleave(r)
+            widened = widen_to(n + 2 if r in S_ROUNDS else n + AHEAD, widened)
             if r > 1:
                 mm(n - 4, 0, 2)
             product(n - 1, 0, 2)
@@ -294,10 +290,12 @@ def tile_stap_clutter_removal_s13_kernel(tc, x, g, p_bytes, p_scale, a, v_words,
             mm(n - 3, 0, 2)
             product(n, 0, 2)
             if r in S_ROUNDS:
-                product_scalar(n + 1)
+                planes = product_scalar(n + 1)
+                widened = widen_to(widened, widened)
+                interleave(nc.scalar.copy, grouped(n + 1), planes, 0, 2 * P)
+                widened = widen_to(n + 3, widened)
             transposes(n + 2)
-            quant_p(n - 2, 0, 2)
-            quant_p(n - 1, 0, 2)
+            quant_p(n - 2, 0, 4)
             mm(n - 2, 0, 2)
             if r not in S_ROUNDS:
                 product(n + 1, 0, 2)
@@ -306,38 +304,53 @@ def tile_stap_clutter_removal_s13_kernel(tc, x, g, p_bytes, p_scale, a, v_words,
             quant_x(r)
         for j in range(NC):
             load_xn(j)
-        mm(SWEEP - 4, 0, 2)
-        mm(SWEEP - 3, 0, 2)
-        before = SWEEP - 2
-        for n in range(SWEEP - 1, STEPS):
-            widened = widen_to(n + AHEAD, widened)
-            if n != S_LATE:
-                product(n, 0, 2 if n < LAST else 1)
-            if n + 2 < FREED:
-                transposes(n + 2)
-            if n + 2 in (FREED - 1, FREED + 1):
-                transposes(n + 3)
-                transposes(n + 4)
-            done = n - (SWEEP - 1)
-            if 0 <= done < PAIRS:
-                h_scalar(2 * done)
-                h_scalar(2 * done + 1)
-            if done == S_AT:
-                product_scalar(S_LATE)
-            if done in (S_AT, S_AT + 1):
-                interleave(nc.scalar.copy, hg[0], hp[0], 256 * (done - S_AT), 256 * (done - S_AT + 1))
-            if n != S_LATE:
-                quant_p(before, 0, 2)
-                mm(before, 0, 2)
-                before = n
-            if n == S_LATE + S_LAG:
-                quant_p(S_LATE, 0, 2)
-                mm(S_LATE, 0, 2)
+        n = SWEEP
+        widen_to(LAST, widened)
+        mm(n - 4, 0, 2)
+        product(n - 1, 0, 2)
+        transposes(n + 1)
+        mm(n - 3, 0, 2)
+        h_scalar(0)
+        h_scalar(1)
+        product(n, 0, 2)
+        transposes(n + 2)
+        quant_p(n - 2, 0, 4)
+        mm(n - 2, 0, 2)
+        h_scalar(2)
+        h_scalar(3)
+        transposes(n + 4, 0)
+        product(n + 1, 0, 2)
+        transposes(n + 3)
+        mm(n - 1, 0, 2)
+        planes = product_scalar(n + 4)
+        h_scalar(4)
+        interleave(nc.scalar.copy, grouped(n + 4), planes, 0, 2 * P)
+        transposes(n + 5, 1)
+        product(n + 2, 0, 2)
+        transposes(n + 6)
+        quant_p(n, 0, 4)
+        mm(n, 0, 2)
+        mm(n + 1, 0, 2)
+        product(n + 3, 0, 2)
+        transposes(n + 7)
+        product(n + 5, 0, 2)
+        quant_p(n + 2, 0, 4)
+        mm(n + 2, 0, 2)
+        mm(n + 3, 0, 2)
+        for h in range(2):
+            interleave(nc.scalar.copy, hg[0], hp[0], 256 * h, 256 * (h + 1))
+        h_scalar(5)
+        product(n + 6, 0, 2)
+        quant_p(n + 4, 0, 4)
+        mm(n + 4, 0, 2)
+        mm(n + 5, 0, 2)
+        product(LAST, 0, 1)
+        quant_p(n + 6, 0, 2)
+        mm(n + 6, 0, 2)
         product(LAST, 1, 2)
-        quant_p(LAST, 0, 1)
-        mm(LAST, 0, 1)
-        quant_p(LAST, 1, 2)
-        mm(LAST, 1, 2)
+        for j in range(2):
+            quant_p(n + 6, 2 + j, 3 + j)
+            mm(LAST, j, j + 1)
         quant_h(0, 0, L)
         h_scalar(6)
         h_vector(7, 0, V_FIRST)

@@ -36,6 +36,7 @@ EARLY = 3
 W0, W1, W2, W3 = 4, 3, 2, 1
 V_FIRST = 256
 LEAD = 3
+SECOND_QUEUE = 6
 Y_BANKS = (0, 1, 4, 6, 5, 7, 2, 3)
 ADD = mybir.AluOpType.add
 H_SPLIT = 352
@@ -377,7 +378,7 @@ def tile_stap_clutter_removal_s13_kernel(tc, x, g, p_bytes, p_scale, a, v_words,
             )
 
         groups = [(i, i + 1) for i in range(4)] + [(i, i + 2) for i in range(4, NT - 2, 2)] + [(NT - 2, NT - 1), (NT - 1, NT)]
-        shared = [i for i in range(9, NT - 4, 4)]
+        shared = [i for i in range(5, NT - 4, 4)]
         order = sorted(range(NT), key=lambda i: i - EARLY - 0.5 if i in shared else i)
         first, O, left = {}, {}, {}
         for lo, hi in groups:
@@ -386,6 +387,13 @@ def tile_stap_clutter_removal_s13_kernel(tc, x, g, p_bytes, p_scale, a, v_words,
                 first[i] = lo
         size = dict(left)
 
+        GX = {}
+
+        def gained(i):
+            GX[i] = work.tile([P, L], F32, name="gx", tag="gx", bufs=3)
+            nc.scalar.activation(out=GX[i][:], in_=xn[i // 4][:, i % 4, :], func=COPY, scale=g_f[:, i : i + 1])
+
+        gained(shared[0])
         for k in range(8):
             y_pass(k, order[k], 0)
         for k in range(NT):
@@ -398,15 +406,16 @@ def tile_stap_clutter_removal_s13_kernel(tc, x, g, p_bytes, p_scale, a, v_words,
                 O[lo] = work.tile([P, 2, L], F32, name="o", tag="o", bufs=7, align_bytes=64)
             xi, gi, oi = xn[i // 4][:, i % 4, :], g_f[:, i : i + 1], O[lo][:, i - lo, :]
             if i in shared:
-                gx = work.tile([P, L], F32, name="gx", tag="gx", bufs=2)
                 ys = work.tile([P, L], F32, name="ys", tag="ys", bufs=2)
-                nc.scalar.activation(out=gx[:], in_=xi, func=COPY, scale=gi)
                 nc.scalar.copy(out=ys[:], in_=Y[i][:])
-                nc.gpsimd.tensor_tensor(out=oi, in0=gx[:], in1=ys[:], op=SUB)
+                if i != shared[-1]:
+                    gained(shared[shared.index(i) + 1])
+                nc.gpsimd.tensor_tensor(out=oi, in0=GX[i][:], in1=ys[:], op=SUB)
             else:
                 nc.vector.scalar_tensor_tensor(out=oi, in0=xi, scalar=gi, in1=Y[i][:], op0=MULT, op1=SUB)
             left[lo] = left[lo] - 1
             if left[lo] == 0:
-                nc.sync.dma_start(
+                queue = nc.scalar if lo >= SECOND_QUEUE and lo % 4 == 2 else nc.sync
+                queue.dma_start(
                     out=out[P * lo : P * (lo + size[lo]), :].rearrange("(i p) l -> p i l", p=P), in_=O[lo][:, 0 : size[lo], :]
                 )

@@ -15,6 +15,7 @@ E4M3 = mybir.dt.float8_e4m3fn
 E4M3X4 = mybir.dt.float8_e4m3fn_x4
 E2M1X4 = mybir.dt.float4_e2m1fn_x4
 MULT = mybir.AluOpType.mult
+ADD = mybir.AluOpType.add
 SUB = mybir.AluOpType.subtract
 COPY = mybir.ActivationFunctionType.Copy
 
@@ -24,28 +25,41 @@ KP = P * PACK
 NC = D // KP
 NG = R // KP
 NT = D // P
+BANKS = 8
+HALF = L // 2
+ALIGN = 64
+
 PAIRS = 3
 SWEEP = PAIRS * NC
 STEPS = SWEEP + NC
 LAST = STEPS - 1
+TURN_BANK = 2 * PAIRS
+SCALAR_ROUNDS = range(2, NC, 2)
 AHEAD = 7
-W_BUFS = 11
-G_COLS = 288
-S_ROUNDS = (2, 4, 6)
-EARLY = 3
-W0, W1, W2, W3 = 4, 3, 2, 1
-V_FIRST = 256
-LEAD = 3
-SECOND_QUEUE = 6
-Y_BANKS = (0, 1, 4, 6, 5, 7, 2, 3)
-ADD = mybir.AluOpType.add
+WIDE_BUFS = AHEAD + 4
+X_SPLIT = 288
 H_SPLIT = 352
+
+OUT_BANKS = (0, 1, 4, 6, 5, 7, 2, 3)
+LEAD = 2
+SINGLES = 4
+SHARED = range(5, NT - 4, 4)
+EARLY = 3
+SECOND_QUEUE = range(6, NT, 4)
 
 
 def step_of(n):
     if n < SWEEP:
         return n % PAIRS, n // PAIRS
     return PAIRS, n - SWEEP
+
+
+def place_of(n):
+    if n < SWEEP:
+        head = n - 1 if n % PAIRS == 2 else n
+    else:
+        head = n - n % 2
+    return head, 2 * P * (n - head)
 
 
 def tile_stap_clutter_removal_s13_kernel(tc, x, g, p_bytes, p_scale, a, v_words, v_scales, out):
@@ -63,38 +77,28 @@ def tile_stap_clutter_removal_s13_kernel(tc, x, g, p_bytes, p_scale, a, v_words,
         make_identity(nc, ident[:])
         g_rows = keep.tile([P, P], F32, name="g_rows")
         nc.gpsimd.memset(g_rows[:], 0.0)
-        warm = keep.tile([P, L], BF16, name="warm")
-        nc.vector.memset(warm[:], 0.0)
-        vs = keep.tile([P, NG, D], U8, name="vs", align_bytes=64)
+        vs = keep.tile([P, NG, D], U8, name="vs", align_bytes=ALIGN)
         nc.vector.memset(vs[:].rearrange("p g n -> p (g n)").bitcast(I32), 0)
 
-
-        def warm_up(count):
-            wb = bank(5, [P, L])
-            for i in range(count):
-                nc.tensor.matmul(out=wb[:], lhsT=warm[:, 0:P], rhs=warm[:], start=True, stop=True)
-
-        warm_up(W0)
         p_by = p_bytes.rearrange("(g m t) k -> g m t k", g=NG, t=PACK)
-        PB, xr = {}, {}
+        raw, x_rows = {}, {}
 
         def load_p(c, j0, j1):
             gg, t0 = j0 // 2, 2 * (j0 % 2)
             rows = 2 * (j1 - j0)
-            t = keep.tile([P, rows, KP], U8, name="pb_%d_%d" % (c, j0), align_bytes=64)
+            t = keep.tile([P, rows, KP], U8, name="pb_%d_%d" % (c, j0), align_bytes=ALIGN)
             nc.sync.dma_start(out=t[:], in_=p_by[gg][:, t0 : t0 + rows, KP * c : KP * (c + 1)])
             for j in range(j0, j1):
-                PB[(j, c)] = t[:, 2 * (j - j0) : 2 * (j - j0) + 2, :].rearrange("p r k -> p (r k)")
+                raw[(j, c)] = t[:, 2 * (j - j0) : 2 * (j - j0) + 2, :].rearrange("p r k -> p (r k)")
 
         def load_x(c):
-            t = work.tile([P, PACK, L], BF16, name="xr_%d" % c, tag="xr", bufs=8, align_bytes=64)
-            nc.sync.dma_start(out=t[:], in_=x[KP * c : KP * (c + 1), :].rearrange("(p j) l -> p j l", j=PACK))
-            xr[c] = t
+            x_rows[c] = work.tile([P, PACK, L], BF16, name="xr_%d" % c, tag="xr", bufs=NC, align_bytes=ALIGN)
+            nc.sync.dma_start(out=x_rows[c][:], in_=x[KP * c : KP * (c + 1), :].rearrange("(p j) l -> p j l", j=PACK))
 
         s4 = keep.tile([P, NC, 8], F32, name="s4")
         a_bf = keep.tile([P, NG, 16], BF16, name="a_bf")
         g_bf = keep.tile([P, P], BF16, name="g_bf")
-        pb_first = [keep.tile([P, KP], U8, name="pb_first%d" % j, align_bytes=64) for j in range(2)]
+        pb_first = [keep.tile([P, KP], U8, name="pb_first%d" % j, align_bytes=ALIGN) for j in range(2)]
         for j in range(2):
             nc.sync.dma_start(out=pb_first[j][:], in_=p_by[0][:, j, 0:KP])
         nc.scalar.dma_start(out=s4[:, :, 0:PACK], in_=p_scale.rearrange("o (c p t) -> p (o c) t", p=P, t=PACK))
@@ -107,91 +111,91 @@ def tile_stap_clutter_removal_s13_kernel(tc, x, g, p_bytes, p_scale, a, v_words,
             load_p(c, 0, 2)
             load_p(c, 2, 3)
             load_x(c)
-        pb_last = keep.tile([P, NC, 2, KP], U8, name="pb_last", align_bytes=64)
+        pb_last = keep.tile([P, NC, 2, KP], U8, name="pb_last", align_bytes=ALIGN)
         for t in range(2):
             nc.sync.dma_start(out=pb_last[:, :, t, :], in_=p_by[1][:, 2 + t, :].rearrange("m (c k) -> m c k", k=KP))
         for c in range(NC):
-            PB[(PAIRS, c)] = pb_last[:, c, :, :].rearrange("p r k -> p (r k)")
+            raw[(PAIRS, c)] = pb_last[:, c, :, :].rearrange("p r k -> p (r k)")
         for q in range(4):
             nc.sync.dma_start(
                 out=vs[32 * q : 32 * q + 4, :, :].bitcast(I32),
                 in_=v_scales[:, 4 * q : 4 * q + 4, :].rearrange("g q n -> q g n").bitcast(I32),
             )
-        vw = keep.tile([P, NG, 2 * D], U8, name="vw", align_bytes=64)
+        vw = keep.tile([P, NG, 2 * D], U8, name="vw", align_bytes=ALIGN)
         for gg in range(NG):
             nc.sync.dma_start(out=vw[:, gg, :].bitcast(I32), in_=v_words[gg].bitcast(I32))
 
-        xq = keep.tile([P, NC, L], U32, name="xq", align_bytes=64)
-        xs = keep.tile([P, NC, L], U8, name="xs", align_bytes=64)
-        hq = keep.tile([P, NG, L], U32, name="hq", align_bytes=64)
-        hs = keep.tile([P, NG, L], U8, name="hs", align_bytes=64)
-        hp = [keep.tile([P, PACK, L], BF16, name="hp%d" % gg, align_bytes=64) for gg in range(NG)]
-        hg = [keep.tile([P, L, PACK], BF16, name="hg%d" % gg, align_bytes=64) for gg in range(NG)]
+        xq = keep.tile([P, NC, L], U32, name="xq", align_bytes=ALIGN)
+        xs = keep.tile([P, NC, L], U8, name="xs", align_bytes=ALIGN)
+        hq = keep.tile([P, NG, L], U32, name="hq", align_bytes=ALIGN)
+        hs = keep.tile([P, NG, L], U8, name="hs", align_bytes=ALIGN)
+        h_planes = [keep.tile([P, PACK, L], BF16, name="hp%d" % gg, align_bytes=ALIGN) for gg in range(NG)]
+        h_packed = [keep.tile([P, L, PACK], BF16, name="hg%d" % gg, align_bytes=ALIGN) for gg in range(NG)]
         a_f = keep.tile([P, NG, PACK], F32, name="a_f")
         g_f = keep.tile([P, NT], F32, name="g_f")
 
-        W, TR, PG, PQ, PS, XG, XS, ACC, xn = {}, {}, {}, {}, {}, {}, {}, {}, {}
+        wide, turned, scaled, pq, ps, x_packed, sums, x_tiles = {}, {}, {}, {}, {}, {}, {}, {}
 
-        def load_xn(j):
-            xn[j] = work.tile([P, PACK, L], BF16, name="xn_%d" % j, tag="xr", bufs=8, align_bytes=64)
-            nc.sync.dma_start(out=xn[j][:], in_=x[KP * j : KP * (j + 1), :].rearrange("(i p) l -> p i l", p=P))
+        def load_x_tiles(j):
+            x_tiles[j] = work.tile([P, PACK, L], BF16, name="xn_%d" % j, tag="xr", bufs=NC, align_bytes=ALIGN)
+            nc.sync.dma_start(out=x_tiles[j][:], in_=x[KP * j : KP * (j + 1), :].rearrange("(i p) l -> p i l", p=P))
 
-        def widen(n):
-            W[n] = work.tile([P, 2 * KP], BF16, name="w", tag="w", bufs=W_BUFS, align_bytes=64)
-            nc.scalar.copy(out=W[n][:], in_=PB[step_of(n)].bitcast(E4M3))
+        def new_wide(n):
+            wide[n] = work.tile([P, 2 * KP], BF16, name="w", tag="w", bufs=WIDE_BUFS, align_bytes=ALIGN)
 
-        def turn(dst, words, j):
+        def widen_to(n):
+            for m in range(len(wide), min(n, LAST) + 1):
+                new_wide(m)
+                nc.scalar.copy(out=wide[m][:], in_=raw[step_of(m)].bitcast(E4M3))
+
+        def turn(dst, n, j):
+            words = wide[n][:].bitcast(F32)
             for u in range(2):
-                nc.tensor.transpose(dst[:, u, j, :], words[:, 256 * j + u : 256 * (j + 1) : 2], ident[:])
+                nc.tensor.transpose(dst[:, u, j, :], words[:, 2 * P * j + u : 2 * P * (j + 1) : 2], ident[:])
 
-        def transposes(n, b=None):
-            TR[n] = bank(6 + n % 2 if b is None else b, [P, 2, 2, P])
+        def transposes(n, b):
+            turned[n] = bank(b, [P, 2, 2, P])
             for j in range(2):
-                turn(TR[n], W[n][:].bitcast(F32), j)
+                turn(turned[n], n, j)
 
-        def place(n):
-            if n < SWEEP:
-                head = n - 1 if n % PAIRS == 2 else n
-            else:
-                head = n - n % 2
-            return head, 2 * P * (n - head)
+        def turn_bank(n):
+            return TURN_BANK + n % 2
 
-        def grouped(n):
-            head, col = place(n)
-            if head not in PG:
-                PG[head] = work.tile([P, 4 * P, PACK], BF16, name="pg", tag="pg", bufs=4, align_bytes=64)
-            return PG[head][:, col : col + 2 * P, :]
+        def scaled_of(n):
+            head, col = place_of(n)
+            if head not in scaled:
+                scaled[head] = work.tile([P, 4 * P, PACK], BF16, name="pg", tag="pg", bufs=4, align_bytes=ALIGN)
+            return scaled[head][:, col : col + 2 * P, :]
 
-        def halves(tr):
-            turned = tr[:].rearrange("p u j m -> p (u j m)").bitcast(BF16)
-            return turned.rearrange("p (u m e) -> p m u e", u=2, e=2)
+        def halves(words):
+            return words[:].rearrange("p u j m -> p (u j m)").bitcast(BF16).rearrange("p (u m e) -> p m u e", u=2, e=2)
 
-        def product(n, lo, hi, tr=None):
+        def product(n, words, lo=0, hi=2):
             c = step_of(n)[1]
             nc.vector.tensor_tensor(
-                out=grouped(n)[:, P * lo : P * hi, :].rearrange("p m (u e) -> p m u e", u=2),
-                in0=halves(TR[n] if tr is None else tr)[:, P * lo : P * hi, :, :],
+                out=scaled_of(n)[:, P * lo : P * hi, :].rearrange("p m (u e) -> p m u e", u=2),
+                in0=halves(words)[:, P * lo : P * hi, :, :],
                 in1=s4[:, c : c + 1, 0:PACK].to_broadcast([P, P * (hi - lo), PACK]),
                 op=MULT,
             )
 
-        def product_scalar(n):
+        def product_planes(n):
             c = step_of(n)[1]
-            planes = work.tile([P, PACK, 2 * P], BF16, name="planes", tag="planes", bufs=1, align_bytes=64)
+            planes = work.tile([P, PACK, 2 * P], BF16, name="planes", tag="planes", bufs=1, align_bytes=ALIGN)
             for t in range(PACK):
                 nc.scalar.activation(
-                    out=planes[:, t, :], in_=halves(TR[n])[:, :, t // 2, t % 2], func=COPY, scale=s4[:, c, t : t + 1]
+                    out=planes[:, t, :], in_=halves(turned[n])[:, :, t // 2, t % 2], func=COPY, scale=s4[:, c, t : t + 1]
                 )
             return planes
 
-        def quant_p(n, lo, hi):
-            if n not in PQ:
-                PQ[n] = work.tile([P, 4 * P], U32, name="pq", tag="pq", bufs=4, align_bytes=64)
-                PS[n] = work.tile([P, 4 * P], U8, name="ps", tag="ps", bufs=4, align_bytes=64)
+        def quant_p(head, lo, hi):
+            if head not in pq:
+                pq[head] = work.tile([P, 4 * P], U32, name="pq", tag="pq", bufs=4, align_bytes=ALIGN)
+                ps[head] = work.tile([P, 4 * P], U8, name="ps", tag="ps", bufs=4, align_bytes=ALIGN)
             nc.vector.quantize_mx(
-                out=PQ[n][:, P * lo : P * hi].bitcast(E4M3X4),
-                scales=PS[n][:, P * lo : P * hi],
-                in_=PG[n][:, P * lo : P * hi, :].rearrange("p m t -> p (m t)"),
+                out=pq[head][:, P * lo : P * hi].bitcast(E4M3X4),
+                scales=ps[head][:, P * lo : P * hi],
+                in_=scaled[head][:, P * lo : P * hi, :].rearrange("p m t -> p (m t)"),
             )
 
         def interleave(engine_copy, dst, src, lo, hi):
@@ -200,30 +204,34 @@ def tile_stap_clutter_removal_s13_kernel(tc, x, g, p_bytes, p_scale, a, v_words,
                 in_=src[:, :, lo:hi].rearrange("p t (c i) -> p c t i", i=4),
             )
 
-        def gpsimd_copy(out, in_):
-            nc.gpsimd.tensor_scalar(out=out, in0=in_, scalar1=1.0, scalar2=0.0, op0=MULT, op1=ADD)
-
-        def x_interleave(c):
-            XG[c] = work.tile([P, L, PACK], BF16, name="xg", tag="xg", bufs=1, align_bytes=64)
-            gpsimd_copy(XG[c][:, 0:G_COLS, :], xr[c][:, :, 0:G_COLS].rearrange("p t l -> p l t"))
-            interleave(nc.scalar.copy, XG[c], xr[c], G_COLS, L)
+        def interleave_x(c):
+            x_packed[c] = work.tile([P, L, PACK], BF16, name="xg", tag="xg", bufs=1, align_bytes=ALIGN)
+            nc.gpsimd.tensor_scalar(
+                out=x_packed[c][:, 0:X_SPLIT, :],
+                in0=x_rows[c][:, :, 0:X_SPLIT].rearrange("p t l -> p l t"),
+                scalar1=1.0,
+                scalar2=0.0,
+                op0=MULT,
+                op1=ADD,
+            )
+            interleave(nc.scalar.copy, x_packed[c], x_rows[c], X_SPLIT, L)
 
         def quant_x(c):
             nc.vector.quantize_mx(
-                out=xq[:, c, :].bitcast(E4M3X4), scales=xs[:, c, :], in_=XG[c][:].rearrange("p l t -> p (l t)")
+                out=xq[:, c, :].bitcast(E4M3X4), scales=xs[:, c, :], in_=x_packed[c][:].rearrange("p l t -> p (l t)")
             )
 
-        def mm(n, lo, hi):
+        def mm(n, lo=0, hi=2):
             pair, c = step_of(n)
-            head, col = place(n)
+            head, col = place_of(n)
             for j in range(lo, hi):
                 r = 2 * pair + j
                 if c == 0:
-                    ACC[r] = bank(r if r < 6 else r - PACK, [P, L])
+                    sums[r] = bank(r if r < 2 * PAIRS else r - PACK, [P, L])
                 nc.tensor.matmul_mx(
-                    out=ACC[r][:],
-                    lhsT=PQ[head][:, col + P * j : col + P * (j + 1)].bitcast(E4M3X4),
-                    lhsT_scale=PS[head][:, col + P * j : col + P * (j + 1)],
+                    out=sums[r][:],
+                    lhsT=pq[head][:, col + P * j : col + P * (j + 1)].bitcast(E4M3X4),
+                    lhsT_scale=ps[head][:, col + P * j : col + P * (j + 1)],
                     rhs=xq[:, c, :].bitcast(E4M3X4),
                     rhs_scale=xs[:, c, :],
                     start=(c == 0),
@@ -234,188 +242,190 @@ def tile_stap_clutter_removal_s13_kernel(tc, x, g, p_bytes, p_scale, a, v_words,
             nc.vector.quantize_mx(
                 out=hq[:, gg, lo:hi].bitcast(E4M3X4),
                 scales=hs[:, gg, lo:hi],
-                in_=hg[gg][:, lo:hi, :].rearrange("p l t -> p (l t)"),
+                in_=h_packed[gg][:, lo:hi, :].rearrange("p l t -> p (l t)"),
             )
 
         def h_scalar(r):
             gg, t = r // PACK, r % PACK
-            nc.scalar.activation(out=hp[gg][:, t, :], in_=ACC[r][:], func=COPY, scale=a_f[:, gg, t : t + 1])
+            nc.scalar.activation(out=h_planes[gg][:, t, :], in_=sums[r][:], func=COPY, scale=a_f[:, gg, t : t + 1])
 
         def h_vector(r, lo, hi):
             gg, t = r // PACK, r % PACK
             nc.vector.tensor_scalar(
-                out=hp[gg][:, t, lo:hi], in0=ACC[r][:, lo:hi], scalar1=a_f[:, gg, t : t + 1], scalar2=None, op0=MULT
+                out=h_planes[gg][:, t, lo:hi],
+                in0=sums[r][:, lo:hi],
+                scalar1=a_f[:, gg, t : t + 1],
+                scalar2=None,
+                op0=MULT,
             )
 
         nc.scalar.activation(out=a_f[:], in_=a_bf[:, :, 0:PACK], func=COPY)
         nc.scalar.copy(out=g_rows[0:NT, :], in_=g_bf[0:NT, :])
-        gt = bank(2, [P, P])
-        nc.tensor.transpose(gt[:], g_rows[:], ident[:])
-        W[0] = work.tile([P, 2 * KP], BF16, name="w", tag="w", bufs=W_BUFS, align_bytes=64)
-        first_tr = [bank(6, [P, 2, 2, P]), bank(0, [P, 2, 2, P])]
+        g_turned = bank(2, [P, P])
+        nc.tensor.transpose(g_turned[:], g_rows[:], ident[:])
+
+        new_wide(0)
+        first_banks = [bank(turn_bank(0), [P, 2, 2, P]), bank(0, [P, 2, 2, P])]
         for j in range(2):
-            nc.vector.tensor_copy(out=W[0][:, KP * j : KP * (j + 1)], in_=pb_first[j][:].bitcast(E4M3))
-            turn(first_tr[j], W[0][:].bitcast(F32), j)
-        widen(1)
-        nc.scalar.copy(out=g_f[:], in_=gt[:, 0:NT])
-        transposes(1)
-        warm_up(W1)
-        x_interleave(0)
-        widen(2)
+            nc.vector.tensor_copy(out=wide[0][:, KP * j : KP * (j + 1)], in_=pb_first[j][:].bitcast(E4M3))
+            turn(first_banks[j], 0, j)
+        widen_to(1)
+        nc.scalar.copy(out=g_f[:], in_=g_turned[:, 0:NT])
+        transposes(1, turn_bank(1))
+        interleave_x(0)
+        widen_to(2)
         for j in range(2):
-            product(0, j, j + 1, first_tr[j])
-        transposes(2)
-        warm_up(W2)
-        product(1, 0, 2)
-        widen(3)
-        transposes(3)
-        warm_up(W3)
+            product(0, first_banks[j], j, j + 1)
+        transposes(2, turn_bank(2))
+        product(1, turned[1])
+        widen_to(3)
+        transposes(3, turn_bank(3))
         quant_p(0, 0, 2)
         quant_x(0)
-        widened = 4
 
-        def widen_to(n, widened):
-            for m in range(widened, min(STEPS, n + 1)):
-                widen(m)
-            return max(widened, min(STEPS, n + 1))
-
-        for r in range(1, NC):
-            n = PAIRS * r
-            widened = widen_to(n + 1, widened)
-            x_interleave(r)
-            widened = widen_to(n + 2 if r in S_ROUNDS else n + AHEAD, widened)
-            if r > 1:
-                mm(n - 4, 0, 2)
-            product(n - 1, 0, 2)
-            transposes(n + 1)
-            mm(n - 3, 0, 2)
-            product(n, 0, 2)
-            if r in S_ROUNDS:
-                planes = product_scalar(n + 1)
-                widened = widen_to(widened, widened)
-                interleave(nc.scalar.copy, grouped(n + 1), planes, 0, 2 * P)
-                widened = widen_to(n + 3, widened)
-            transposes(n + 2)
+        for c in range(1, NC):
+            n = PAIRS * c
+            on_scalar = c in SCALAR_ROUNDS
+            widen_to(n + 1)
+            interleave_x(c)
+            widen_to(n + 2 if on_scalar else n + AHEAD)
+            if c > 1:
+                mm(n - 4)
+            product(n - 1, turned[n - 1])
+            transposes(n + 1, turn_bank(n + 1))
+            mm(n - 3)
+            product(n, turned[n])
+            if on_scalar:
+                planes = product_planes(n + 1)
+                widen_to(len(wide))
+                interleave(nc.scalar.copy, scaled_of(n + 1), planes, 0, 2 * P)
+            transposes(n + 2, turn_bank(n + 2))
             quant_p(n - 2, 0, 4)
-            mm(n - 2, 0, 2)
-            if r not in S_ROUNDS:
-                product(n + 1, 0, 2)
-            transposes(n + 3)
+            mm(n - 2)
+            if not on_scalar:
+                product(n + 1, turned[n + 1])
+            transposes(n + 3, turn_bank(n + 3))
             quant_p(n, 0, 2)
-            quant_x(r)
+            quant_x(c)
         for j in range(NC):
-            load_xn(j)
+            load_x_tiles(j)
+
         n = SWEEP
-        widen_to(LAST, widened)
-        mm(n - 4, 0, 2)
-        product(n - 1, 0, 2)
-        transposes(n + 1)
-        mm(n - 3, 0, 2)
+        widen_to(LAST)
+        mm(n - 4)
+        product(n - 1, turned[n - 1])
+        transposes(n + 1, turn_bank(n + 1))
+        mm(n - 3)
         h_scalar(0)
         h_scalar(1)
-        product(n, 0, 2)
-        transposes(n + 2)
+        product(n, turned[n])
+        transposes(n + 2, turn_bank(n + 2))
         quant_p(n - 2, 0, 4)
-        mm(n - 2, 0, 2)
+        mm(n - 2)
         h_scalar(2)
         h_scalar(3)
         transposes(n + 4, 0)
-        product(n + 1, 0, 2)
-        transposes(n + 3)
-        mm(n - 1, 0, 2)
-        planes = product_scalar(n + 4)
+        product(n + 1, turned[n + 1])
+        transposes(n + 3, turn_bank(n + 3))
+        mm(n - 1)
+        planes = product_planes(n + 4)
         h_scalar(4)
-        interleave(nc.scalar.copy, grouped(n + 4), planes, 0, 2 * P)
+        interleave(nc.scalar.copy, scaled_of(n + 4), planes, 0, 2 * P)
         transposes(n + 5, 1)
-        product(n + 2, 0, 2)
-        transposes(n + 6)
+        product(n + 2, turned[n + 2])
+        transposes(n + 6, turn_bank(n + 6))
         quant_p(n, 0, 4)
-        mm(n, 0, 2)
-        mm(n + 1, 0, 2)
-        product(n + 3, 0, 2)
-        transposes(n + 7)
-        product(n + 5, 0, 2)
+        mm(n)
+        mm(n + 1)
+        product(n + 3, turned[n + 3])
+        transposes(LAST, turn_bank(LAST))
+        product(n + 5, turned[n + 5])
         quant_p(n + 2, 0, 4)
-        mm(n + 2, 0, 2)
-        mm(n + 3, 0, 2)
-        for h in range(2):
-            interleave(nc.scalar.copy, hg[0], hp[0], 256 * h, 256 * (h + 1))
+        mm(n + 2)
+        mm(n + 3)
+        for lo in (0, HALF):
+            interleave(nc.scalar.copy, h_packed[0], h_planes[0], lo, lo + HALF)
         h_scalar(5)
-        product(n + 6, 0, 2)
+        product(n + 6, turned[n + 6])
         quant_p(n + 4, 0, 4)
-        mm(n + 4, 0, 2)
-        mm(n + 5, 0, 2)
-        product(LAST, 0, 1)
+        mm(n + 4)
+        mm(n + 5)
+        product(LAST, turned[LAST], 0, 1)
         quant_p(n + 6, 0, 2)
-        mm(n + 6, 0, 2)
-        product(LAST, 1, 2)
+        mm(n + 6)
+        product(LAST, turned[LAST], 1, 2)
         for j in range(2):
             quant_p(n + 6, 2 + j, 3 + j)
             mm(LAST, j, j + 1)
+
         quant_h(0, 0, L)
         h_scalar(6)
-        h_vector(7, 0, V_FIRST)
-        h_vector(7, V_FIRST, L)
-        interleave(nc.vector.tensor_copy, hg[1], hp[1], 0, V_FIRST)
-        interleave(nc.scalar.copy, hg[1], hp[1], H_SPLIT, L)
-        interleave(nc.vector.tensor_copy, hg[1], hp[1], V_FIRST, H_SPLIT)
-        quant_h(1, 0, V_FIRST)
-        quant_h(1, V_FIRST, L)
+        h_vector(7, 0, HALF)
+        h_vector(7, HALF, L)
+        interleave(nc.vector.tensor_copy, h_packed[1], h_planes[1], 0, HALF)
+        interleave(nc.scalar.copy, h_packed[1], h_planes[1], H_SPLIT, L)
+        interleave(nc.vector.tensor_copy, h_packed[1], h_planes[1], HALF, H_SPLIT)
+        quant_h(1, 0, HALF)
+        quant_h(1, HALF, L)
 
-        Y = {}
+        order = sorted(range(1, NT), key=lambda i: i - EARLY - 0.5 if i in SHARED else i)
+        jobs = [(0, 0, HALF), (0, HALF, L)] + [(i, 0, L) for i in order]
+        pair_heads = range(SINGLES, NT - 2, 2)
+        y, gx, o = {}, {}, {}
 
-        def y_pass(k, i, gg):
+        def y_pass(k, gg):
+            i, lo, hi = jobs[k]
             if gg == 0:
-                Y[i] = bank(Y_BANKS[k % 8], [P, L])
+                y[k] = bank(OUT_BANKS[k % BANKS], [P, hi - lo])
             nc.tensor.matmul_mx(
-                out=Y[i][:],
-                lhsT=vw[:, gg, 256 * i : 256 * (i + 1)].bitcast(E2M1X4),
+                out=y[k][:],
+                lhsT=vw[:, gg, 2 * P * i : 2 * P * (i + 1)].bitcast(E2M1X4),
                 lhsT_scale=vs[:, gg, P * i : P * (i + 1)],
-                rhs=hq[:, gg, :].bitcast(E4M3X4),
-                rhs_scale=hs[:, gg, :],
+                rhs=hq[:, gg, lo:hi].bitcast(E4M3X4),
+                rhs_scale=hs[:, gg, lo:hi],
                 start=(gg == 0),
                 stop=(gg == NG - 1),
             )
 
-        groups = [(i, i + 1) for i in range(4)] + [(i, i + 2) for i in range(4, NT - 2, 2)] + [(NT - 2, NT - 1), (NT - 1, NT)]
-        shared = [i for i in range(5, NT - 4, 4)]
-        order = sorted(range(NT), key=lambda i: i - EARLY - 0.5 if i in shared else i)
-        first, O, left = {}, {}, {}
-        for lo, hi in groups:
-            left[lo] = hi - lo
-            for i in range(lo, hi):
-                first[i] = lo
-        size = dict(left)
-
-        GX = {}
-
         def gained(i):
-            GX[i] = work.tile([P, L], F32, name="gx", tag="gx", bufs=3)
-            nc.scalar.activation(out=GX[i][:], in_=xn[i // 4][:, i % 4, :], func=COPY, scale=g_f[:, i : i + 1])
+            gx[i] = work.tile([P, L], F32, name="gx", tag="gx", bufs=3)
+            nc.scalar.activation(
+                out=gx[i][:], in_=x_tiles[i // PACK][:, i % PACK, :], func=COPY, scale=g_f[:, i : i + 1]
+            )
 
-        gained(shared[0])
-        for k in range(8):
-            y_pass(k, order[k], 0)
-        for k in range(NT):
-            i = order[k]
-            y_pass(k, i, 1)
-            if 8 <= k + LEAD < NT:
-                y_pass(k + LEAD, order[k + LEAD], 0)
-            lo = first[i]
-            if lo not in O:
-                O[lo] = work.tile([P, 2, L], F32, name="o", tag="o", bufs=7, align_bytes=64)
-            xi, gi, oi = xn[i // 4][:, i % 4, :], g_f[:, i : i + 1], O[lo][:, i - lo, :]
-            if i in shared:
+        gained(SHARED[0])
+        for k in range(BANKS):
+            y_pass(k, 0)
+        made = []
+        for k in range(len(jobs)):
+            i, lo, hi = jobs[k]
+            y_pass(k, 1)
+            if BANKS <= k + LEAD < len(jobs):
+                y_pass(k + LEAD, 0)
+            first = i - 1 if i - 1 in pair_heads else i
+            rows = 2 if first in pair_heads else 1
+            if first not in o:
+                o[first] = work.tile([P, 2, L], F32, name="o", tag="o", bufs=7, align_bytes=ALIGN)
+            dst = o[first][:, i - first, lo:hi]
+            if i in SHARED:
                 ys = work.tile([P, L], F32, name="ys", tag="ys", bufs=2)
-                nc.scalar.copy(out=ys[:], in_=Y[i][:])
-                if i != shared[-1]:
-                    gained(shared[shared.index(i) + 1])
-                nc.gpsimd.tensor_tensor(out=oi, in0=GX[i][:], in1=ys[:], op=SUB)
+                nc.scalar.copy(out=ys[:], in_=y[k][:])
+                if i != SHARED[-1]:
+                    gained(i + SHARED.step)
+                nc.gpsimd.tensor_tensor(out=dst, in0=gx[i][:], in1=ys[:], op=SUB)
             else:
-                nc.vector.scalar_tensor_tensor(out=oi, in0=xi, scalar=gi, in1=Y[i][:], op0=MULT, op1=SUB)
-            left[lo] = left[lo] - 1
-            if left[lo] == 0:
-                queue = nc.scalar if lo >= SECOND_QUEUE and lo % 4 == 2 else nc.sync
+                nc.vector.scalar_tensor_tensor(
+                    out=dst,
+                    in0=x_tiles[i // PACK][:, i % PACK, lo:hi],
+                    scalar=g_f[:, i : i + 1],
+                    in1=y[k][:],
+                    op0=MULT,
+                    op1=SUB,
+                )
+            made.append(i)
+            if all(j in made for j in range(first, first + rows)):
+                queue = nc.scalar if first in SECOND_QUEUE else nc.sync
                 queue.dma_start(
-                    out=out[P * lo : P * (lo + size[lo]), :].rearrange("(i p) l -> p i l", p=P), in_=O[lo][:, 0 : size[lo], :]
+                    out=out[P * first : P * (first + rows), lo:hi].rearrange("(i p) l -> p i l", p=P),
+                    in_=o[first][:, 0:rows, lo:hi],
                 )

@@ -34,13 +34,15 @@ SWEEP = PAIRS * NC
 STEPS = SWEEP + NC
 LAST = STEPS - 1
 TURN_BANK = 2 * PAIRS
-SCALAR_ROUNDS = range(2, NC, 2)
-AHEAD = 7
-WIDE_BUFS = AHEAD + 4
-X_SPLIT = 288
+VECTOR_ROUNDS = (0, 2, 5)
+LAG = 5
+AHEAD = 9
+WIDE_BUFS = 10
+X_SPLIT = 384
+X0_SPLIT = 448
 H_SPLIT = 352
 
-OUT_BANKS = (0, 1, 4, 6, 5, 7, 2, 3)
+OUT_BANKS = (4, 5, 6, 7, 3, 2, 0, 1)
 LEAD = 2
 SINGLES = 4
 SHARED = range(5, NT - 4, 4)
@@ -55,10 +57,7 @@ def step_of(n):
 
 
 def place_of(n):
-    if n < SWEEP:
-        head = n - 1 if n % PAIRS == 2 else n
-    else:
-        head = n - n % 2
+    head = n - n % PAIRS if n < SWEEP else n - n % 2
     return head, 2 * P * (n - head)
 
 
@@ -75,10 +74,6 @@ def tile_stap_clutter_removal_s13_kernel(tc, x, g, p_bytes, p_scale, a, v_words,
 
         ident = keep.tile([P, P], F32, name="ident")
         make_identity(nc, ident[:])
-        g_rows = keep.tile([P, P], F32, name="g_rows")
-        nc.gpsimd.memset(g_rows[:], 0.0)
-        vs = keep.tile([P, NG, D], U8, name="vs", align_bytes=ALIGN)
-        nc.vector.memset(vs[:].rearrange("p g n -> p (g n)").bitcast(I32), 0)
 
         p_by = p_bytes.rearrange("(g m t) k -> g m t k", g=NG, t=PACK)
         raw, x_rows = {}, {}
@@ -95,19 +90,28 @@ def tile_stap_clutter_removal_s13_kernel(tc, x, g, p_bytes, p_scale, a, v_words,
             x_rows[c] = work.tile([P, PACK, L], BF16, name="xr_%d" % c, tag="xr", bufs=NC, align_bytes=ALIGN)
             nc.sync.dma_start(out=x_rows[c][:], in_=x[KP * c : KP * (c + 1), :].rearrange("(p j) l -> p j l", j=PACK))
 
-        s4 = keep.tile([P, NC, 8], F32, name="s4")
+        s_first = keep.tile([P, 1, 8], F32, name="s_first")
+        s_rest = keep.tile([P, NC - 1, 8], F32, name="s_rest")
+        s_by = p_scale.rearrange("o (c p t) -> p (o c) t", p=P, t=PACK)
         a_bf = keep.tile([P, NG, 16], BF16, name="a_bf")
         g_bf = keep.tile([P, P], BF16, name="g_bf")
+
+        def scales(c):
+            return s_first[:, 0:1, 0:PACK] if c == 0 else s_rest[:, c - 1 : c, 0:PACK]
+
         pb_first = [keep.tile([P, KP], U8, name="pb_first%d" % j, align_bytes=ALIGN) for j in range(2)]
         for j in range(2):
             nc.sync.dma_start(out=pb_first[j][:], in_=p_by[0][:, j, 0:KP])
-        nc.scalar.dma_start(out=s4[:, :, 0:PACK], in_=p_scale.rearrange("o (c p t) -> p (o c) t", p=P, t=PACK))
         nc.scalar.dma_start(out=a_bf[:, :, 0:PACK], in_=a.rearrange("(g m t) -> m g t", g=NG, t=PACK))
-        nc.scalar.dma_start(out=g_bf[0:NT, :], in_=g.rearrange("(i p) -> i p", p=P))
+        nc.scalar.dma_start(out=s_first[:, :, 0:PACK], in_=s_by[:, 0:1, :])
         load_p(0, 1, 2)
         load_x(0)
         load_p(0, 2, 3)
-        for c in range(1, NC):
+        load_p(1, 0, 2)
+        nc.sync.dma_start(out=s_rest[:, :, 0:PACK], in_=s_by[:, 1:NC, :])
+        load_p(1, 2, 3)
+        load_x(1)
+        for c in range(2, NC):
             load_p(c, 0, 2)
             load_p(c, 2, 3)
             load_x(c)
@@ -116,6 +120,11 @@ def tile_stap_clutter_removal_s13_kernel(tc, x, g, p_bytes, p_scale, a, v_words,
             nc.sync.dma_start(out=pb_last[:, :, t, :], in_=p_by[1][:, 2 + t, :].rearrange("m (c k) -> m c k", k=KP))
         for c in range(NC):
             raw[(PAIRS, c)] = pb_last[:, c, :, :].rearrange("p r k -> p (r k)")
+        nc.sync.dma_start(out=g_bf[0:NT, :], in_=g.rearrange("(i p) -> i p", p=P))
+        vs = keep.tile([P, NG, D], U8, name="vs", align_bytes=ALIGN)
+        nc.vector.memset(vs[:].rearrange("p g n -> p (g n)").bitcast(I32), 0)
+        g_rows = keep.tile([P, P], F32, name="g_rows")
+        nc.gpsimd.memset(g_rows[:], 0.0)
         for q in range(4):
             nc.sync.dma_start(
                 out=vs[32 * q : 32 * q + 4, :, :].bitcast(I32),
@@ -164,7 +173,7 @@ def tile_stap_clutter_removal_s13_kernel(tc, x, g, p_bytes, p_scale, a, v_words,
         def scaled_of(n):
             head, col = place_of(n)
             if head not in scaled:
-                scaled[head] = work.tile([P, 4 * P, PACK], BF16, name="pg", tag="pg", bufs=4, align_bytes=ALIGN)
+                scaled[head] = work.tile([P, 6 * P, PACK], BF16, name="pg", tag="pg", bufs=3, align_bytes=ALIGN)
             return scaled[head][:, col : col + 2 * P, :]
 
         def halves(words):
@@ -175,7 +184,7 @@ def tile_stap_clutter_removal_s13_kernel(tc, x, g, p_bytes, p_scale, a, v_words,
             nc.vector.tensor_tensor(
                 out=scaled_of(n)[:, P * lo : P * hi, :].rearrange("p m (u e) -> p m u e", u=2),
                 in0=halves(words)[:, P * lo : P * hi, :, :],
-                in1=s4[:, c : c + 1, 0:PACK].to_broadcast([P, P * (hi - lo), PACK]),
+                in1=scales(c).to_broadcast([P, P * (hi - lo), PACK]),
                 op=MULT,
             )
 
@@ -184,18 +193,19 @@ def tile_stap_clutter_removal_s13_kernel(tc, x, g, p_bytes, p_scale, a, v_words,
             planes = work.tile([P, PACK, 2 * P], BF16, name="planes", tag="planes", bufs=1, align_bytes=ALIGN)
             for t in range(PACK):
                 nc.scalar.activation(
-                    out=planes[:, t, :], in_=halves(turned[n])[:, :, t // 2, t % 2], func=COPY, scale=s4[:, c, t : t + 1]
+                    out=planes[:, t, :], in_=halves(turned[n])[:, :, t // 2, t % 2], func=COPY, scale=scales(c)[:, 0, t : t + 1]
                 )
             return planes
 
-        def quant_p(head, lo, hi):
+        def quant_p(head, lo, hi, src=None):
             if head not in pq:
-                pq[head] = work.tile([P, 4 * P], U32, name="pq", tag="pq", bufs=4, align_bytes=ALIGN)
-                ps[head] = work.tile([P, 4 * P], U8, name="ps", tag="ps", bufs=4, align_bytes=ALIGN)
+                pq[head] = work.tile([P, 6 * P], U32, name="pq", tag="pq", bufs=3, align_bytes=ALIGN)
+                ps[head] = work.tile([P, 6 * P], U8, name="ps", tag="ps", bufs=3, align_bytes=ALIGN)
+            src = scaled[head][:, P * lo : P * hi, :] if src is None else src
             nc.vector.quantize_mx(
                 out=pq[head][:, P * lo : P * hi].bitcast(E4M3X4),
                 scales=ps[head][:, P * lo : P * hi],
-                in_=scaled[head][:, P * lo : P * hi, :].rearrange("p m t -> p (m t)"),
+                in_=src.rearrange("p m t -> p (m t)"),
             )
 
         def interleave(engine_copy, dst, src, lo, hi):
@@ -204,17 +214,18 @@ def tile_stap_clutter_removal_s13_kernel(tc, x, g, p_bytes, p_scale, a, v_words,
                 in_=src[:, :, lo:hi].rearrange("p t (c i) -> p c t i", i=4),
             )
 
-        def interleave_x(c):
-            x_packed[c] = work.tile([P, L, PACK], BF16, name="xg", tag="xg", bufs=1, align_bytes=ALIGN)
+        def new_packed():
+            return work.tile([P, L, PACK], BF16, name="xg", tag="xg", bufs=1, align_bytes=ALIGN)
+
+        def interleave_gpsimd(dst, src, lo, hi):
             nc.gpsimd.tensor_scalar(
-                out=x_packed[c][:, 0:X_SPLIT, :],
-                in0=x_rows[c][:, :, 0:X_SPLIT].rearrange("p t l -> p l t"),
+                out=dst[:, lo:hi, :],
+                in0=src[:, :, lo:hi].rearrange("p t l -> p l t"),
                 scalar1=1.0,
                 scalar2=0.0,
                 op0=MULT,
                 op1=ADD,
             )
-            interleave(nc.scalar.copy, x_packed[c], x_rows[c], X_SPLIT, L)
 
         def quant_x(c):
             nc.vector.quantize_mx(
@@ -227,7 +238,7 @@ def tile_stap_clutter_removal_s13_kernel(tc, x, g, p_bytes, p_scale, a, v_words,
             for j in range(lo, hi):
                 r = 2 * pair + j
                 if c == 0:
-                    sums[r] = bank(r if r < 2 * PAIRS else r - PACK, [P, L])
+                    sums[r] = bank(r % (2 * PAIRS), [P, L])
                 nc.tensor.matmul_mx(
                     out=sums[r][:],
                     lhsT=pq[head][:, col + P * j : col + P * (j + 1)].bitcast(E4M3X4),
@@ -238,11 +249,11 @@ def tile_stap_clutter_removal_s13_kernel(tc, x, g, p_bytes, p_scale, a, v_words,
                     stop=(c == NC - 1),
                 )
 
-        def quant_h(gg, lo, hi):
+        def quant_h(gg, lo, hi, src):
             nc.vector.quantize_mx(
                 out=hq[:, gg, lo:hi].bitcast(E4M3X4),
                 scales=hs[:, gg, lo:hi],
-                in_=h_packed[gg][:, lo:hi, :].rearrange("p l t -> p (l t)"),
+                in_=src[:, lo:hi, :].rearrange("p l t -> p (l t)"),
             )
 
         def h_scalar(r):
@@ -259,97 +270,116 @@ def tile_stap_clutter_removal_s13_kernel(tc, x, g, p_bytes, p_scale, a, v_words,
                 op0=MULT,
             )
 
-        nc.scalar.activation(out=a_f[:], in_=a_bf[:, :, 0:PACK], func=COPY)
-        nc.scalar.copy(out=g_rows[0:NT, :], in_=g_bf[0:NT, :])
-        g_turned = bank(2, [P, P])
-        nc.tensor.transpose(g_turned[:], g_rows[:], ident[:])
+        def turn_and_multiply(n, b):
+            transposes(n, b)
+            if n >= LAG:
+                mm(n - LAG)
 
+        def tb(n):
+            return turn_bank(n + 1)
+
+        def pack_x(c, split):
+            x_packed[c] = new_packed()
+            interleave_gpsimd(x_packed[c], x_rows[c], 0, split)
+
+        def pack_x_rest(c, split):
+            if split < L:
+                interleave(nc.scalar.copy, x_packed[c], x_rows[c], split, L)
+
+        nc.scalar.activation(out=a_f[:], in_=a_bf[:, :, 0:PACK], func=COPY)
         new_wide(0)
-        first_banks = [bank(turn_bank(0), [P, 2, 2, P]), bank(0, [P, 2, 2, P])]
+        first_banks = [bank(turn_bank(0), [P, 2, 2, P]), bank(1, [P, 2, 2, P])]
         for j in range(2):
-            nc.vector.tensor_copy(out=wide[0][:, KP * j : KP * (j + 1)], in_=pb_first[j][:].bitcast(E4M3))
+            nc.scalar.copy(out=wide[0][:, KP * j : KP * (j + 1)], in_=pb_first[j][:].bitcast(E4M3))
             turn(first_banks[j], 0, j)
         widen_to(1)
-        nc.scalar.copy(out=g_f[:], in_=g_turned[:, 0:NT])
         transposes(1, turn_bank(1))
-        interleave_x(0)
         widen_to(2)
+        transposes(2, 5)
+        pack_x(0, X0_SPLIT)
         for j in range(2):
             product(0, first_banks[j], j, j + 1)
-        transposes(2, turn_bank(2))
-        product(1, turned[1])
         widen_to(3)
-        transposes(3, turn_bank(3))
-        quant_p(0, 0, 2)
+        transposes(3, tb(3))
+        product(1, turned[1])
+        widen_to(4)
+        transposes(4, tb(4))
+        pack_x_rest(0, X0_SPLIT)
+        widen_to(5)
+        product(2, turned[2])
+        if 1 not in VECTOR_ROUNDS:
+            planes = product_planes(3)
+        quant_p(0, 0, 4)
         quant_x(0)
+        quant_p(0, 4, 6)
 
         for c in range(1, NC):
             n = PAIRS * c
-            on_scalar = c in SCALAR_ROUNDS
-            widen_to(n + 1)
-            interleave_x(c)
-            widen_to(n + 2 if on_scalar else n + AHEAD)
-            if c > 1:
-                mm(n - 4)
-            product(n - 1, turned[n - 1])
-            transposes(n + 1, turn_bank(n + 1))
-            mm(n - 3)
-            product(n, turned[n])
+            on_scalar = c not in VECTOR_ROUNDS
+            split = X_SPLIT if on_scalar else L
+            pack_x(c, split)
             if on_scalar:
-                planes = product_planes(n + 1)
                 widen_to(len(wide))
-                interleave(nc.scalar.copy, scaled_of(n + 1), planes, 0, 2 * P)
-            transposes(n + 2, turn_bank(n + 2))
-            quant_p(n - 2, 0, 4)
-            mm(n - 2)
-            if not on_scalar:
-                product(n + 1, turned[n + 1])
-            transposes(n + 3, turn_bank(n + 3))
-            quant_p(n, 0, 2)
+                interleave(nc.scalar.copy, scaled_of(n), planes, 0, 2 * P)
+            else:
+                widen_to(n + 2)
+                product(n, turned[n])
+            turn_and_multiply(n + 2, tb(n + 2))
+            widen_to(n + 3 if on_scalar else n + AHEAD)
+            product(n + 1, turned[n + 1])
+            turn_and_multiply(n + 3, tb(n + 3))
+            pack_x_rest(c, split)
+            widen_to(n + 4)
+            if c + 1 not in VECTOR_ROUNDS:
+                widen_to(n + 5)
+                planes = product_planes(n + 3)
+            product(n + 2, turned[n + 2])
+            turn_and_multiply(n + 4, tb(n + 4))
+            quant_p(n, 0, 4)
             quant_x(c)
+            quant_p(n, 4, 6)
         for j in range(NC):
             load_x_tiles(j)
 
         n = SWEEP
-        widen_to(LAST)
-        mm(n - 4)
-        product(n - 1, turned[n - 1])
-        transposes(n + 1, turn_bank(n + 1))
-        mm(n - 3)
+        own = new_packed()
+        interleave_gpsimd(own, planes, 0, 2 * P)
+        turn_and_multiply(n + 2, tb(n + 2))
+        widen_to(n + 5)
         h_scalar(0)
         h_scalar(1)
-        product(n, turned[n])
-        transposes(n + 2, turn_bank(n + 2))
-        quant_p(n - 2, 0, 4)
-        mm(n - 2)
+        product(n + 1, turned[n + 1])
+        turn_and_multiply(n + 3, tb(n + 3))
         h_scalar(2)
         h_scalar(3)
-        transposes(n + 4, 0)
-        product(n + 1, turned[n + 1])
-        transposes(n + 3, turn_bank(n + 3))
-        mm(n - 1)
-        planes = product_planes(n + 4)
-        h_scalar(4)
-        interleave(nc.scalar.copy, scaled_of(n + 4), planes, 0, 2 * P)
-        transposes(n + 5, 1)
         product(n + 2, turned[n + 2])
-        transposes(n + 6, turn_bank(n + 6))
-        quant_p(n, 0, 4)
-        mm(n)
-        mm(n + 1)
+        turn_and_multiply(n + 4, tb(n + 4))
+        quant_p(n, 2, 4)
+        quant_p(n, 0, 2, own[:, 0 : 2 * P, :])
+        h_own = new_packed()
+        interleave_gpsimd(h_own, h_planes[0], 0, HALF)
+        widen_to(LAST)
         product(n + 3, turned[n + 3])
-        transposes(LAST, turn_bank(LAST))
+        turn_and_multiply(n + 5, tb(n + 5))
+        product(n + 4, turned[n + 4])
+        transposes(n + 6, tb(n + 6))
+        mm(n + 1)
+        transposes(LAST, 2)
+        interleave(nc.scalar.copy, h_packed[0], h_planes[0], HALF, L)
+        h_scalar(4)
+        h_scalar(5)
+        nc.scalar.copy(out=g_rows[0:NT, :], in_=g_bf[0:NT, :])
         product(n + 5, turned[n + 5])
         quant_p(n + 2, 0, 4)
         mm(n + 2)
         mm(n + 3)
-        for lo in (0, HALF):
-            interleave(nc.scalar.copy, h_packed[0], h_planes[0], lo, lo + HALF)
-        h_scalar(5)
-        product(n + 6, turned[n + 6])
         quant_p(n + 4, 0, 4)
         mm(n + 4)
         mm(n + 5)
+        product(n + 6, turned[n + 6])
+        g_turned = bank(3, [P, P])
+        nc.tensor.transpose(g_turned[:], g_rows[:], ident[:])
+        nc.scalar.copy(out=g_f[:], in_=g_turned[:, 0:NT])
         product(LAST, turned[LAST], 0, 1)
         quant_p(n + 6, 0, 2)
         mm(n + 6)
@@ -358,15 +388,16 @@ def tile_stap_clutter_removal_s13_kernel(tc, x, g, p_bytes, p_scale, a, v_words,
             quant_p(n + 6, 2 + j, 3 + j)
             mm(LAST, j, j + 1)
 
-        quant_h(0, 0, L)
+        quant_h(0, 0, HALF, h_own)
+        quant_h(0, HALF, L, h_packed[0])
         h_scalar(6)
         h_vector(7, 0, HALF)
         h_vector(7, HALF, L)
         interleave(nc.vector.tensor_copy, h_packed[1], h_planes[1], 0, HALF)
         interleave(nc.scalar.copy, h_packed[1], h_planes[1], H_SPLIT, L)
         interleave(nc.vector.tensor_copy, h_packed[1], h_planes[1], HALF, H_SPLIT)
-        quant_h(1, 0, HALF)
-        quant_h(1, HALF, L)
+        quant_h(1, 0, HALF, h_packed[1])
+        quant_h(1, HALF, L, h_packed[1])
 
         order = sorted(range(1, NT), key=lambda i: i - EARLY - 0.5 if i in SHARED else i)
         jobs = [(0, 0, HALF), (0, HALF, L)] + [(i, 0, L) for i in order]

@@ -35,6 +35,7 @@ STEPS = SWEEP + NC
 LAST = STEPS - 1
 TURN_BANK = 2 * PAIRS
 VECTOR_ROUNDS = (0, 2, 5)
+WORD_STEPS = (9, 10, 18, 19, 29, 30, 31)
 LAG = 5
 AHEAD = 9
 WIDE_BUFS = 10
@@ -69,9 +70,11 @@ def tile_stap_clutter_removal_s13_kernel(tc, x, g, p_bytes, p_scale, a, v_words,
         psum = ctx.enter_context(tc.psum_pool(name="psum", bufs=1))
         ctx.enter_context(tc.manual_schedule())
 
-        def bank(b, shape):
-            return psum.tile(shape, F32, name="bank%d" % b, tag="bank%d" % b)
+        def bank(b, shape, dtype=F32):
+            return psum.tile(shape, dtype, name="bank%d" % b, tag="bank%d" % b)
 
+        ident_bf = keep.tile([P, P], BF16, name="ident_bf")
+        make_identity(nc, ident_bf[:])
         ident = keep.tile([P, P], F32, name="ident")
         make_identity(nc, ident[:])
 
@@ -95,6 +98,7 @@ def tile_stap_clutter_removal_s13_kernel(tc, x, g, p_bytes, p_scale, a, v_words,
         s_by = p_scale.rearrange("o (c p t) -> p (o c) t", p=P, t=PACK)
         a_bf = keep.tile([P, NG, 16], BF16, name="a_bf")
         g_bf = keep.tile([P, P], BF16, name="g_bf")
+        nc.gpsimd.memset(g_bf[:], 0.0)
 
         def scales(c):
             return s_first[:, 0:1, 0:PACK] if c == 0 else s_rest[:, c - 1 : c, 0:PACK]
@@ -123,8 +127,6 @@ def tile_stap_clutter_removal_s13_kernel(tc, x, g, p_bytes, p_scale, a, v_words,
         nc.sync.dma_start(out=g_bf[0:NT, :], in_=g.rearrange("(i p) -> i p", p=P))
         vs = keep.tile([P, NG, D], U8, name="vs", align_bytes=ALIGN)
         nc.vector.memset(vs[:].rearrange("p g n -> p (g n)").bitcast(I32), 0)
-        g_rows = keep.tile([P, P], F32, name="g_rows")
-        nc.gpsimd.memset(g_rows[:], 0.0)
         for q in range(4):
             nc.sync.dma_start(
                 out=vs[32 * q : 32 * q + 4, :, :].bitcast(I32),
@@ -157,13 +159,28 @@ def tile_stap_clutter_removal_s13_kernel(tc, x, g, p_bytes, p_scale, a, v_words,
                 new_wide(m)
                 nc.scalar.copy(out=wide[m][:], in_=raw[step_of(m)].bitcast(E4M3))
 
+        def new_turned(n, b):
+            if n in WORD_STEPS:
+                return bank(b, [P, 2, 2, P])
+            return bank(b, [P, PACK, 2, P], BF16)
+
         def turn(dst, n, j):
-            words = wide[n][:].bitcast(F32)
-            for u in range(2):
-                nc.tensor.transpose(dst[:, u, j, :], words[:, 2 * P * j + u : 2 * P * (j + 1) : 2], ident[:])
+            if n in WORD_STEPS:
+                words = wide[n][:].bitcast(F32)
+                for u in range(2):
+                    nc.tensor.transpose(dst[:, u, j, :], words[:, 2 * P * j + u : 2 * P * (j + 1) : 2], ident[:])
+            else:
+                for t in range(PACK):
+                    nc.tensor.matmul(
+                        dst[:, t, j, :],
+                        lhsT=wide[n][:, KP * j + t : KP * (j + 1) : PACK],
+                        rhs=ident_bf[:],
+                        start=True,
+                        stop=True,
+                    )
 
         def transposes(n, b):
-            turned[n] = bank(b, [P, 2, 2, P])
+            turned[n] = new_turned(n, b)
             for j in range(2):
                 turn(turned[n], n, j)
 
@@ -179,22 +196,33 @@ def tile_stap_clutter_removal_s13_kernel(tc, x, g, p_bytes, p_scale, a, v_words,
         def halves(words):
             return words[:].rearrange("p u j m -> p (u j m)").bitcast(BF16).rearrange("p (u m e) -> p m u e", u=2, e=2)
 
-        def product(n, words, lo=0, hi=2):
+        def product(n, src, lo=0, hi=2):
             c = step_of(n)[1]
-            nc.vector.tensor_tensor(
-                out=scaled_of(n)[:, P * lo : P * hi, :].rearrange("p m (u e) -> p m u e", u=2),
-                in0=halves(words)[:, P * lo : P * hi, :, :],
-                in1=scales(c).to_broadcast([P, P * (hi - lo), PACK]),
-                op=MULT,
-            )
+            dst = scaled_of(n)[:, P * lo : P * hi, :]
+            if n in WORD_STEPS:
+                nc.vector.tensor_tensor(
+                    out=dst.rearrange("p m (u e) -> p m u e", u=2),
+                    in0=halves(src)[:, P * lo : P * hi, :, :],
+                    in1=scales(c).to_broadcast([P, P * (hi - lo), PACK]),
+                    op=MULT,
+                )
+            else:
+                nc.vector.tensor_tensor(
+                    out=dst.rearrange("p (m i) t -> p m t i", i=2),
+                    in0=src[:, :, lo:hi, :].rearrange("p t j (m i) -> p (j m) t i", i=2),
+                    in1=scales(c).unsqueeze(3).to_broadcast([P, P * (hi - lo) // 2, PACK, 2]),
+                    op=MULT,
+                )
 
         def product_planes(n):
             c = step_of(n)[1]
             planes = work.tile([P, PACK, 2 * P], BF16, name="planes", tag="planes", bufs=1, align_bytes=ALIGN)
             for t in range(PACK):
-                nc.scalar.activation(
-                    out=planes[:, t, :], in_=halves(turned[n])[:, :, t // 2, t % 2], func=COPY, scale=scales(c)[:, 0, t : t + 1]
-                )
+                if n in WORD_STEPS:
+                    src = halves(turned[n])[:, :, t // 2, t % 2]
+                else:
+                    src = turned[n][:, t, :, :].rearrange("p j m -> p (j m)")
+                nc.scalar.activation(out=planes[:, t, :], in_=src, func=COPY, scale=scales(c)[:, 0, t : t + 1])
             return planes
 
         def quant_p(head, lo, hi, src=None):
@@ -288,7 +316,7 @@ def tile_stap_clutter_removal_s13_kernel(tc, x, g, p_bytes, p_scale, a, v_words,
 
         nc.scalar.activation(out=a_f[:], in_=a_bf[:, :, 0:PACK], func=COPY)
         new_wide(0)
-        first_banks = [bank(turn_bank(0), [P, 2, 2, P]), bank(1, [P, 2, 2, P])]
+        first_banks = [new_turned(0, turn_bank(0)), new_turned(0, 1)]
         for j in range(2):
             nc.scalar.copy(out=wide[0][:, KP * j : KP * (j + 1)], in_=pb_first[j][:].bitcast(E4M3))
             turn(first_banks[j], 0, j)
@@ -368,7 +396,6 @@ def tile_stap_clutter_removal_s13_kernel(tc, x, g, p_bytes, p_scale, a, v_words,
         interleave(nc.scalar.copy, h_packed[0], h_planes[0], HALF, L)
         h_scalar(4)
         h_scalar(5)
-        nc.scalar.copy(out=g_rows[0:NT, :], in_=g_bf[0:NT, :])
         product(n + 5, turned[n + 5])
         quant_p(n + 2, 0, 4)
         mm(n + 2)
@@ -377,9 +404,9 @@ def tile_stap_clutter_removal_s13_kernel(tc, x, g, p_bytes, p_scale, a, v_words,
         mm(n + 4)
         mm(n + 5)
         product(n + 6, turned[n + 6])
-        g_turned = bank(3, [P, P])
-        nc.tensor.transpose(g_turned[:], g_rows[:], ident[:])
-        nc.scalar.copy(out=g_f[:], in_=g_turned[:, 0:NT])
+        g_turned = bank(3, [P, NT])
+        nc.tensor.matmul(g_turned[:], lhsT=g_bf[:], rhs=ident_bf[:, 0:NT], start=True, stop=True)
+        nc.scalar.copy(out=g_f[:], in_=g_turned[:])
         product(LAST, turned[LAST], 0, 1)
         quant_p(n + 6, 0, 2)
         mm(n + 6)

@@ -29,21 +29,24 @@ BANKS = 8
 HALF = L // 2
 ALIGN = 64
 
-PAIRS = 3
-SWEEP = PAIRS * NC
-STEPS = SWEEP + NC
+FIRST = 5
+PERIODS = NC // 2
+SWEEP = FIRST * PERIODS
+STEPS = SWEEP + 3 * PERIODS
 LAST = STEPS - 1
-TURN_BANK = 2 * PAIRS
-VECTOR_ROUNDS = (0, 2, 5)
-WORD_STEPS = (9, 10, 18, 19, 29, 30, 31)
-LAG = 5
-AHEAD = 9
-WIDE_BUFS = 10
-X_SPLIT = 384
+TURN_BANKS = 3
+TURN_STEPS = (7, 8, 11, 12, 13, 16, 17)
+TURN_UNITS = [(n, j) for n in TURN_STEPS for j in range(2)][1:]
+SCALAR_PERIODS = (1, 2, 3)
+WIDE_BUFS = 9
+X_SPLIT = 352
 X0_SPLIT = 448
+X1_SPLIT = 352
+AHEAD = (8, 8, 8, 8)
+AFTER = (9, 9, 9, 11)
 H_SPLIT = 352
 
-OUT_BANKS = (4, 5, 6, 7, 3, 2, 0, 1)
+OUT_BANKS = (4, 3, 6, 7, 5, 0, 1, 2)
 LEAD = 2
 SINGLES = 4
 SHARED = range(5, NT - 4, 4)
@@ -51,15 +54,17 @@ EARLY = 3
 SECOND_QUEUE = range(6, NT, 4)
 
 
-def step_of(n):
+def units_of(n):
     if n < SWEEP:
-        return n % PAIRS, n // PAIRS
-    return PAIRS, n - SWEEP
-
-
-def place_of(n):
-    head = n - n % PAIRS if n < SWEEP else n - n % 2
-    return head, 2 * P * (n - head)
+        c, i = 2 * (n // FIRST), n % FIRST
+        if i == 2:
+            return (4, c), (4, c + 1)
+        r, c = 2 * (i % 3), c + i // 3
+        return (r, c), (r + 1, c)
+    c, i = 2 * ((n - SWEEP) // 3), (n - SWEEP) % 3
+    if i == 2:
+        return (7, c), (7, c + 1)
+    return (5, c + i), (6, c + i)
 
 
 def tile_stap_clutter_removal_s13_kernel(tc, x, g, p_bytes, p_scale, a, v_words, v_scales, out):
@@ -75,55 +80,60 @@ def tile_stap_clutter_removal_s13_kernel(tc, x, g, p_bytes, p_scale, a, v_words,
 
         ident_bf = keep.tile([P, P], BF16, name="ident_bf")
         make_identity(nc, ident_bf[:])
-        ident = keep.tile([P, P], F32, name="ident")
-        make_identity(nc, ident[:])
 
         p_by = p_bytes.rearrange("(g m t) k -> g m t k", g=NG, t=PACK)
         raw, x_rows = {}, {}
 
-        def load_p(c, j0, j1):
-            gg, t0 = j0 // 2, 2 * (j0 % 2)
-            rows = 2 * (j1 - j0)
-            t = keep.tile([P, rows, KP], U8, name="pb_%d_%d" % (c, j0), align_bytes=ALIGN)
-            nc.sync.dma_start(out=t[:], in_=p_by[gg][:, t0 : t0 + rows, KP * c : KP * (c + 1)])
-            for j in range(j0, j1):
-                raw[(j, c)] = t[:, 2 * (j - j0) : 2 * (j - j0) + 2, :].rearrange("p r k -> p (r k)")
+        def load_p(n, steps):
+            (r, c), (r2, c2) = units_of(n)[0], units_of(n + steps - 1)[1]
+            t = keep.tile([P, r2 - r + 1, KP * (c2 - c + 1)], U8, name="pb_%d" % n, align_bytes=ALIGN)
+            nc.sync.dma_start(out=t[:], in_=p_by[r // PACK][:, r % PACK : r2 % PACK + 1, KP * c : KP * (c2 + 1)])
+            flat = t[:].rearrange("p r k -> p (r k)")
+            for i in range(steps):
+                raw[n + i] = flat[:, 2 * KP * i : 2 * KP * (i + 1)]
 
         def load_x(c):
             x_rows[c] = work.tile([P, PACK, L], BF16, name="xr_%d" % c, tag="xr", bufs=NC, align_bytes=ALIGN)
             nc.sync.dma_start(out=x_rows[c][:], in_=x[KP * c : KP * (c + 1), :].rearrange("(p j) l -> p j l", j=PACK))
 
-        s_first = keep.tile([P, 1, 8], F32, name="s_first")
-        s_rest = keep.tile([P, NC - 1, 8], F32, name="s_rest")
+        s_first = keep.tile([P, 2, 8], F32, name="s_first")
+        s_rest = keep.tile([P, NC - 2, 8], F32, name="s_rest")
         s_by = p_scale.rearrange("o (c p t) -> p (o c) t", p=P, t=PACK)
         a_bf = keep.tile([P, NG, 16], BF16, name="a_bf")
         g_bf = keep.tile([P, P], BF16, name="g_bf")
-        nc.gpsimd.memset(g_bf[:], 0.0)
+        nc.vector.memset(g_bf[:], 0.0)
 
         def scales(c):
-            return s_first[:, 0:1, 0:PACK] if c == 0 else s_rest[:, c - 1 : c, 0:PACK]
+            return s_first[:, c : c + 1, 0:PACK] if c < 2 else s_rest[:, c - 2 : c - 1, 0:PACK]
 
         pb_first = [keep.tile([P, KP], U8, name="pb_first%d" % j, align_bytes=ALIGN) for j in range(2)]
         for j in range(2):
             nc.sync.dma_start(out=pb_first[j][:], in_=p_by[0][:, j, 0:KP])
         nc.scalar.dma_start(out=a_bf[:, :, 0:PACK], in_=a.rearrange("(g m t) -> m g t", g=NG, t=PACK))
-        nc.scalar.dma_start(out=s_first[:, :, 0:PACK], in_=s_by[:, 0:1, :])
-        load_p(0, 1, 2)
+        nc.scalar.dma_start(out=s_first[:, :, 0:PACK], in_=s_by[:, 0:2, :])
+        load_p(1, 1)
         load_x(0)
-        load_p(0, 2, 3)
-        load_p(1, 0, 2)
-        nc.sync.dma_start(out=s_rest[:, :, 0:PACK], in_=s_by[:, 1:NC, :])
-        load_p(1, 2, 3)
+        load_p(2, 1)
+        load_p(3, 2)
         load_x(1)
-        for c in range(2, NC):
-            load_p(c, 0, 2)
-            load_p(c, 2, 3)
-            load_x(c)
-        pb_last = keep.tile([P, NC, 2, KP], U8, name="pb_last", align_bytes=ALIGN)
+        nc.sync.dma_start(out=s_rest[:, :, 0:PACK], in_=s_by[:, 2:NC, :])
+        for n in range(FIRST, SWEEP, FIRST):
+            load_p(n, 2)
+            load_p(n + 2, 1)
+            load_x(units_of(n)[0][1])
+            load_p(n + 3, 2)
+            load_x(units_of(n + 3)[0][1])
+        pb_pair = keep.tile([P, NC, 2, KP], U8, name="pb_pair", align_bytes=ALIGN)
         for t in range(2):
-            nc.sync.dma_start(out=pb_last[:, :, t, :], in_=p_by[1][:, 2 + t, :].rearrange("m (c k) -> m c k", k=KP))
-        for c in range(NC):
-            raw[(PAIRS, c)] = pb_last[:, c, :, :].rearrange("p r k -> p (r k)")
+            nc.sync.dma_start(out=pb_pair[:, :, t, :], in_=p_by[1][:, 1 + t, :].rearrange("m (c k) -> m c k", k=KP))
+        pb_last = keep.tile([P, D], U8, name="pb_last", align_bytes=ALIGN)
+        nc.sync.dma_start(out=pb_last[:], in_=p_by[1][:, 3, :])
+        for n in range(SWEEP, STEPS):
+            r, c = units_of(n)[0]
+            if r == 7:
+                raw[n] = pb_last[:, KP * c : KP * (c + 2)]
+            else:
+                raw[n] = pb_pair[:, c, :, :].rearrange("p r k -> p (r k)")
         nc.sync.dma_start(out=g_bf[0:NT, :], in_=g.rearrange("(i p) -> i p", p=P))
         vs = keep.tile([P, NG, D], U8, name="vs", align_bytes=ALIGN)
         nc.vector.memset(vs[:].rearrange("p g n -> p (g n)").bitcast(I32), 0)
@@ -141,7 +151,7 @@ def tile_stap_clutter_removal_s13_kernel(tc, x, g, p_bytes, p_scale, a, v_words,
         hq = keep.tile([P, NG, L], U32, name="hq", align_bytes=ALIGN)
         hs = keep.tile([P, NG, L], U8, name="hs", align_bytes=ALIGN)
         h_planes = [keep.tile([P, PACK, L], BF16, name="hp%d" % gg, align_bytes=ALIGN) for gg in range(NG)]
-        h_packed = [keep.tile([P, L, PACK], BF16, name="hg%d" % gg, align_bytes=ALIGN) for gg in range(NG)]
+        h_packed = [None, keep.tile([P, L, PACK], BF16, name="hg1", align_bytes=ALIGN)]
         a_f = keep.tile([P, NG, PACK], F32, name="a_f")
         g_f = keep.tile([P, NT], F32, name="g_f")
 
@@ -157,84 +167,67 @@ def tile_stap_clutter_removal_s13_kernel(tc, x, g, p_bytes, p_scale, a, v_words,
         def widen_to(n):
             for m in range(len(wide), min(n, LAST) + 1):
                 new_wide(m)
-                nc.scalar.copy(out=wide[m][:], in_=raw[step_of(m)].bitcast(E4M3))
+                nc.scalar.copy(out=wide[m][:], in_=raw[m].bitcast(E4M3))
 
-        def new_turned(n, b):
-            if n in WORD_STEPS:
-                return bank(b, [P, 2, 2, P])
+        def new_turned(b):
             return bank(b, [P, PACK, 2, P], BF16)
 
-        def turn(dst, n, j):
-            if n in WORD_STEPS:
-                words = wide[n][:].bitcast(F32)
-                for u in range(2):
-                    nc.tensor.transpose(dst[:, u, j, :], words[:, 2 * P * j + u : 2 * P * (j + 1) : 2], ident[:])
-            else:
-                for t in range(PACK):
-                    nc.tensor.matmul(
-                        dst[:, t, j, :],
-                        lhsT=wide[n][:, KP * j + t : KP * (j + 1) : PACK],
-                        rhs=ident_bf[:],
-                        start=True,
-                        stop=True,
-                    )
-
-        def transposes(n, b):
-            turned[n] = new_turned(n, b)
-            for j in range(2):
-                turn(turned[n], n, j)
+        def turn_unit(dst, n, j):
+            for t in range(PACK):
+                src = wide[n][:, KP * j + t : KP * (j + 1) : PACK]
+                if (n, j) in TURN_UNITS:
+                    nc.tensor.transpose(dst[:, t, j, :], src, ident_bf[:])
+                else:
+                    nc.tensor.matmul(dst[:, t, j, :], lhsT=src, rhs=ident_bf[:], start=True, stop=True)
 
         def turn_bank(n):
-            return TURN_BANK + n % 2
+            return FIRST + n % TURN_BANKS
 
-        def scaled_of(n):
-            head, col = place_of(n)
-            if head not in scaled:
-                scaled[head] = work.tile([P, 6 * P, PACK], BF16, name="pg", tag="pg", bufs=3, align_bytes=ALIGN)
-            return scaled[head][:, col : col + 2 * P, :]
+        def turn(n, b=None):
+            turned[n] = new_turned(turn_bank(n) if b is None else b)
+            for j in range(2):
+                turn_unit(turned[n], n, j)
 
-        def halves(words):
-            return words[:].rearrange("p u j m -> p (u j m)").bitcast(BF16).rearrange("p (u m e) -> p m u e", u=2, e=2)
+        def new_scaled(n, steps):
+            t = work.tile([P, 4 * P, PACK], BF16, name="pg", tag="pg", bufs=4, align_bytes=ALIGN)
+            for i in range(steps):
+                scaled[n + i] = t[:, 2 * P * i : 2 * P * (i + 1), :]
+            return t
 
-        def product(n, src, lo=0, hi=2):
-            c = step_of(n)[1]
-            dst = scaled_of(n)[:, P * lo : P * hi, :]
-            if n in WORD_STEPS:
-                nc.vector.tensor_tensor(
-                    out=dst.rearrange("p m (u e) -> p m u e", u=2),
-                    in0=halves(src)[:, P * lo : P * hi, :, :],
-                    in1=scales(c).to_broadcast([P, P * (hi - lo), PACK]),
-                    op=MULT,
-                )
+        def product_units(n, src, lo, hi):
+            nc.vector.tensor_tensor(
+                out=scaled[n][:, P * lo : P * hi, :].rearrange("p (m i) t -> p m t i", i=2),
+                in0=src[:, :, lo:hi, :].rearrange("p t j (m i) -> p (j m) t i", i=2),
+                in1=scales(units_of(n)[lo][1]).unsqueeze(3).to_broadcast([P, P * (hi - lo) // 2, PACK, 2]),
+                op=MULT,
+            )
+
+        def product(n):
+            (r0, c0), (r1, c1) = units_of(n)
+            if c0 == c1:
+                product_units(n, turned[n], 0, 2)
             else:
-                nc.vector.tensor_tensor(
-                    out=dst.rearrange("p (m i) t -> p m t i", i=2),
-                    in0=src[:, :, lo:hi, :].rearrange("p t j (m i) -> p (j m) t i", i=2),
-                    in1=scales(c).unsqueeze(3).to_broadcast([P, P * (hi - lo) // 2, PACK, 2]),
-                    op=MULT,
-                )
+                product_units(n, turned[n], 0, 1)
+                product_units(n, turned[n], 1, 2)
 
         def product_planes(n):
-            c = step_of(n)[1]
-            planes = work.tile([P, PACK, 2 * P], BF16, name="planes", tag="planes", bufs=1, align_bytes=ALIGN)
+            c = units_of(n)[0][1]
+            planes = work.tile([P, PACK, 2 * P], BF16, name="planes", tag="planes", bufs=2, align_bytes=ALIGN)
             for t in range(PACK):
-                if n in WORD_STEPS:
-                    src = halves(turned[n])[:, :, t // 2, t % 2]
-                else:
-                    src = turned[n][:, t, :, :].rearrange("p j m -> p (j m)")
+                src = turned[n][:, t, :, :].rearrange("p j m -> p (j m)")
                 nc.scalar.activation(out=planes[:, t, :], in_=src, func=COPY, scale=scales(c)[:, 0, t : t + 1])
             return planes
 
-        def quant_p(head, lo, hi, src=None):
-            if head not in pq:
-                pq[head] = work.tile([P, 6 * P], U32, name="pq", tag="pq", bufs=3, align_bytes=ALIGN)
-                ps[head] = work.tile([P, 6 * P], U8, name="ps", tag="ps", bufs=3, align_bytes=ALIGN)
-            src = scaled[head][:, P * lo : P * hi, :] if src is None else src
+        def quant_p(n, src, units, first=0):
+            q = work.tile([P, 4 * P], U32, name="pq", tag="pq", bufs=5, align_bytes=ALIGN)
+            sc = work.tile([P, 4 * P], U8, name="ps", tag="ps", bufs=5, align_bytes=ALIGN)
             nc.vector.quantize_mx(
-                out=pq[head][:, P * lo : P * hi].bitcast(E4M3X4),
-                scales=ps[head][:, P * lo : P * hi],
-                in_=src.rearrange("p m t -> p (m t)"),
+                out=q[:, 0 : P * units].bitcast(E4M3X4),
+                scales=sc[:, 0 : P * units],
+                in_=src[:, 0 : P * units, :].rearrange("p m t -> p (m t)"),
             )
+            for i in range(units):
+                pq[(n + (first + i) // 2, (first + i) % 2)] = (q[:, P * i : P * (i + 1)], sc[:, P * i : P * (i + 1)])
 
         def interleave(engine_copy, dst, src, lo, hi):
             engine_copy(
@@ -260,21 +253,22 @@ def tile_stap_clutter_removal_s13_kernel(tc, x, g, p_bytes, p_scale, a, v_words,
                 out=xq[:, c, :].bitcast(E4M3X4), scales=xs[:, c, :], in_=x_packed[c][:].rearrange("p l t -> p (l t)")
             )
 
+        done = {}
+
         def mm(n, lo=0, hi=2):
-            pair, c = step_of(n)
-            head, col = place_of(n)
             for j in range(lo, hi):
-                r = 2 * pair + j
+                r, c = units_of(n)[j]
+                done[r] = done.get(r, 0) + 1
                 if c == 0:
-                    sums[r] = bank(r % (2 * PAIRS), [P, L])
+                    sums[r] = bank(r % FIRST, [P, L])
                 nc.tensor.matmul_mx(
                     out=sums[r][:],
-                    lhsT=pq[head][:, col + P * j : col + P * (j + 1)].bitcast(E4M3X4),
-                    lhsT_scale=ps[head][:, col + P * j : col + P * (j + 1)],
+                    lhsT=pq[(n, j)][0].bitcast(E4M3X4),
+                    lhsT_scale=pq[(n, j)][1],
                     rhs=xq[:, c, :].bitcast(E4M3X4),
                     rhs_scale=xs[:, c, :],
                     start=(c == 0),
-                    stop=(c == NC - 1),
+                    stop=(done[r] == NC),
                 )
 
         def quant_h(gg, lo, hi, src):
@@ -284,9 +278,11 @@ def tile_stap_clutter_removal_s13_kernel(tc, x, g, p_bytes, p_scale, a, v_words,
                 in_=src[:, lo:hi, :].rearrange("p l t -> p (l t)"),
             )
 
-        def h_scalar(r):
+        def h_scalar(r, lo, hi):
             gg, t = r // PACK, r % PACK
-            nc.scalar.activation(out=h_planes[gg][:, t, :], in_=sums[r][:], func=COPY, scale=a_f[:, gg, t : t + 1])
+            nc.scalar.activation(
+                out=h_planes[gg][:, t, lo:hi], in_=sums[r][:, lo:hi], func=COPY, scale=a_f[:, gg, t : t + 1]
+            )
 
         def h_vector(r, lo, hi):
             gg, t = r // PACK, r % PACK
@@ -298,14 +294,6 @@ def tile_stap_clutter_removal_s13_kernel(tc, x, g, p_bytes, p_scale, a, v_words,
                 op0=MULT,
             )
 
-        def turn_and_multiply(n, b):
-            transposes(n, b)
-            if n >= LAG:
-                mm(n - LAG)
-
-        def tb(n):
-            return turn_bank(n + 1)
-
         def pack_x(c, split):
             x_packed[c] = new_packed()
             interleave_gpsimd(x_packed[c], x_rows[c], 0, split)
@@ -316,108 +304,147 @@ def tile_stap_clutter_removal_s13_kernel(tc, x, g, p_bytes, p_scale, a, v_words,
 
         nc.scalar.activation(out=a_f[:], in_=a_bf[:, :, 0:PACK], func=COPY)
         new_wide(0)
-        first_banks = [new_turned(0, turn_bank(0)), new_turned(0, 1)]
+        first_banks = [new_turned(FIRST), new_turned(FIRST - 1)]
         for j in range(2):
-            nc.scalar.copy(out=wide[0][:, KP * j : KP * (j + 1)], in_=pb_first[j][:].bitcast(E4M3))
-            turn(first_banks[j], 0, j)
-        widen_to(1)
-        transposes(1, turn_bank(1))
-        widen_to(2)
-        transposes(2, 5)
-        pack_x(0, X0_SPLIT)
-        for j in range(2):
-            product(0, first_banks[j], j, j + 1)
-        widen_to(3)
-        transposes(3, tb(3))
-        product(1, turned[1])
+            first_copy = nc.scalar.copy if j else nc.vector.tensor_copy
+            first_copy(out=wide[0][:, KP * j : KP * (j + 1)], in_=pb_first[j][:].bitcast(E4M3))
+            turn_unit(first_banks[j], 0, j)
+        for n in range(1, TURN_BANKS):
+            widen_to(n)
+            turn(n)
         widen_to(4)
-        transposes(4, tb(4))
-        pack_x_rest(0, X0_SPLIT)
-        widen_to(5)
-        product(2, turned[2])
-        if 1 not in VECTOR_ROUNDS:
-            planes = product_planes(3)
-        quant_p(0, 0, 4)
-        quant_x(0)
-        quant_p(0, 4, 6)
 
-        for c in range(1, NC):
-            n = PAIRS * c
-            on_scalar = c not in VECTOR_ROUNDS
-            split = X_SPLIT if on_scalar else L
+        ab = new_scaled(0, 2)
+        planes = None
+        for k in range(PERIODS):
+            n = FIRST * k
+            c = 2 * k
+            on_scalar = k in SCALAR_PERIODS
+            split = X0_SPLIT if k == 0 else (X_SPLIT if on_scalar else L)
+            mixed = new_scaled(n + 2, 1)
             pack_x(c, split)
-            if on_scalar:
-                widen_to(len(wide))
-                interleave(nc.scalar.copy, scaled_of(n), planes, 0, 2 * P)
-            else:
-                widen_to(n + 2)
-                product(n, turned[n])
-            turn_and_multiply(n + 2, tb(n + 2))
-            widen_to(n + 3 if on_scalar else n + AHEAD)
-            product(n + 1, turned[n + 1])
-            turn_and_multiply(n + 3, tb(n + 3))
+            if k == 0:
+                for j in range(2):
+                    product_units(0, first_banks[j], j, j + 1)
+            elif not on_scalar:
+                product(n)
             pack_x_rest(c, split)
-            widen_to(n + 4)
-            if c + 1 not in VECTOR_ROUNDS:
-                widen_to(n + 5)
-                planes = product_planes(n + 3)
-            product(n + 2, turned[n + 2])
-            turn_and_multiply(n + 4, tb(n + 4))
-            quant_p(n, 0, 4)
+            turn(n + 3)
+            if k > 0:
+                mm(n - 2)
+            product(n + 1)
+            turn(n + 4)
+            if k > 0:
+                mm(n - 1)
+            widen_to(n + 5)
+            product(n + 2)
+            turn(n + 5)
+            if k > 0:
+                mm(n - 3, 1, 2)
+            widen_to(n + AHEAD[k])
+            quant_p(n, ab, 4)
             quant_x(c)
-            quant_p(n, 4, 6)
+            quant_p(n + 2, mixed, 2)
+            mm(n)
+            split = X1_SPLIT if k == 0 else X_SPLIT
+            ab = new_scaled(n + 3, 2)
+            pack_x(c + 1, split)
+            pack_x_rest(c + 1, split)
+            product(n + 3)
+            turn(n + 6)
+            mm(n + 1)
+            product(n + 4)
+            turn(n + 7)
+            mm(n + 2, 0, 1)
+            quant_x(c + 1)
+            quant_p(n + 3, ab, 4)
+            if k + 1 < PERIODS:
+                ab = new_scaled(n + 5, 2)
+            if k + 1 in SCALAR_PERIODS or k + 1 == PERIODS:
+                planes = product_planes(n + 5)
+                widen_to(len(wide))
+                if k + 1 < PERIODS:
+                    interleave(nc.scalar.copy, scaled[n + 5], planes, 0, 2 * P)
+            widen_to(n + AFTER[k])
         for j in range(NC):
             load_x_tiles(j)
 
         n = SWEEP
         own = new_packed()
         interleave_gpsimd(own, planes, 0, 2 * P)
-        turn_and_multiply(n + 2, tb(n + 2))
-        widen_to(n + 5)
-        h_scalar(0)
-        h_scalar(1)
-        product(n + 1, turned[n + 1])
-        turn_and_multiply(n + 3, tb(n + 3))
-        h_scalar(2)
-        h_scalar(3)
-        product(n + 2, turned[n + 2])
-        turn_and_multiply(n + 4, tb(n + 4))
-        quant_p(n, 2, 4)
-        quant_p(n, 0, 2, own[:, 0 : 2 * P, :])
-        h_own = new_packed()
-        interleave_gpsimd(h_own, h_planes[0], 0, HALF)
-        widen_to(LAST)
-        product(n + 3, turned[n + 3])
-        turn_and_multiply(n + 5, tb(n + 5))
-        product(n + 4, turned[n + 4])
-        transposes(n + 6, tb(n + 6))
+        both = new_scaled(n + 1, 2)
+        turn(n + 3)
+        mm(n - 2)
+        planes = product_planes(n + 3)
+        h_scalar(0, 0, L)
+        h_scalar(1, 0, L)
+        product(n + 1)
+        turn(n + 4)
+        mm(n - 1)
+        mm(n - 3, 1, 2)
+        product(n + 2)
+        turn(n + 5)
+        turn(n + 6)
+        quant_p(n, own, 2)
+        quant_p(n + 1, both, 4)
+        mm(n)
         mm(n + 1)
-        transposes(LAST, 2)
-        interleave(nc.scalar.copy, h_packed[0], h_planes[0], HALF, L)
-        h_scalar(4)
-        h_scalar(5)
-        product(n + 5, turned[n + 5])
-        quant_p(n + 2, 0, 4)
+        own = new_packed()
+        interleave_gpsimd(own, planes, 0, 2 * P)
+        both = new_scaled(n + 4, 2)
+        widen_to(n + 7)
+        h_scalar(2, 0, L)
+        product(n + 4)
+        turn(n + 7)
         mm(n + 2)
+        widen_to(n + 8)
+        h_scalar(3, 0, L)
+        product(n + 5)
+        turn(n + 8)
+        widen_to(n + 9)
+        turn(n + 9, 3)
+        widen_to(LAST)
+        planes = product_planes(n + 9)
+        quant_p(n + 3, own, 2)
+        quant_p(n + 4, both, 4)
         mm(n + 3)
-        quant_p(n + 4, 0, 4)
         mm(n + 4)
+        h_own = new_packed()
+        interleave_gpsimd(h_own, h_planes[0], 0, L)
+        both = new_scaled(n + 6, 2)
+        mixed = new_scaled(n + 8, 2)
+        h_scalar(4, 0, HALF)
+        interleave(nc.scalar.copy, scaled[n + 9], planes, 0, 2 * P)
+        h_scalar(4, HALF, L)
+        product(n + 6)
+        turn(n + 10, turn_bank(n + 9))
         mm(n + 5)
-        product(n + 6, turned[n + 6])
+        product(n + 7)
+        turn(LAST, turn_bank(n + 10))
+        product(n + 8)
         g_turned = bank(3, [P, NT])
         nc.tensor.matmul(g_turned[:], lhsT=g_bf[:], rhs=ident_bf[:, 0:NT], start=True, stop=True)
         nc.scalar.copy(out=g_f[:], in_=g_turned[:])
-        product(LAST, turned[LAST], 0, 1)
-        quant_p(n + 6, 0, 2)
-        mm(n + 6)
-        product(LAST, turned[LAST], 1, 2)
+        quant_p(n + 6, both, 4)
+        quant_p(n + 8, mixed, 2)
+        for i in range(6, 9):
+            mm(n + i)
+        new_scaled(n + 10, 2)
+        product(n + 10)
+        quant_p(n + 9, scaled[n + 9], 2)
+        mm(n + 9)
+        product_units(LAST, turned[LAST], 0, 1)
+        quant_p(n + 10, scaled[n + 10], 2)
+        mm(n + 10)
+        product_units(LAST, turned[LAST], 1, 2)
         for j in range(2):
-            quant_p(n + 6, 2 + j, 3 + j)
+            quant_p(LAST, scaled[LAST][:, P * j : P * (j + 1), :], 1, j)
             mm(LAST, j, j + 1)
 
-        quant_h(0, 0, HALF, h_own)
-        quant_h(0, HALF, L, h_packed[0])
-        h_scalar(6)
+        quant_h(0, 0, L, h_own)
+        for lo in (0, HALF):
+            h_scalar(5, lo, lo + HALF)
+            h_scalar(6, lo, lo + HALF)
         h_vector(7, 0, HALF)
         h_vector(7, HALF, L)
         interleave(nc.vector.tensor_copy, h_packed[1], h_planes[1], 0, HALF)

@@ -35,8 +35,7 @@ SWEEP = FIRST * PERIODS
 STEPS = SWEEP + 3 * PERIODS
 LAST = STEPS - 1
 TURN_BANKS = 3
-TURN_STEPS = (7, 8, 11, 12, 13, 16, 17)
-TURN_UNITS = [(n, j) for n in TURN_STEPS for j in range(2)][1:]
+WORD_STEPS = (6, 9, 11, 14, 16, 19, 21)
 SCALAR_PERIODS = (1, 2, 3)
 WIDE_BUFS = 9
 X_SPLIT = 352
@@ -169,22 +168,26 @@ def tile_stap_clutter_removal_s13_kernel(tc, x, g, p_bytes, p_scale, a, v_words,
                 new_wide(m)
                 nc.scalar.copy(out=wide[m][:], in_=raw[m].bitcast(E4M3))
 
-        def new_turned(b):
+        def new_turned(n, b):
+            if n in WORD_STEPS:
+                return bank(b, [P, 2, 2, P])
             return bank(b, [P, PACK, 2, P], BF16)
 
         def turn_unit(dst, n, j):
-            for t in range(PACK):
-                src = wide[n][:, KP * j + t : KP * (j + 1) : PACK]
-                if (n, j) in TURN_UNITS:
-                    nc.tensor.transpose(dst[:, t, j, :], src, ident_bf[:])
-                else:
+            if n in WORD_STEPS:
+                words = wide[n][:].bitcast(F32)
+                for u in range(2):
+                    nc.tensor.transpose(dst[:, u, j, :], words[:, 2 * P * j + u : 2 * P * (j + 1) : 2], ident[:])
+            else:
+                for t in range(PACK):
+                    src = wide[n][:, KP * j + t : KP * (j + 1) : PACK]
                     nc.tensor.matmul(dst[:, t, j, :], lhsT=src, rhs=ident_bf[:], start=True, stop=True)
 
         def turn_bank(n):
             return FIRST + n % TURN_BANKS
 
         def turn(n, b=None):
-            turned[n] = new_turned(turn_bank(n) if b is None else b)
+            turned[n] = new_turned(n, turn_bank(n) if b is None else b)
             for j in range(2):
                 turn_unit(turned[n], n, j)
 
@@ -204,7 +207,15 @@ def tile_stap_clutter_removal_s13_kernel(tc, x, g, p_bytes, p_scale, a, v_words,
 
         def product(n):
             (r0, c0), (r1, c1) = units_of(n)
-            if c0 == c1:
+            if n in WORD_STEPS:
+                words = turned[n][:].rearrange("p u j m -> p (u j m)").bitcast(BF16)
+                nc.vector.tensor_tensor(
+                    out=scaled[n].rearrange("p m (u e) -> p m u e", u=2),
+                    in0=words.rearrange("p (u m e) -> p m u e", u=2, e=2),
+                    in1=scales(c0).to_broadcast([P, 2 * P, PACK]),
+                    op=MULT,
+                )
+            elif c0 == c1:
                 product_units(n, turned[n], 0, 2)
             else:
                 product_units(n, turned[n], 0, 1)
@@ -304,11 +315,13 @@ def tile_stap_clutter_removal_s13_kernel(tc, x, g, p_bytes, p_scale, a, v_words,
 
         nc.scalar.activation(out=a_f[:], in_=a_bf[:, :, 0:PACK], func=COPY)
         new_wide(0)
-        first_banks = [new_turned(FIRST), new_turned(FIRST - 1)]
+        first_banks = [new_turned(0, FIRST), new_turned(0, FIRST - 1)]
         for j in range(2):
             first_copy = nc.scalar.copy if j else nc.vector.tensor_copy
             first_copy(out=wide[0][:, KP * j : KP * (j + 1)], in_=pb_first[j][:].bitcast(E4M3))
             turn_unit(first_banks[j], 0, j)
+        ident = keep.tile([P, P], F32, name="ident")
+        nc.vector.tensor_copy(out=ident[:], in_=ident_bf[:])
         for n in range(1, TURN_BANKS):
             widen_to(n)
             turn(n)

@@ -199,9 +199,9 @@ def tile_stap_clutter_removal_s13_kernel(tc, x, g, p_bytes, p_scale, a, v_words,
 
         def product_units(n, src, lo, hi):
             nc.vector.tensor_tensor(
-                out=scaled[n][:, P * lo : P * hi, :].rearrange("p (m i) t -> p m t i", i=2),
-                in0=src[:, :, lo:hi, :].rearrange("p t j (m i) -> p (j m) t i", i=2),
-                in1=scales(units_of(n)[lo][1]).unsqueeze(3).to_broadcast([P, P * (hi - lo) // 2, PACK, 2]),
+                out=scaled[n][:, P * lo : P * hi, :],
+                in0=src[:, :, lo:hi, :].rearrange("p t j m -> p (j m) t"),
+                in1=scales(units_of(n)[lo][1]).to_broadcast([P, P * (hi - lo), PACK]),
                 op=MULT,
             )
 

@@ -35,13 +35,13 @@ SWEEP = FIRST * PERIODS
 STEPS = SWEEP + 3 * PERIODS
 LAST = STEPS - 1
 TURN_BANKS = 3
-WORD_STEPS = (6, 9, 11, 14, 16, 19, 21)
+WORD_STEPS = (6, 9, 11, 13, 14, 16, 19, 21)
 SCALAR_PERIODS = (1, 2, 3)
 WIDE_BUFS = 9
 X_SPLIT = 352
-X0_SPLIT = 448
+X0_SPLIT = 416
 X1_SPLIT = 352
-AHEAD = (8, 8, 8, 8)
+AHEAD = (7, 8, 8, 8)
 AFTER = (9, 9, 9, 11)
 H_SPLIT = 352
 
@@ -111,17 +111,20 @@ def tile_stap_clutter_removal_s13_kernel(tc, x, g, p_bytes, p_scale, a, v_words,
         nc.scalar.dma_start(out=a_bf[:, :, 0:PACK], in_=a.rearrange("(g m t) -> m g t", g=NG, t=PACK))
         nc.scalar.dma_start(out=s_first[:, :, 0:PACK], in_=s_by[:, 0:2, :])
         load_p(1, 1)
-        load_x(0)
         load_p(2, 1)
+        load_x(0)
         load_p(3, 2)
-        load_x(1)
+        load_p(FIRST, 2)
         nc.sync.dma_start(out=s_rest[:, :, 0:PACK], in_=s_by[:, 2:NC, :])
+        load_x(1)
         for n in range(FIRST, SWEEP, FIRST):
-            load_p(n, 2)
+            c = units_of(n)[0][1]
             load_p(n + 2, 1)
-            load_x(units_of(n)[0][1])
             load_p(n + 3, 2)
-            load_x(units_of(n + 3)[0][1])
+            load_x(c)
+            if n + FIRST < SWEEP:
+                load_p(n + FIRST, 2)
+            load_x(c + 1)
         pb_pair = keep.tile([P, NC, 2, KP], U8, name="pb_pair", align_bytes=ALIGN)
         for t in range(2):
             nc.sync.dma_start(out=pb_pair[:, :, t, :], in_=p_by[1][:, 1 + t, :].rearrange("m (c k) -> m c k", k=KP))
@@ -133,18 +136,7 @@ def tile_stap_clutter_removal_s13_kernel(tc, x, g, p_bytes, p_scale, a, v_words,
                 raw[n] = pb_last[:, KP * c : KP * (c + 2)]
             else:
                 raw[n] = pb_pair[:, c, :, :].rearrange("p r k -> p (r k)")
-        nc.sync.dma_start(out=g_bf[0:NT, :], in_=g.rearrange("(i p) -> i p", p=P))
         vs = keep.tile([P, NG, D], U8, name="vs", align_bytes=ALIGN)
-        nc.vector.memset(vs[:].rearrange("p g n -> p (g n)").bitcast(I32), 0)
-        for q in range(4):
-            nc.sync.dma_start(
-                out=vs[32 * q : 32 * q + 4, :, :].bitcast(I32),
-                in_=v_scales[:, 4 * q : 4 * q + 4, :].rearrange("g q n -> q g n").bitcast(I32),
-            )
-        vw = keep.tile([P, NG, 2 * D], U8, name="vw", align_bytes=ALIGN)
-        for gg in range(NG):
-            nc.sync.dma_start(out=vw[:, gg, :].bitcast(I32), in_=v_words[gg].bitcast(I32))
-
         xq = keep.tile([P, NC, L], U32, name="xq", align_bytes=ALIGN)
         xs = keep.tile([P, NC, L], U8, name="xs", align_bytes=ALIGN)
         hq = keep.tile([P, NG, L], U32, name="hq", align_bytes=ALIGN)
@@ -314,19 +306,31 @@ def tile_stap_clutter_removal_s13_kernel(tc, x, g, p_bytes, p_scale, a, v_words,
                 interleave(nc.scalar.copy, x_packed[c], x_rows[c], split, L)
 
         nc.scalar.activation(out=a_f[:], in_=a_bf[:, :, 0:PACK], func=COPY)
+        ident = keep.tile([P, P], F32, name="ident")
+        nc.vector.tensor_copy(out=ident[:], in_=ident_bf[:])
+        nc.vector.memset(vs[:, 0, :].bitcast(I32), 0)
         new_wide(0)
         first_banks = [new_turned(0, FIRST), new_turned(0, FIRST - 1)]
         for j in range(2):
             first_copy = nc.scalar.copy if j else nc.vector.tensor_copy
             first_copy(out=wide[0][:, KP * j : KP * (j + 1)], in_=pb_first[j][:].bitcast(E4M3))
             turn_unit(first_banks[j], 0, j)
-        ident = keep.tile([P, P], F32, name="ident")
-        nc.vector.tensor_copy(out=ident[:], in_=ident_bf[:])
+        nc.vector.memset(vs[:, 1, :].bitcast(I32), 0)
         for n in range(1, TURN_BANKS):
             widen_to(n)
             turn(n)
         widen_to(4)
 
+        for q in range(4):
+            nc.sync.dma_start(
+                out=vs[32 * q : 32 * q + 4, :, :].bitcast(I32),
+                in_=v_scales[:, 4 * q : 4 * q + 4, :].rearrange("g q n -> q g n").bitcast(I32),
+            )
+        vw = keep.tile([P, NG, 2 * D], U8, name="vw", align_bytes=ALIGN)
+        for gg in range(NG):
+            nc.sync.dma_start(out=vw[:, gg, :].bitcast(I32), in_=v_words[gg].bitcast(I32))
+
+        nc.sync.dma_start(out=g_bf[0:NT, :], in_=g.rearrange("(i p) -> i p", p=P))
         ab = new_scaled(0, 2)
         planes = None
         for k in range(PERIODS):
@@ -367,6 +371,7 @@ def tile_stap_clutter_removal_s13_kernel(tc, x, g, p_bytes, p_scale, a, v_words,
             turn(n + 6)
             mm(n + 1)
             product(n + 4)
+            widen_to(n + 7)
             turn(n + 7)
             mm(n + 2, 0, 1)
             quant_x(c + 1)

@@ -37,6 +37,7 @@ LAST = STEPS - 1
 TURN_BANKS = 3
 WORD_STEPS = (6, 9, 11, 13, 14, 16, 19, 21)
 SCALAR_PERIODS = (1, 2, 3)
+WARM_UPS = 3
 WIDE_BUFS = 9
 X_SPLIT = 352
 X0_SPLIT = 416
@@ -309,6 +310,9 @@ def tile_stap_clutter_removal_s13_kernel(tc, x, g, p_bytes, p_scale, a, v_words,
         ident = keep.tile([P, P], F32, name="ident")
         nc.vector.tensor_copy(out=ident[:], in_=ident_bf[:])
         nc.vector.memset(vs[:, 0, :].bitcast(I32), 0)
+        warm = bank(0, [P, PACK, P])
+        for i in range(WARM_UPS):
+            nc.tensor.matmul(warm[:], lhsT=g_bf[:], rhs=g_bf[:].unsqueeze(1).to_broadcast([P, PACK, P]), start=True, stop=True)
         new_wide(0)
         first_banks = [new_turned(0, FIRST), new_turned(0, FIRST - 1)]
         for j in range(2):

@@ -38,6 +38,8 @@ TURN_BANKS = 3
 WORD_STEPS = (6, 9, 11, 13, 14, 16, 19, 21)
 SCALAR_PERIODS = (1, 2, 3)
 WARM_UPS = 3
+SCALE_LOADS = ((0, 2), (2, 8))
+H0_SPLIT = 320
 WIDE_BUFS = 9
 X_SPLIT = 352
 X0_SPLIT = 416
@@ -96,27 +98,32 @@ def tile_stap_clutter_removal_s13_kernel(tc, x, g, p_bytes, p_scale, a, v_words,
             x_rows[c] = work.tile([P, PACK, L], BF16, name="xr_%d" % c, tag="xr", bufs=NC, align_bytes=ALIGN)
             nc.sync.dma_start(out=x_rows[c][:], in_=x[KP * c : KP * (c + 1), :].rearrange("(p j) l -> p j l", j=PACK))
 
-        s_first = keep.tile([P, 2, 8], F32, name="s_first")
-        s_rest = keep.tile([P, NC - 2, 8], F32, name="s_rest")
+        s_part = [keep.tile([P, hi - lo, 8], F32, name="s_%d" % lo) for lo, hi in SCALE_LOADS]
         s_by = p_scale.rearrange("o (c p t) -> p (o c) t", p=P, t=PACK)
         a_bf = keep.tile([P, NG, 16], BF16, name="a_bf")
         g_bf = keep.tile([P, P], BF16, name="g_bf")
         nc.vector.memset(g_bf[:], 0.0)
 
-        def scales(c):
-            return s_first[:, c : c + 1, 0:PACK] if c < 2 else s_rest[:, c - 2 : c - 1, 0:PACK]
+        def load_scales(queue, i):
+            lo, hi = SCALE_LOADS[i]
+            queue.dma_start(out=s_part[i][:, :, 0:PACK], in_=s_by[:, lo:hi, :])
+
+        def scales(c, passes=1):
+            i = max(i for i in range(len(SCALE_LOADS)) if SCALE_LOADS[i][0] <= c)
+            c -= SCALE_LOADS[i][0]
+            return s_part[i][:, c : c + passes, 0:PACK]
 
         pb_first = [keep.tile([P, KP], U8, name="pb_first%d" % j, align_bytes=ALIGN) for j in range(2)]
         for j in range(2):
             nc.sync.dma_start(out=pb_first[j][:], in_=p_by[0][:, j, 0:KP])
         nc.scalar.dma_start(out=a_bf[:, :, 0:PACK], in_=a.rearrange("(g m t) -> m g t", g=NG, t=PACK))
-        nc.scalar.dma_start(out=s_first[:, :, 0:PACK], in_=s_by[:, 0:2, :])
+        load_scales(nc.scalar, 0)
         load_p(1, 1)
         load_p(2, 1)
         load_x(0)
         load_p(3, 2)
         load_p(FIRST, 2)
-        nc.sync.dma_start(out=s_rest[:, :, 0:PACK], in_=s_by[:, 2:NC, :])
+        load_scales(nc.sync, 1)
         load_x(1)
         for n in range(FIRST, SWEEP, FIRST):
             c = units_of(n)[0][1]
@@ -126,6 +133,8 @@ def tile_stap_clutter_removal_s13_kernel(tc, x, g, p_bytes, p_scale, a, v_words,
             if n + FIRST < SWEEP:
                 load_p(n + FIRST, 2)
             load_x(c + 1)
+            if n == FIRST and len(SCALE_LOADS) > 2:
+                load_scales(nc.sync, 2)
         pb_pair = keep.tile([P, NC, 2, KP], U8, name="pb_pair", align_bytes=ALIGN)
         for t in range(2):
             nc.sync.dma_start(out=pb_pair[:, :, t, :], in_=p_by[1][:, 1 + t, :].rearrange("m (c k) -> m c k", k=KP))
@@ -211,8 +220,12 @@ def tile_stap_clutter_removal_s13_kernel(tc, x, g, p_bytes, p_scale, a, v_words,
             elif c0 == c1:
                 product_units(n, turned[n], 0, 2)
             else:
-                product_units(n, turned[n], 0, 1)
-                product_units(n, turned[n], 1, 2)
+                nc.vector.tensor_tensor(
+                    out=scaled[n].rearrange("p (j m) t -> p j m t", j=2),
+                    in0=turned[n][:].rearrange("p t j m -> p j m t"),
+                    in1=scales(c0, 2).unsqueeze(2).to_broadcast([P, 2, P, PACK]),
+                    op=MULT,
+                )
 
         def product_planes(n):
             c = units_of(n)[0][1]
@@ -419,25 +432,27 @@ def tile_stap_clutter_removal_s13_kernel(tc, x, g, p_bytes, p_scale, a, v_words,
         product(n + 4)
         turn(n + 7)
         mm(n + 2)
-        widen_to(n + 8)
         h_scalar(3, 0, L)
         product(n + 5)
+        quant_p(n + 3, own, 2)
+        quant_p(n + 4, both, 4)
+        mm(n + 3)
+        widen_to(n + 8)
         turn(n + 8)
+        mm(n + 4)
         widen_to(n + 9)
         turn(n + 9, 3)
         widen_to(LAST)
         planes = product_planes(n + 9)
-        quant_p(n + 3, own, 2)
-        quant_p(n + 4, both, 4)
-        mm(n + 3)
-        mm(n + 4)
         h_own = new_packed()
-        interleave_gpsimd(h_own, h_planes[0], 0, L)
+        interleave_gpsimd(h_own, h_planes[0], 0, H0_SPLIT)
         both = new_scaled(n + 6, 2)
         mixed = new_scaled(n + 8, 2)
         h_scalar(4, 0, HALF)
         interleave(nc.scalar.copy, scaled[n + 9], planes, 0, 2 * P)
         h_scalar(4, HALF, L)
+        if H0_SPLIT < L:
+            interleave(nc.scalar.copy, h_own, h_planes[0], H0_SPLIT, L)
         product(n + 6)
         turn(n + 10, turn_bank(n + 9))
         mm(n + 5)
@@ -453,11 +468,11 @@ def tile_stap_clutter_removal_s13_kernel(tc, x, g, p_bytes, p_scale, a, v_words,
             mm(n + i)
         new_scaled(n + 10, 2)
         product(n + 10)
-        quant_p(n + 9, scaled[n + 9], 2)
-        mm(n + 9)
         product_units(LAST, turned[LAST], 0, 1)
         quant_p(n + 10, scaled[n + 10], 2)
+        quant_p(n + 9, scaled[n + 9], 2)
         mm(n + 10)
+        mm(n + 9)
         product_units(LAST, turned[LAST], 1, 2)
         for j in range(2):
             quant_p(LAST, scaled[LAST][:, P * j : P * (j + 1), :], 1, j)

@@ -257,8 +257,8 @@ def tile_stap_clutter_removal_s13_kernel(tc, x, g, p_bytes, p_scale, a, v_words,
 
         def interleave_gpsimd(dst, src, lo, hi):
             nc.gpsimd.tensor_scalar(
-                out=dst[:, lo:hi, :],
-                in0=src[:, :, lo:hi].rearrange("p t l -> p l t"),
+                out=dst[:, lo:hi, :].rearrange("p (c i) t -> p c t i", i=4),
+                in0=src[:, :, lo:hi].rearrange("p t (c i) -> p c t i", i=4),
                 scalar1=1.0,
                 scalar2=0.0,
                 op0=MULT,

@@ -10,6 +10,7 @@ F32 = mybir.dt.float32
 BF16 = mybir.dt.bfloat16
 I32 = mybir.dt.int32
 U32 = mybir.dt.uint32
+U16 = mybir.dt.uint16
 U8 = mybir.dt.uint8
 E4M3 = mybir.dt.float8_e4m3fn
 E4M3X4 = mybir.dt.float8_e4m3fn_x4
@@ -24,49 +25,46 @@ PACK = 4
 KP = P * PACK
 NC = D // KP
 NG = R // KP
-NT = D // P
 BANKS = 8
 HALF = L // 2
 ALIGN = 64
+STEP = 2 * P
 
 FIRST = 5
+TURN_BANKS = 3
 PERIODS = NC // 2
 SWEEP = FIRST * PERIODS
-STEPS = SWEEP + 3 * PERIODS
-LAST = STEPS - 1
-TURN_BANKS = 3
-WORD_STEPS = (6, 9, 11, 13, 14, 16, 19, 21)
-SCALAR_PERIODS = (1, 2, 3)
+STEPS = 32
 WARM_UPS = 3
-SCALE_LOADS = ((0, 2), (2, 8))
-H0_SPLIT = 320
-WIDE_BUFS = 9
-X_SPLIT = 352
-X0_SPLIT = 416
-X1_SPLIT = 352
-AHEAD = (7, 8, 8, 8)
-AFTER = (9, 9, 9, 11)
+X_SPLIT = (400, 400, 288)
+X0_SPLIT = (416, 368)
 H_SPLIT = 352
+PLAIN = 2
+LEAD = 1
+SHARED = (4, 9, 12, 20, 28)
+EARLY = 2
+PAIRED = (2, 3, 7)
+OUT_BANKS = (0, 1, 7, 5, 6, 4, 2, 3)
+SUM_BANK = (0, 1, 2, 3, 4, 4, 2, 3)
 
-OUT_BANKS = (4, 3, 6, 7, 5, 0, 1, 2)
-LEAD = 2
-SINGLES = 4
-SHARED = range(5, NT - 4, 4)
-EARLY = 3
-SECOND_QUEUE = range(6, NT, 4)
+
+def steps_in_order():
+    steps = []
+    for k in range(PERIODS):
+        c = 2 * k
+        steps.extend([((0, c), (1, c)), ((2, c), (3, c)), ((4, c), (4, c + 1)), ((0, c + 1), (1, c + 1)), ((2, c + 1), (3, c + 1))])
+    steps[-2], steps[-1] = steps[-1], steps[-2]
+    pair = [((5, c), (6, c)) for c in range(NC)]
+    last = [((7, c), (7, c + 1)) for c in range(0, NC, 2)]
+    steps.extend([pair[0], pair[1]])
+    steps.extend([pair[2], last[0], pair[3]])
+    steps.extend([pair[4], last[1], pair[5], last[2]])
+    steps.extend([pair[6], pair[7], last[3]])
+    return steps
 
 
-def units_of(n):
-    if n < SWEEP:
-        c, i = 2 * (n // FIRST), n % FIRST
-        if i == 2:
-            return (4, c), (4, c + 1)
-        r, c = 2 * (i % 3), c + i // 3
-        return (r, c), (r + 1, c)
-    c, i = 2 * ((n - SWEEP) // 3), (n - SWEEP) % 3
-    if i == 2:
-        return (7, c), (7, c + 1)
-    return (5, c + i), (6, c + i)
+UNITS = steps_in_order()
+WORD_STEPS = (6, 8, 9, 11, 13, 14, 16, 18)
 
 
 def tile_stap_clutter_removal_s13_kernel(tc, x, g, p_bytes, p_scale, a, v_words, v_scales, out):
@@ -82,93 +80,91 @@ def tile_stap_clutter_removal_s13_kernel(tc, x, g, p_bytes, p_scale, a, v_words,
 
         ident_bf = keep.tile([P, P], BF16, name="ident_bf")
         make_identity(nc, ident_bf[:])
+        g_rows = keep.tile([P, P], BF16, name="g_rows")
+        nc.vector.memset(g_rows[:], 0.0)
 
         p_by = p_bytes.rearrange("(g m t) k -> g m t k", g=NG, t=PACK)
-        raw, x_rows = {}, {}
+        pieces = []
 
-        def load_p(n, steps):
-            (r, c), (r2, c2) = units_of(n)[0], units_of(n + steps - 1)[1]
-            t = keep.tile([P, r2 - r + 1, KP * (c2 - c + 1)], U8, name="pb_%d" % n, align_bytes=ALIGN)
-            nc.sync.dma_start(out=t[:], in_=p_by[r // PACK][:, r % PACK : r2 % PACK + 1, KP * c : KP * (c2 + 1)])
-            flat = t[:].rearrange("p r k -> p (r k)")
-            for i in range(steps):
-                raw[n + i] = flat[:, 2 * KP * i : 2 * KP * (i + 1)]
+        def load_p(r, tiles, c, passes):
+            t = keep.tile([P, tiles, KP * passes], U8, name="pb_%d_%d" % (r, c), align_bytes=ALIGN)
+            nc.sync.dma_start(out=t[:], in_=p_by[r // PACK][:, r % PACK : r % PACK + tiles, KP * c : KP * (c + passes)])
+            pieces.append((t, [(r + i, c + j) for i in range(tiles) for j in range(passes)]))
+
+        x_rows = {}
+
+        def new_x(name):
+            return work.tile([P, 2, PACK, L], BF16, name=name, tag="xr", bufs=PERIODS, align_bytes=ALIGN)
 
         def load_x(c):
-            x_rows[c] = work.tile([P, PACK, L], BF16, name="xr_%d" % c, tag="xr", bufs=NC, align_bytes=ALIGN)
-            nc.sync.dma_start(out=x_rows[c][:], in_=x[KP * c : KP * (c + 1), :].rearrange("(p j) l -> p j l", j=PACK))
+            if c % 2 == 0:
+                x_rows[c // 2] = new_x("xr_%d" % c)
+            nc.sync.dma_start(
+                out=x_rows[c // 2][:, c % 2, :, :], in_=x[KP * c : KP * (c + 1), :].rearrange("(p j) l -> p j l", j=PACK)
+            )
 
-        s_part = [keep.tile([P, hi - lo, 8], F32, name="s_%d" % lo) for lo, hi in SCALE_LOADS]
         s_by = p_scale.rearrange("o (c p t) -> p (o c) t", p=P, t=PACK)
-        a_bf = keep.tile([P, NG, 16], BF16, name="a_bf")
-        g_bf = keep.tile([P, P], BF16, name="g_bf")
-        nc.vector.memset(g_bf[:], 0.0)
-
-        def load_scales(queue, i):
-            lo, hi = SCALE_LOADS[i]
-            queue.dma_start(out=s_part[i][:, :, 0:PACK], in_=s_by[:, lo:hi, :])
+        s_first = keep.tile([P, 2, 8], F32, name="s_first")
+        s_rest = keep.tile([P, NC - 2, 8], F32, name="s_rest")
 
         def scales(c, passes=1):
-            i = max(i for i in range(len(SCALE_LOADS)) if SCALE_LOADS[i][0] <= c)
-            c -= SCALE_LOADS[i][0]
-            return s_part[i][:, c : c + passes, 0:PACK]
+            if c < 2:
+                return s_first[:, c : c + passes, 0:PACK]
+            return s_rest[:, c - 2 : c - 2 + passes, 0:PACK]
 
-        pb_first = [keep.tile([P, KP], U8, name="pb_first%d" % j, align_bytes=ALIGN) for j in range(2)]
-        for j in range(2):
-            nc.sync.dma_start(out=pb_first[j][:], in_=p_by[0][:, j, 0:KP])
-        nc.scalar.dma_start(out=a_bf[:, :, 0:PACK], in_=a.rearrange("(g m t) -> m g t", g=NG, t=PACK))
-        load_scales(nc.scalar, 0)
-        load_p(1, 1)
-        load_p(2, 1)
+        load_p(0, 1, 0, 1)
+        load_p(1, 1, 0, 1)
+        nc.scalar.dma_start(out=s_first[:, :, 0:PACK], in_=s_by[:, 0:2, :])
+        vs_rows = keep.tile([P, 2 * KP], U8, name="vs_rows", align_bytes=ALIGN)
+        nc.sync.dma_start(out=vs_rows[:], in_=v_scales.rearrange("g q (h n) -> (g q h) n", h=4))
+        load_p(2, 2, 0, 1)
+        load_p(4, 1, 0, 2)
         load_x(0)
-        load_p(3, 2)
-        load_p(FIRST, 2)
-        load_scales(nc.sync, 1)
-        load_x(1)
-        for n in range(FIRST, SWEEP, FIRST):
-            c = units_of(n)[0][1]
-            load_p(n + 2, 1)
-            load_p(n + 3, 2)
-            load_x(c)
-            if n + FIRST < SWEEP:
-                load_p(n + FIRST, 2)
-            load_x(c + 1)
-            if n == FIRST and len(SCALE_LOADS) > 2:
-                load_scales(nc.sync, 2)
-        pb_pair = keep.tile([P, NC, 2, KP], U8, name="pb_pair", align_bytes=ALIGN)
-        for t in range(2):
-            nc.sync.dma_start(out=pb_pair[:, :, t, :], in_=p_by[1][:, 1 + t, :].rearrange("m (c k) -> m c k", k=KP))
-        pb_last = keep.tile([P, D], U8, name="pb_last", align_bytes=ALIGN)
-        nc.sync.dma_start(out=pb_last[:], in_=p_by[1][:, 3, :])
-        for n in range(SWEEP, STEPS):
-            r, c = units_of(n)[0]
-            if r == 7:
-                raw[n] = pb_last[:, KP * c : KP * (c + 2)]
-            else:
-                raw[n] = pb_pair[:, c, :, :].rearrange("p r k -> p (r k)")
+        load_p(0, 2, 1, 1)
+        load_p(2, 2, 1, 1)
+        for k in range(1, PERIODS):
+            load_p(0, 2, 2 * k, 2)
+            if k == 1:
+                load_x(1)
+            load_p(2, 2, 2 * k, 2)
+            if k == 1:
+                nc.sync.dma_start(out=s_rest[:, :, 0:PACK], in_=s_by[:, 2:NC, :])
+            load_p(4, 1, 2 * k, 2)
+            load_x(2 * k)
+            load_x(2 * k + 1)
+        for r, k in ((5, 0), (5, 1), (7, 0), (5, 2), (7, 1), (7, 2), (5, 3), (7, 3)):
+            load_p(r, 2 if r == 5 else 1, 2 * k, 2)
+        a_bf = keep.tile([P, NG, 16], BF16, name="a_bf")
+        nc.sync.dma_start(out=a_bf[:, :, 0:PACK], in_=a.rearrange("(g m t) -> m g t", g=NG, t=PACK))
+        g_bf = keep.tile([P, NC - PLAIN, 16], BF16, name="g_bf")
+        nc.sync.dma_start(
+            out=g_bf[:, :, 0:PACK], in_=g[KP * PLAIN : D].rearrange("(c m j) -> m c j", m=P, j=PACK)
+        )
+
         vs = keep.tile([P, NG, D], U8, name="vs", align_bytes=ALIGN)
+        vs_turned = keep.tile([P, 2 * KP], U8, name="vs_turned", align_bytes=ALIGN)
         xq = keep.tile([P, NC, L], U32, name="xq", align_bytes=ALIGN)
         xs = keep.tile([P, NC, L], U8, name="xs", align_bytes=ALIGN)
         hq = keep.tile([P, NG, L], U32, name="hq", align_bytes=ALIGN)
         hs = keep.tile([P, NG, L], U8, name="hs", align_bytes=ALIGN)
         h_planes = [keep.tile([P, PACK, L], BF16, name="hp%d" % gg, align_bytes=ALIGN) for gg in range(NG)]
-        h_packed = [None, keep.tile([P, L, PACK], BF16, name="hg1", align_bytes=ALIGN)]
+        h_packed = [keep.tile([P, L, PACK], BF16, name="hg%d" % gg, align_bytes=ALIGN) for gg in range(NG)]
         a_f = keep.tile([P, NG, PACK], F32, name="a_f")
-        g_f = keep.tile([P, NT], F32, name="g_f")
+        g_f = keep.tile([P, NC, PACK], F32, name="g_f")
 
-        wide, turned, scaled, pq, ps, x_packed, sums, x_tiles = {}, {}, {}, {}, {}, {}, {}, {}
+        wide, turned, scaled, planes, pq, sums, done = {}, {}, {}, {}, {}, {}, {}
+        widened = []
 
-        def load_x_tiles(j):
-            x_tiles[j] = work.tile([P, PACK, L], BF16, name="xn_%d" % j, tag="xr", bufs=NC, align_bytes=ALIGN)
-            nc.sync.dma_start(out=x_tiles[j][:], in_=x[KP * j : KP * (j + 1), :].rearrange("(i p) l -> p i l", p=P))
-
-        def new_wide(n):
-            wide[n] = work.tile([P, 2 * KP], BF16, name="w", tag="w", bufs=WIDE_BUFS, align_bytes=ALIGN)
-
-        def widen_to(n):
-            for m in range(len(wide), min(n, LAST) + 1):
-                new_wide(m)
-                nc.scalar.copy(out=wide[m][:], in_=raw[m].bitcast(E4M3))
+        def widen(copy=nc.scalar.copy):
+            t, units = pieces[len(widened)]
+            widened.append(units)
+            if len(units) > 2:
+                w = work.tile([P, 4 * KP], BF16, name="w", tag="w4", bufs=4, align_bytes=ALIGN)
+            else:
+                w = work.tile([P, 2 * KP], BF16, name="w", tag="w2", bufs=4, align_bytes=ALIGN)
+            copy(out=w[:, 0 : KP * len(units)], in_=t[:].rearrange("p r k -> p (r k)").bitcast(E4M3))
+            for i, u in enumerate(units):
+                wide[u] = w[:, KP * i : KP * (i + 1)]
 
         def new_turned(n, b):
             if n in WORD_STEPS:
@@ -176,39 +172,39 @@ def tile_stap_clutter_removal_s13_kernel(tc, x, g, p_bytes, p_scale, a, v_words,
             return bank(b, [P, PACK, 2, P], BF16)
 
         def turn_unit(dst, n, j):
+            src = wide[UNITS[n][j]]
             if n in WORD_STEPS:
-                words = wide[n][:].bitcast(F32)
+                words = src.bitcast(F32)
                 for u in range(2):
-                    nc.tensor.transpose(dst[:, u, j, :], words[:, 2 * P * j + u : 2 * P * (j + 1) : 2], ident[:])
+                    nc.tensor.transpose(dst[:, u, j, :], words[:, u : 2 * P : 2], ident[:])
             else:
                 for t in range(PACK):
-                    src = wide[n][:, KP * j + t : KP * (j + 1) : PACK]
-                    nc.tensor.matmul(dst[:, t, j, :], lhsT=src, rhs=ident_bf[:], start=True, stop=True)
-
-        def turn_bank(n):
-            return FIRST + n % TURN_BANKS
+                    nc.tensor.matmul(dst[:, t, j, :], lhsT=src[:, t:KP:PACK], rhs=ident_bf[:], start=True, stop=True)
 
         def turn(n, b=None):
-            turned[n] = new_turned(n, turn_bank(n) if b is None else b)
+            turned[n] = new_turned(n, FIRST + n % TURN_BANKS if b is None else b)
             for j in range(2):
                 turn_unit(turned[n], n, j)
 
-        def new_scaled(n, steps):
-            t = work.tile([P, 4 * P, PACK], BF16, name="pg", tag="pg", bufs=4, align_bytes=ALIGN)
-            for i in range(steps):
-                scaled[n + i] = t[:, 2 * P * i : 2 * P * (i + 1), :]
+        def new_scaled(steps, tag="pg", bufs=4):
+            t = work.tile([P, FIRST * STEP if tag == "pg" else 2 * L, PACK], BF16, name=tag, tag=tag, bufs=bufs, align_bytes=ALIGN)
+            for i, n in enumerate(steps):
+                scaled[n] = t[:, STEP * i : STEP * (i + 1), :]
             return t
+
+        def new_packed(steps=()):
+            return new_scaled(steps, "xg", 1)
 
         def product_units(n, src, lo, hi):
             nc.vector.tensor_tensor(
                 out=scaled[n][:, P * lo : P * hi, :],
                 in0=src[:, :, lo:hi, :].rearrange("p t j m -> p (j m) t"),
-                in1=scales(units_of(n)[lo][1]).to_broadcast([P, P * (hi - lo), PACK]),
+                in1=scales(UNITS[n][lo][1]).to_broadcast([P, P * (hi - lo), PACK]),
                 op=MULT,
             )
 
         def product(n):
-            (r0, c0), (r1, c1) = units_of(n)
+            c0, c1 = UNITS[n][0][1], UNITS[n][1][1]
             if n in WORD_STEPS:
                 words = turned[n][:].rearrange("p u j m -> p (u j m)").bitcast(BF16)
                 nc.vector.tensor_tensor(
@@ -228,23 +224,24 @@ def tile_stap_clutter_removal_s13_kernel(tc, x, g, p_bytes, p_scale, a, v_words,
                 )
 
         def product_planes(n):
-            c = units_of(n)[0][1]
-            planes = work.tile([P, PACK, 2 * P], BF16, name="planes", tag="planes", bufs=2, align_bytes=ALIGN)
+            c = UNITS[n][0][1]
+            planes[n] = work.tile([P, PACK, STEP], BF16, name="planes", tag="planes", bufs=2, align_bytes=ALIGN)
             for t in range(PACK):
                 src = turned[n][:, t, :, :].rearrange("p j m -> p (j m)")
-                nc.scalar.activation(out=planes[:, t, :], in_=src, func=COPY, scale=scales(c)[:, 0, t : t + 1])
-            return planes
+                nc.scalar.activation(out=planes[n][:, t, :], in_=src, func=COPY, scale=scales(c)[:, 0, t : t + 1])
 
-        def quant_p(n, src, units, first=0):
-            q = work.tile([P, 4 * P], U32, name="pq", tag="pq", bufs=5, align_bytes=ALIGN)
-            sc = work.tile([P, 4 * P], U8, name="ps", tag="ps", bufs=5, align_bytes=ALIGN)
+        def quant_p(src, units):
+            q = work.tile([P, 2 * STEP], U32, name="pq", tag="pq", bufs=6, align_bytes=ALIGN)
+            sc = work.tile([P, 2 * STEP], U8, name="ps", tag="ps", bufs=6, align_bytes=ALIGN)
+            w = P * len(units)
             nc.vector.quantize_mx(
-                out=q[:, 0 : P * units].bitcast(E4M3X4),
-                scales=sc[:, 0 : P * units],
-                in_=src[:, 0 : P * units, :].rearrange("p m t -> p (m t)"),
+                out=q[:, 0:w].bitcast(E4M3X4), scales=sc[:, 0:w], in_=src[:, 0:w, :].rearrange("p m t -> p (m t)")
             )
-            for i in range(units):
-                pq[(n + (first + i) // 2, (first + i) % 2)] = (q[:, P * i : P * (i + 1)], sc[:, P * i : P * (i + 1)])
+            for i, u in enumerate(units):
+                pq[u] = (q[:, P * i : P * (i + 1)], sc[:, P * i : P * (i + 1)])
+
+        def both(*steps):
+            return [(n, j) for n in steps for j in range(2)]
 
         def interleave(engine_copy, dst, src, lo, hi):
             engine_copy(
@@ -252,47 +249,40 @@ def tile_stap_clutter_removal_s13_kernel(tc, x, g, p_bytes, p_scale, a, v_words,
                 in_=src[:, :, lo:hi].rearrange("p t (c i) -> p c t i", i=4),
             )
 
-        def new_packed():
-            return work.tile([P, L, PACK], BF16, name="xg", tag="xg", bufs=1, align_bytes=ALIGN)
+        def gpsimd_copy(dst, src):
+            nc.gpsimd.tensor_scalar(out=dst, in0=src, scalar1=1.0, scalar2=0.0, op0=MULT, op1=ADD)
 
         def interleave_gpsimd(dst, src, lo, hi):
-            nc.gpsimd.tensor_scalar(
-                out=dst[:, lo:hi, :].rearrange("p (c i) t -> p c t i", i=4),
-                in0=src[:, :, lo:hi].rearrange("p t (c i) -> p c t i", i=4),
-                scalar1=1.0,
-                scalar2=0.0,
-                op0=MULT,
-                op1=ADD,
-            )
+            gpsimd_copy(dst[:, lo:hi, :], src[:, :, lo:hi].rearrange("p t l -> p l t"))
 
-        def quant_x(c):
+        def quant_x(c, packed):
             nc.vector.quantize_mx(
-                out=xq[:, c, :].bitcast(E4M3X4), scales=xs[:, c, :], in_=x_packed[c][:].rearrange("p l t -> p (l t)")
+                out=xq[:, c, :].bitcast(E4M3X4),
+                scales=xs[:, c, :],
+                in_=packed[:, L * (c % 2) : L * (c % 2 + 1), :].rearrange("p l t -> p (l t)"),
             )
-
-        done = {}
 
         def mm(n, lo=0, hi=2):
             for j in range(lo, hi):
-                r, c = units_of(n)[j]
+                r, c = UNITS[n][j]
                 done[r] = done.get(r, 0) + 1
-                if c == 0:
-                    sums[r] = bank(r % FIRST, [P, L])
+                if done[r] == 1:
+                    sums[r] = bank(SUM_BANK[r], [P, L])
                 nc.tensor.matmul_mx(
                     out=sums[r][:],
                     lhsT=pq[(n, j)][0].bitcast(E4M3X4),
                     lhsT_scale=pq[(n, j)][1],
                     rhs=xq[:, c, :].bitcast(E4M3X4),
                     rhs_scale=xs[:, c, :],
-                    start=(c == 0),
+                    start=(done[r] == 1),
                     stop=(done[r] == NC),
                 )
 
-        def quant_h(gg, lo, hi, src):
+        def quant_h(gg, lo, hi):
             nc.vector.quantize_mx(
                 out=hq[:, gg, lo:hi].bitcast(E4M3X4),
                 scales=hs[:, gg, lo:hi],
-                in_=src[:, lo:hi, :].rearrange("p l t -> p (l t)"),
+                in_=h_packed[gg][:, lo:hi, :].rearrange("p l t -> p (l t)"),
             )
 
         def h_scalar(r, lo, hi):
@@ -311,174 +301,236 @@ def tile_stap_clutter_removal_s13_kernel(tc, x, g, p_bytes, p_scale, a, v_words,
                 op0=MULT,
             )
 
-        def pack_x(c, split):
-            x_packed[c] = new_packed()
-            interleave_gpsimd(x_packed[c], x_rows[c], 0, split)
-
-        def pack_x_rest(c, split):
-            if split < L:
-                interleave(nc.scalar.copy, x_packed[c], x_rows[c], split, L)
-
-        nc.scalar.activation(out=a_f[:], in_=a_bf[:, :, 0:PACK], func=COPY)
         ident = keep.tile([P, P], F32, name="ident")
-        nc.vector.tensor_copy(out=ident[:], in_=ident_bf[:])
-        nc.vector.memset(vs[:, 0, :].bitcast(I32), 0)
+        nc.scalar.activation(out=ident[:], in_=ident_bf[:], func=COPY)
+        for gg in range(NG):
+            nc.vector.memset(vs[:, gg, :].bitcast(I32), 0)
         warm = bank(0, [P, PACK, P])
         for i in range(WARM_UPS):
-            nc.tensor.matmul(warm[:], lhsT=g_bf[:], rhs=g_bf[:].unsqueeze(1).to_broadcast([P, PACK, P]), start=True, stop=True)
-        new_wide(0)
+            nc.tensor.matmul(warm[:], lhsT=g_rows[:], rhs=g_rows[:].unsqueeze(1).to_broadcast([P, PACK, P]), start=True, stop=True)
         first_banks = [new_turned(0, FIRST), new_turned(0, FIRST - 1)]
-        for j in range(2):
-            first_copy = nc.scalar.copy if j else nc.vector.tensor_copy
-            first_copy(out=wide[0][:, KP * j : KP * (j + 1)], in_=pb_first[j][:].bitcast(E4M3))
-            turn_unit(first_banks[j], 0, j)
-        nc.vector.memset(vs[:, 1, :].bitcast(I32), 0)
-        for n in range(1, TURN_BANKS):
-            widen_to(n)
-            turn(n)
-        widen_to(4)
+        widen(nc.vector.tensor_copy)
+        turn_unit(first_banks[0], 0, 0)
+        widen()
+        turn_unit(first_banks[1], 0, 1)
+        nc.vector.tensor_copy(
+            out=vs_turned[:].rearrange("p (c j m) -> p c j m", c=2, j=PACK),
+            in_=vs_rows[:].rearrange("p (c m j) -> p c j m", c=2, j=PACK),
+        )
+        widen()
+        turn(1)
+        widen()
+        turn(2)
+        widen()
+        widen()
 
         for q in range(4):
             nc.sync.dma_start(
-                out=vs[32 * q : 32 * q + 4, :, :].bitcast(I32),
-                in_=v_scales[:, 4 * q : 4 * q + 4, :].rearrange("g q n -> q g n").bitcast(I32),
+                out=vs[32 * q : 32 * q + 4, :, 0 : KP * PLAIN].bitcast(I32),
+                in_=v_scales[:, 4 * q : 4 * q + 4, 0 : KP * PLAIN].rearrange("g q n -> q g n").bitcast(I32),
             )
+        for gg in range(NG):
+            for q in range(4):
+                for h in range(PLAIN // 2, 4):
+                    row = 64 * gg + 16 * q + h
+                    nc.sync.dma_start(
+                        out=vs[32 * q : 32 * q + 4, gg, 2 * KP * h : 2 * KP * (h + 1)].bitcast(I32),
+                        in_=vs_turned[row : row + 13 : 4, :].bitcast(I32),
+                    )
         vw = keep.tile([P, NG, 2 * D], U8, name="vw", align_bytes=ALIGN)
         for gg in range(NG):
             nc.sync.dma_start(out=vw[:, gg, :].bitcast(I32), in_=v_words[gg].bitcast(I32))
+        nc.sync.dma_start(out=g_rows[0 : PACK * PLAIN, :], in_=g[0 : KP * PLAIN].rearrange("(i p) -> i p", p=P))
 
-        nc.sync.dma_start(out=g_bf[0:NT, :], in_=g.rearrange("(i p) -> i p", p=P))
-        ab = new_scaled(0, 2)
-        planes = None
-        for k in range(PERIODS):
-            n = FIRST * k
-            c = 2 * k
-            on_scalar = k in SCALAR_PERIODS
-            split = X0_SPLIT if k == 0 else (X_SPLIT if on_scalar else L)
-            mixed = new_scaled(n + 2, 1)
-            pack_x(c, split)
-            if k == 0:
-                for j in range(2):
-                    product_units(0, first_banks[j], j, j + 1)
-            elif not on_scalar:
-                product(n)
-            pack_x_rest(c, split)
-            turn(n + 3)
-            if k > 0:
-                mm(n - 2)
+        pg = new_scaled(range(FIRST))
+        xg = new_packed()
+        interleave_gpsimd(xg, x_rows[0][:, 0, :, :], 0, X0_SPLIT[0])
+        for j in range(2):
+            product_units(0, first_banks[j], j, j + 1)
+        turn(3)
+        interleave(nc.scalar.copy, xg, x_rows[0][:, 0, :, :], X0_SPLIT[0], L)
+        product(1)
+        turn(4)
+        widen()
+        product(2)
+        turn(5)
+        quant_p(pg, both(0, 1))
+        quant_x(0, xg)
+        quant_p(scaled[2], both(2))
+        mm(0)
+        xg = new_packed()
+        interleave_gpsimd(xg[:, L : 2 * L, :], x_rows[0][:, 1, :, :], 0, X0_SPLIT[1])
+        interleave(nc.scalar.copy, xg[:, L : 2 * L, :], x_rows[0][:, 1, :, :], X0_SPLIT[1], L)
+        widen()
+        widen()
+        product(3)
+        mm(1)
+        turn(6)
+        product_planes(5)
+        product(4)
+        mm(2, 0, 1)
+        turn(7)
+        quant_x(1, xg)
+        quant_p(pg[:, 3 * STEP :, :], both(3, 4))
+        turn(8)
+        mm(2, 1, 2)
+        def pack_x(k):
+            t = new_packed()
+            split = X_SPLIT[k - 1]
+            gpsimd_copy(
+                t[:].rearrange("p (j l) t -> p j l t", j=2)[:, :, 0:split, :],
+                x_rows[k][:, :, :, 0:split].rearrange("p j t l -> p j l t"),
+            )
+            return t
+
+        def pack_x_rest(k, t):
+            split = X_SPLIT[k - 1]
+            nc.scalar.copy(
+                out=t[:].rearrange("p (j c i) t -> p j c t i", j=2, i=4)[:, :, split // 4 : L // 4, :, :],
+                in_=x_rows[k][:, :, :, split:L].rearrange("p j t (c i) -> p j c t i", i=4),
+            )
+
+        for k in range(1, PERIODS - 1):
+            n, c = FIRST * k, 2 * k
+            pg = new_scaled(range(n, n + FIRST))
+            xg = pack_x(k)
+            widen()
+            interleave(nc.scalar.copy, scaled[n], planes[n], 0, STEP)
             product(n + 1)
             turn(n + 4)
-            if k > 0:
-                mm(n - 1)
-            widen_to(n + 5)
+            mm(n - 2)
             product(n + 2)
             turn(n + 5)
-            if k > 0:
-                mm(n - 3, 1, 2)
-            widen_to(n + AHEAD[k])
-            quant_p(n, ab, 4)
-            quant_x(c)
-            quant_p(n + 2, mixed, 2)
-            mm(n)
-            split = X1_SPLIT if k == 0 else X_SPLIT
-            ab = new_scaled(n + 3, 2)
-            pack_x(c + 1, split)
-            pack_x_rest(c + 1, split)
+            mm(n - 1)
+            pack_x_rest(k, xg)
+            widen()
+            widen()
             product(n + 3)
             turn(n + 6)
-            mm(n + 1)
+            product_planes(n + 5)
             product(n + 4)
-            widen_to(n + 7)
             turn(n + 7)
-            mm(n + 2, 0, 1)
-            quant_x(c + 1)
-            quant_p(n + 3, ab, 4)
-            if k + 1 < PERIODS:
-                ab = new_scaled(n + 5, 2)
-            if k + 1 in SCALAR_PERIODS or k + 1 == PERIODS:
-                planes = product_planes(n + 5)
-                widen_to(len(wide))
-                if k + 1 < PERIODS:
-                    interleave(nc.scalar.copy, scaled[n + 5], planes, 0, 2 * P)
-            widen_to(n + AFTER[k])
-        for j in range(NC):
-            load_x_tiles(j)
-
-        n = SWEEP
-        own = new_packed()
-        interleave_gpsimd(own, planes, 0, 2 * P)
-        both = new_scaled(n + 1, 2)
-        turn(n + 3)
+            quant_p(pg, both(n, n + 1))
+            quant_x(c, xg)
+            quant_p(pg[:, 2 * STEP :, :], both(n + 2, n + 3))
+            quant_x(c + 1, xg)
+            quant_p(scaled[n + 4], both(n + 4))
+            mm(n)
+            turn(n + 8)
+            mm(n + 1)
+            mm(n + 2)
+        n, c = 15, 6
+        pg = new_scaled(range(n, n + 4))
+        xg = pack_x(PERIODS - 1)
+        interleave(nc.scalar.copy, scaled[n], planes[n], 0, STEP)
+        widen()
+        pack_x_rest(PERIODS - 1, xg)
+        product(n + 1)
+        turn(n + 4)
         mm(n - 2)
-        planes = product_planes(n + 3)
-        h_scalar(0, 0, L)
-        h_scalar(1, 0, L)
+        product_planes(n + 4)
+        product(n + 2)
+        turn(n + 5)
+        mm(n - 1)
+        product(n + 3)
+        turn(n + 6)
+        quant_p(pg, both(n, n + 1))
+        quant_x(c, xg)
+        quant_x(c + 1, xg)
+        quant_p(pg[:, 2 * STEP :, :], both(n + 2, n + 3))
+        mm(n)
+        mm(n + 1)
+        widen()
+        turn(n + 7)
+        mm(n + 2)
+        x_plain = new_x("xn")
+        for j in range(PLAIN):
+            nc.sync.dma_start(out=x_plain[:, j, :, :], in_=x[KP * j : KP * (j + 1), :].rearrange("(i p) l -> p i l", p=P))
+
+        n = 19
+        pg = new_scaled((n + 1, n + 2))
+        xg = new_packed((n,))
+        interleave_gpsimd(scaled[n], planes[n], 0, STEP)
+        nc.scalar.activation(out=a_f[:], in_=a_bf[:, :, 0:PACK], func=COPY)
+        widen()
+        product_planes(n + 3)
         product(n + 1)
         turn(n + 4)
         mm(n - 1)
-        mm(n - 3, 1, 2)
+        h_scalar(4, 0, L)
+        widen()
+        h_scalar(2, 0, L)
         product(n + 2)
         turn(n + 5)
-        turn(n + 6)
-        quant_p(n, own, 2)
-        quant_p(n + 1, both, 4)
+        quant_p(xg, both(n))
+        quant_p(pg, both(n + 1, n + 2))
         mm(n)
+        turn(n + 6)
         mm(n + 1)
-        own = new_packed()
-        interleave_gpsimd(own, planes, 0, 2 * P)
-        both = new_scaled(n + 4, 2)
-        widen_to(n + 7)
-        h_scalar(2, 0, L)
-        product(n + 4)
-        turn(n + 7)
-        mm(n + 2)
-        h_scalar(3, 0, L)
-        product(n + 5)
-        quant_p(n + 3, own, 2)
-        quant_p(n + 4, both, 4)
-        mm(n + 3)
-        widen_to(n + 8)
-        turn(n + 8)
-        mm(n + 4)
-        widen_to(n + 9)
-        turn(n + 9, 3)
-        widen_to(LAST)
-        planes = product_planes(n + 9)
-        h_own = new_packed()
-        interleave_gpsimd(h_own, h_planes[0], 0, H0_SPLIT)
-        both = new_scaled(n + 6, 2)
-        mixed = new_scaled(n + 8, 2)
-        h_scalar(4, 0, HALF)
-        interleave(nc.scalar.copy, scaled[n + 9], planes, 0, 2 * P)
-        h_scalar(4, HALF, L)
-        if H0_SPLIT < L:
-            interleave(nc.scalar.copy, h_own, h_planes[0], H0_SPLIT, L)
-        product(n + 6)
-        turn(n + 10, turn_bank(n + 9))
-        mm(n + 5)
-        product(n + 7)
-        turn(LAST, turn_bank(n + 10))
-        product(n + 8)
-        g_turned = bank(3, [P, NT])
-        nc.tensor.matmul(g_turned[:], lhsT=g_bf[:], rhs=ident_bf[:, 0:NT], start=True, stop=True)
-        nc.scalar.copy(out=g_f[:], in_=g_turned[:])
-        quant_p(n + 6, both, 4)
-        quant_p(n + 8, mixed, 2)
-        for i in range(6, 9):
-            mm(n + i)
-        new_scaled(n + 10, 2)
-        product(n + 10)
-        product_units(LAST, turned[LAST], 0, 1)
-        quant_p(n + 10, scaled[n + 10], 2)
-        quant_p(n + 9, scaled[n + 9], 2)
-        mm(n + 10)
-        mm(n + 9)
-        product_units(LAST, turned[LAST], 1, 2)
-        for j in range(2):
-            quant_p(LAST, scaled[LAST][:, P * j : P * (j + 1), :], 1, j)
-            mm(LAST, j, j + 1)
 
-        quant_h(0, 0, L, h_own)
+        n = 22
+        pg = new_scaled((n + 1, n + 2))
+        xg = new_packed((n,))
+        interleave_gpsimd(scaled[n], planes[n], 0, STEP)
+        widen()
+        widen()
+        product_planes(n + 3)
+        h_scalar(3, 0, L)
+        product(n + 1)
+        turn(n + 4)
+        mm(n - 1)
+        product(n + 2)
+        turn(n + 5)
+        quant_p(xg, both(n))
+        quant_p(pg, both(n + 1, n + 2))
+        mm(n)
+        turn(n + 6)
+        mm(n + 2)
+
+        n = 25
+        pg = new_scaled((n + 1, n + 2))
+        xg = new_packed((n, n + 3))
+        interleave_gpsimd(scaled[n], planes[n], 0, STEP)
+        widen()
+        widen()
+        product(n + 1)
+        turn(n + 4)
+        mm(n - 2)
+        h_scalar(0, 0, L)
+        product_planes(n + 4)
+        h_scalar(1, 0, L)
+        product(n + 2)
+        turn(n + 5)
+        product(n + 3)
+        turn(n + 6)
+        quant_p(pg, both(n + 1, n + 2))
+        quant_p(xg, both(n, n + 3))
+        mm(n + 1)
+        mm(n + 2)
+
+        n = 29
+        pg = new_scaled((n + 1, n + 2))
+        xg = new_packed((n,))
+        interleave_gpsimd(scaled[n], planes[n], 0, STEP)
+        interleave(nc.scalar.copy, h_packed[0], h_planes[0], 0, L)
+        product(n + 1)
+        mm(n - 4)
+        mm(n - 1)
+        g_turned = bank(OUT_BANKS[0], [P, PACK * PLAIN])
+        nc.tensor.matmul(g_turned[:], lhsT=g_rows[:], rhs=ident_bf[:, 0 : PACK * PLAIN], start=True, stop=True)
+        nc.scalar.copy(out=g_f[:, 0:PLAIN, :].rearrange("p c j -> p (c j)"), in_=g_turned[:])
+        nc.scalar.activation(out=g_f[:, PLAIN:NC, :], in_=g_bf[:, :, 0:PACK], func=COPY)
+        product_units(n + 2, turned[n + 2], 0, 1)
+        quant_p(scaled[n + 1], both(n + 1))
+        quant_p(xg, both(n))
+        mm(n + 1)
+        mm(n)
+        product_units(n + 2, turned[n + 2], 1, 2)
+        for j in range(2):
+            quant_p(scaled[n + 2][:, P * j : P * (j + 1), :], [(n + 2, j)])
+            mm(n + 2, j, j + 1)
+
+        quant_h(0, 0, L)
         for lo in (0, HALF):
             h_scalar(5, lo, lo + HALF)
             h_scalar(6, lo, lo + HALF)
@@ -487,21 +539,40 @@ def tile_stap_clutter_removal_s13_kernel(tc, x, g, p_bytes, p_scale, a, v_words,
         interleave(nc.vector.tensor_copy, h_packed[1], h_planes[1], 0, HALF)
         interleave(nc.scalar.copy, h_packed[1], h_planes[1], H_SPLIT, L)
         interleave(nc.vector.tensor_copy, h_packed[1], h_planes[1], HALF, H_SPLIT)
-        quant_h(1, 0, HALF, h_packed[1])
-        quant_h(1, HALF, L, h_packed[1])
+        quant_h(1, 0, HALF)
+        quant_h(1, HALF, L)
 
-        order = sorted(range(1, NT), key=lambda i: i - EARLY - 0.5 if i in SHARED else i)
+        tiles = PACK * NC
+        order = sorted(range(1, tiles), key=lambda i: i - EARLY - 0.5 if i in SHARED[:2] else i)
         jobs = [(0, 0, HALF), (0, HALF, L)] + [(i, 0, L) for i in order]
-        pair_heads = range(SINGLES, NT - 2, 2)
-        y, gx, o = {}, {}, {}
+        y, gx, o, words = {}, {}, {}, {}
+        vw16 = vw[:].bitcast(U16)
+
+        def reorder(c):
+            words[c] = work.tile([P, NG, 2 * KP], U8, name="vp", tag="vp", bufs=3, align_bytes=ALIGN)
+            nc.scalar.copy(
+                out=words[c][:].bitcast(U16).rearrange("p g (j m) -> p g j m", j=PACK),
+                in_=vw16[:, :, KP * c : KP * (c + 1)].rearrange("p g (m j) -> p g j m", j=PACK),
+            )
+
+        def x_tile(i):
+            c, j = divmod(i, PACK)
+            if c < PLAIN:
+                return x_plain[:, c, j, :]
+            return x_rows[c // 2][:, c % 2, j, :]
 
         def y_pass(k, gg):
             i, lo, hi = jobs[k]
+            c, j = divmod(i, PACK)
             if gg == 0:
                 y[k] = bank(OUT_BANKS[k % BANKS], [P, hi - lo])
+            if c < PLAIN:
+                w = vw[:, gg, 2 * P * i : 2 * P * (i + 1)]
+            else:
+                w = words[c][:, gg, 2 * P * j : 2 * P * (j + 1)]
             nc.tensor.matmul_mx(
                 out=y[k][:],
-                lhsT=vw[:, gg, 2 * P * i : 2 * P * (i + 1)].bitcast(E2M1X4),
+                lhsT=w.bitcast(E2M1X4),
                 lhsT_scale=vs[:, gg, P * i : P * (i + 1)],
                 rhs=hq[:, gg, lo:hi].bitcast(E4M3X4),
                 rhs_scale=hs[:, gg, lo:hi],
@@ -510,44 +581,48 @@ def tile_stap_clutter_removal_s13_kernel(tc, x, g, p_bytes, p_scale, a, v_words,
             )
 
         def gained(i):
-            gx[i] = work.tile([P, L], F32, name="gx", tag="gx", bufs=3)
-            nc.scalar.activation(
-                out=gx[i][:], in_=x_tiles[i // PACK][:, i % PACK, :], func=COPY, scale=g_f[:, i : i + 1]
-            )
+            gx[i] = work.tile([P, L], F32, name="gx", tag="gx", bufs=2)
+            nc.scalar.activation(out=gx[i][:], in_=x_tile(i), func=COPY, scale=g_f[:, i // PACK, i % PACK : i % PACK + 1])
 
+        reorder(PLAIN)
         gained(SHARED[0])
         for k in range(BANKS):
             y_pass(k, 0)
-        made = []
+        made, stored = [], [0]
         for k in range(len(jobs)):
             i, lo, hi = jobs[k]
+            c, j = divmod(i, PACK)
             y_pass(k, 1)
             if BANKS <= k + LEAD < len(jobs):
                 y_pass(k + LEAD, 0)
-            first = i - 1 if i - 1 in pair_heads else i
-            rows = 2 if first in pair_heads else 1
-            if first not in o:
-                o[first] = work.tile([P, 2, L], F32, name="o", tag="o", bufs=7, align_bytes=ALIGN)
-            dst = o[first][:, i - first, lo:hi]
+            if c not in o:
+                o[c] = work.tile([P, PACK, L], F32, name="o", tag="pg", bufs=4, align_bytes=ALIGN)
+            dst = o[c][:, j, lo:hi]
             if i in SHARED:
                 ys = work.tile([P, L], F32, name="ys", tag="ys", bufs=2)
                 nc.scalar.copy(out=ys[:], in_=y[k][:])
                 if i != SHARED[-1]:
-                    gained(i + SHARED.step)
+                    gained(SHARED[SHARED.index(i) + 1])
                 nc.gpsimd.tensor_tensor(out=dst, in0=gx[i][:], in1=ys[:], op=SUB)
             else:
                 nc.vector.scalar_tensor_tensor(
-                    out=dst,
-                    in0=x_tiles[i // PACK][:, i % PACK, lo:hi],
-                    scalar=g_f[:, i : i + 1],
-                    in1=y[k][:],
-                    op0=MULT,
-                    op1=SUB,
+                    out=dst, in0=x_tile(i)[:, lo:hi], scalar=g_f[:, c, j : j + 1], in1=y[k][:], op0=MULT, op1=SUB
                 )
             made.append(i)
-            if all(j in made for j in range(first, first + rows)):
-                queue = nc.scalar if first in SECOND_QUEUE else nc.sync
-                queue.dma_start(
-                    out=out[P * first : P * (first + rows), lo:hi].rearrange("(i p) l -> p i l", p=P),
-                    in_=o[first][:, 0:rows, lo:hi],
+            if j == 1 and PLAIN < c + 2 < NC:
+                reorder(c + 2)
+            while stored[0] < PACK * PLAIN and stored[0] in made and stored[0] <= max(e for e in made if e not in SHARED):
+                e = stored[0]
+                nc.sync.dma_start(out=out[P * e : P * (e + 1), lo:hi], in_=o[e // PACK][:, e % PACK, lo:hi])
+                if hi < L:
+                    break
+                stored[0] = e + 1
+            if c < PLAIN:
+                continue
+            rows = 2 if c in PAIRED else PACK
+            j0 = j - j % rows
+            if all(PACK * c + e in made for e in range(j0, j0 + rows)):
+                nc.sync.dma_start(
+                    out=out[KP * c : KP * (c + 1), :].rearrange("(m j) l -> m j l", j=PACK)[:, j0 : j0 + rows, :],
+                    in_=o[c][:, j0 : j0 + rows, :],
                 )

@@ -36,8 +36,7 @@ PERIODS = NC // 2
 SWEEP = FIRST * PERIODS
 STEPS = 32
 WARM_UPS = 3
-X_SPLIT = (400, 400, 288)
-X0_SPLIT = (416, 368)
+X_SPLIT = (416, 352, 352, 352, 352, 352, 352, 128)
 H_SPLIT = 352
 PLAIN = 2
 LEAD = 1
@@ -187,7 +186,7 @@ def tile_stap_clutter_removal_s13_kernel(tc, x, g, p_bytes, p_scale, a, v_words,
                 turn_unit(turned[n], n, j)
 
         def new_scaled(steps, tag="pg", bufs=4):
-            t = work.tile([P, FIRST * STEP if tag == "pg" else 2 * L, PACK], BF16, name=tag, tag=tag, bufs=bufs, align_bytes=ALIGN)
+            t = work.tile([P, FIRST * STEP if tag == "pg" else L, PACK], BF16, name=tag, tag=tag, bufs=bufs, align_bytes=ALIGN)
             for i, n in enumerate(steps):
                 scaled[n] = t[:, STEP * i : STEP * (i + 1), :]
             return t
@@ -255,11 +254,11 @@ def tile_stap_clutter_removal_s13_kernel(tc, x, g, p_bytes, p_scale, a, v_words,
         def interleave_gpsimd(dst, src, lo, hi):
             gpsimd_copy(dst[:, lo:hi, :], src[:, :, lo:hi].rearrange("p t l -> p l t"))
 
-        def quant_x(c, packed):
+        def quant_x(c, packed, lo=0, hi=L):
             nc.vector.quantize_mx(
-                out=xq[:, c, :].bitcast(E4M3X4),
-                scales=xs[:, c, :],
-                in_=packed[:, L * (c % 2) : L * (c % 2 + 1), :].rearrange("p l t -> p (l t)"),
+                out=xq[:, c, lo:hi].bitcast(E4M3X4),
+                scales=xs[:, c, lo:hi],
+                in_=packed[:, lo:hi, :].rearrange("p l t -> p (l t)"),
             )
 
         def mm(n, lo=0, hi=2):
@@ -342,107 +341,67 @@ def tile_stap_clutter_removal_s13_kernel(tc, x, g, p_bytes, p_scale, a, v_words,
             nc.sync.dma_start(out=vw[:, gg, :].bitcast(I32), in_=v_words[gg].bitcast(I32))
         nc.sync.dma_start(out=g_rows[0 : PACK * PLAIN, :], in_=g[0 : KP * PLAIN].rearrange("(i p) -> i p", p=P))
 
-        pg = new_scaled(range(FIRST))
-        xg = new_packed()
-        interleave_gpsimd(xg, x_rows[0][:, 0, :, :], 0, X0_SPLIT[0])
-        for j in range(2):
-            product_units(0, first_banks[j], j, j + 1)
-        turn(3)
-        interleave(nc.scalar.copy, xg, x_rows[0][:, 0, :, :], X0_SPLIT[0], L)
-        product(1)
-        turn(4)
-        widen()
-        product(2)
-        turn(5)
-        quant_p(pg, both(0, 1))
-        quant_x(0, xg)
-        quant_p(scaled[2], both(2))
-        mm(0)
-        xg = new_packed()
-        interleave_gpsimd(xg[:, L : 2 * L, :], x_rows[0][:, 1, :, :], 0, X0_SPLIT[1])
-        interleave(nc.scalar.copy, xg[:, L : 2 * L, :], x_rows[0][:, 1, :, :], X0_SPLIT[1], L)
-        widen()
-        widen()
-        product(3)
-        mm(1)
-        turn(6)
-        product_planes(5)
-        product(4)
-        mm(2, 0, 1)
-        turn(7)
-        quant_x(1, xg)
-        quant_p(pg[:, 3 * STEP :, :], both(3, 4))
-        turn(8)
-        mm(2, 1, 2)
-        def pack_x(k):
+        def pack_x(c):
             t = new_packed()
-            split = X_SPLIT[k - 1]
-            gpsimd_copy(
-                t[:].rearrange("p (j l) t -> p j l t", j=2)[:, :, 0:split, :],
-                x_rows[k][:, :, :, 0:split].rearrange("p j t l -> p j l t"),
-            )
+            interleave_gpsimd(t, x_rows[c // 2][:, c % 2, :, :], 0, X_SPLIT[c])
             return t
 
-        def pack_x_rest(k, t):
-            split = X_SPLIT[k - 1]
-            nc.scalar.copy(
-                out=t[:].rearrange("p (j c i) t -> p j c t i", j=2, i=4)[:, :, split // 4 : L // 4, :, :],
-                in_=x_rows[k][:, :, :, split:L].rearrange("p j t (c i) -> p j c t i", i=4),
-            )
+        def pack_x_rest(c, t):
+            interleave(nc.scalar.copy, t, x_rows[c // 2][:, c % 2, :, :], X_SPLIT[c], L)
 
-        for k in range(1, PERIODS - 1):
+        for k in range(PERIODS):
             n, c = FIRST * k, 2 * k
-            pg = new_scaled(range(n, n + FIRST))
-            xg = pack_x(k)
+            last = k == PERIODS - 1
+            pg = new_scaled(range(n, n + FIRST - last))
+            xg = pack_x(c)
+            if k == 0:
+                for j in range(2):
+                    product_units(0, first_banks[j], j, j + 1)
+                turn(3)
+                pack_x_rest(c, xg)
+            else:
+                interleave(nc.scalar.copy, scaled[n], planes[n], 0, STEP)
+                pack_x_rest(c, xg)
+                turn(n + 3)
+                mm(n - 2)
             widen()
-            interleave(nc.scalar.copy, scaled[n], planes[n], 0, STEP)
             product(n + 1)
             turn(n + 4)
-            mm(n - 2)
+            if k > 0:
+                mm(n - 1)
+            if last:
+                interleave(nc.scalar.copy, h_packed[1], x_rows[k][:, 1, :, :], X_SPLIT[c + 1], L)
+                product_planes(n + 4)
             product(n + 2)
             turn(n + 5)
-            mm(n - 1)
-            pack_x_rest(k, xg)
-            widen()
-            widen()
-            product(n + 3)
-            turn(n + 6)
-            product_planes(n + 5)
-            product(n + 4)
-            turn(n + 7)
+            if k > 0:
+                mm(n - 3, 1, 2)
             quant_p(pg, both(n, n + 1))
             quant_x(c, xg)
-            quant_p(pg[:, 2 * STEP :, :], both(n + 2, n + 3))
-            quant_x(c + 1, xg)
-            quant_p(scaled[n + 4], both(n + 4))
+            quant_p(scaled[n + 2], both(n + 2))
             mm(n)
-            turn(n + 8)
+            xg = pack_x(c + 1)
+            widen()
+            if not last:
+                pack_x_rest(c + 1, xg)
+            product(n + 3)
             mm(n + 1)
-            mm(n + 2)
-        n, c = 15, 6
-        pg = new_scaled(range(n, n + 4))
-        xg = pack_x(PERIODS - 1)
-        interleave(nc.scalar.copy, scaled[n], planes[n], 0, STEP)
-        widen()
-        pack_x_rest(PERIODS - 1, xg)
-        product(n + 1)
-        turn(n + 4)
-        mm(n - 2)
-        product_planes(n + 4)
-        product(n + 2)
-        turn(n + 5)
-        mm(n - 1)
-        product(n + 3)
-        turn(n + 6)
-        quant_p(pg, both(n, n + 1))
-        quant_x(c, xg)
-        quant_x(c + 1, xg)
-        quant_p(pg[:, 2 * STEP :, :], both(n + 2, n + 3))
-        mm(n)
-        mm(n + 1)
-        widen()
+            turn(n + 6)
+            if last:
+                break
+            widen()
+            product_planes(n + 5)
+            product(n + 4)
+            mm(n + 2, 0, 1)
+            turn(n + 7)
+            quant_x(c + 1, xg)
+            quant_p(pg[:, 3 * STEP :, :], both(n + 3, n + 4))
+        quant_x(c + 1, h_packed[1], X_SPLIT[c + 1], L)
+        quant_x(c + 1, xg, 0, X_SPLIT[c + 1])
+        quant_p(scaled[n + 3], both(n + 3))
+        mm(n + 2, 0, 1)
         turn(n + 7)
-        mm(n + 2)
+        mm(n + 2, 1, 2)
         x_plain = new_x("xn")
         for j in range(PLAIN):
             nc.sync.dma_start(out=x_plain[:, j, :, :], in_=x[KP * j : KP * (j + 1), :].rearrange("(i p) l -> p i l", p=P))
@@ -453,12 +412,12 @@ def tile_stap_clutter_removal_s13_kernel(tc, x, g, p_bytes, p_scale, a, v_words,
         interleave_gpsimd(scaled[n], planes[n], 0, STEP)
         nc.scalar.activation(out=a_f[:], in_=a_bf[:, :, 0:PACK], func=COPY)
         widen()
+        widen()
         product_planes(n + 3)
         product(n + 1)
         turn(n + 4)
         mm(n - 1)
         h_scalar(4, 0, L)
-        widen()
         h_scalar(2, 0, L)
         product(n + 2)
         turn(n + 5)
@@ -475,6 +434,7 @@ def tile_stap_clutter_removal_s13_kernel(tc, x, g, p_bytes, p_scale, a, v_words,
         widen()
         widen()
         product_planes(n + 3)
+        widen()
         h_scalar(3, 0, L)
         product(n + 1)
         turn(n + 4)
@@ -485,27 +445,26 @@ def tile_stap_clutter_removal_s13_kernel(tc, x, g, p_bytes, p_scale, a, v_words,
         quant_p(pg, both(n + 1, n + 2))
         mm(n)
         turn(n + 6)
-        mm(n + 2)
 
         n = 25
-        pg = new_scaled((n + 1, n + 2))
-        xg = new_packed((n, n + 3))
+        pg = new_scaled((n + 1, n + 3))
+        xg = new_packed((n, n + 2))
         interleave_gpsimd(scaled[n], planes[n], 0, STEP)
-        widen()
         widen()
         product(n + 1)
         turn(n + 4)
+        mm(n - 1)
         mm(n - 2)
-        h_scalar(0, 0, L)
         product_planes(n + 4)
+        h_scalar(0, 0, L)
         h_scalar(1, 0, L)
         product(n + 2)
         turn(n + 5)
         product(n + 3)
         turn(n + 6)
-        quant_p(pg, both(n + 1, n + 2))
-        quant_p(xg, both(n, n + 3))
-        mm(n + 1)
+        quant_p(xg, both(n, n + 2))
+        quant_p(pg, both(n + 1, n + 3))
+        mm(n)
         mm(n + 2)
 
         n = 29
@@ -514,7 +473,7 @@ def tile_stap_clutter_removal_s13_kernel(tc, x, g, p_bytes, p_scale, a, v_words,
         interleave_gpsimd(scaled[n], planes[n], 0, STEP)
         interleave(nc.scalar.copy, h_packed[0], h_planes[0], 0, L)
         product(n + 1)
-        mm(n - 4)
+        mm(n - 3)
         mm(n - 1)
         g_turned = bank(OUT_BANKS[0], [P, PACK * PLAIN])
         nc.tensor.matmul(g_turned[:], lhsT=g_rows[:], rhs=ident_bf[:, 0 : PACK * PLAIN], start=True, stop=True)

@@ -28,6 +28,7 @@ NG = R // KP
 BANKS = 8
 HALF = L // 2
 ALIGN = 64
+MX_ALIGN = 256
 STEP = 2 * P
 
 FIRST = 5
@@ -140,12 +141,12 @@ def tile_stap_clutter_removal_s13_kernel(tc, x, g, p_bytes, p_scale, a, v_words,
             out=g_bf[:, :, 0:PACK], in_=g[KP * PLAIN : D].rearrange("(c m j) -> m c j", m=P, j=PACK)
         )
 
-        vs = keep.tile([P, NG, D], U8, name="vs", align_bytes=ALIGN)
+        vs = keep.tile([P, NG, D], U8, name="vs", align_bytes=MX_ALIGN)
         vs_turned = keep.tile([P, 2 * KP], U8, name="vs_turned", align_bytes=ALIGN)
-        xq = keep.tile([P, NC, L], U32, name="xq", align_bytes=ALIGN)
-        xs = keep.tile([P, NC, L], U8, name="xs", align_bytes=ALIGN)
-        hq = keep.tile([P, NG, L], U32, name="hq", align_bytes=ALIGN)
-        hs = keep.tile([P, NG, L], U8, name="hs", align_bytes=ALIGN)
+        xq = keep.tile([P, NC, L], U32, name="xq", align_bytes=MX_ALIGN)
+        xs = keep.tile([P, NC, L], U8, name="xs", align_bytes=MX_ALIGN)
+        hq = keep.tile([P, NG, L], U32, name="hq", align_bytes=MX_ALIGN)
+        hs = keep.tile([P, NG, L], U8, name="hs", align_bytes=MX_ALIGN)
         h_planes = [keep.tile([P, PACK, L], BF16, name="hp%d" % gg, align_bytes=ALIGN) for gg in range(NG)]
         h_packed = [keep.tile([P, L, PACK], BF16, name="hg%d" % gg, align_bytes=ALIGN) for gg in range(NG)]
         a_f = keep.tile([P, NG, PACK], F32, name="a_f")
@@ -230,8 +231,8 @@ def tile_stap_clutter_removal_s13_kernel(tc, x, g, p_bytes, p_scale, a, v_words,
                 nc.scalar.activation(out=planes[n][:, t, :], in_=src, func=COPY, scale=scales(c)[:, 0, t : t + 1])
 
         def quant_p(src, units):
-            q = work.tile([P, 2 * STEP], U32, name="pq", tag="pq", bufs=6, align_bytes=ALIGN)
-            sc = work.tile([P, 2 * STEP], U8, name="ps", tag="ps", bufs=6, align_bytes=ALIGN)
+            q = work.tile([P, 2 * STEP], U32, name="pq", tag="pq", bufs=6, align_bytes=MX_ALIGN)
+            sc = work.tile([P, 2 * STEP], U8, name="ps", tag="ps", bufs=6, align_bytes=MX_ALIGN)
             w = P * len(units)
             nc.vector.quantize_mx(
                 out=q[:, 0:w].bitcast(E4M3X4), scales=sc[:, 0:w], in_=src[:, 0:w, :].rearrange("p m t -> p (m t)")
@@ -336,7 +337,7 @@ def tile_stap_clutter_removal_s13_kernel(tc, x, g, p_bytes, p_scale, a, v_words,
                         out=vs[32 * q : 32 * q + 4, gg, 2 * KP * h : 2 * KP * (h + 1)].bitcast(I32),
                         in_=vs_turned[row : row + 13 : 4, :].bitcast(I32),
                     )
-        vw = keep.tile([P, NG, 2 * D], U8, name="vw", align_bytes=ALIGN)
+        vw = keep.tile([P, NG, 2 * D], U8, name="vw", align_bytes=MX_ALIGN)
         for gg in range(NG):
             nc.sync.dma_start(out=vw[:, gg, :].bitcast(I32), in_=v_words[gg].bitcast(I32))
         nc.sync.dma_start(out=g_rows[0 : PACK * PLAIN, :], in_=g[0 : KP * PLAIN].rearrange("(i p) -> i p", p=P))
@@ -508,7 +509,7 @@ def tile_stap_clutter_removal_s13_kernel(tc, x, g, p_bytes, p_scale, a, v_words,
         vw16 = vw[:].bitcast(U16)
 
         def reorder(c):
-            words[c] = work.tile([P, NG, 2 * KP], U8, name="vp", tag="vp", bufs=3, align_bytes=ALIGN)
+            words[c] = work.tile([P, NG, 2 * KP], U8, name="vp", tag="vp", bufs=3, align_bytes=MX_ALIGN)
             nc.scalar.copy(
                 out=words[c][:].bitcast(U16).rearrange("p g (j m) -> p g j m", j=PACK),
                 in_=vw16[:, :, KP * c : KP * (c + 1)].rearrange("p g (m j) -> p g j m", j=PACK),

@@ -159,7 +159,7 @@ def tile_stap_clutter_removal_s13_kernel(tc, x, g, p_bytes, p_scale, a, v_words,
             t, units = pieces[len(widened)]
             widened.append(units)
             if len(units) > 2:
-                w = work.tile([P, 4 * KP], BF16, name="w", tag="w4", bufs=4, align_bytes=ALIGN)
+                w = work.tile([P, 4 * KP], BF16, name="w", tag="w4", bufs=5, align_bytes=ALIGN)
             else:
                 w = work.tile([P, 2 * KP], BF16, name="w", tag="w2", bufs=4, align_bytes=ALIGN)
             copy(out=w[:, 0 : KP * len(units)], in_=t[:].rearrange("p r k -> p (r k)").bitcast(E4M3))
@@ -186,14 +186,23 @@ def tile_stap_clutter_removal_s13_kernel(tc, x, g, p_bytes, p_scale, a, v_words,
             for j in range(2):
                 turn_unit(turned[n], n, j)
 
-        def new_scaled(steps, tag="pg", bufs=4):
-            t = work.tile([P, FIRST * STEP if tag == "pg" else L, PACK], BF16, name=tag, tag=tag, bufs=bufs, align_bytes=ALIGN)
+        def new_scaled(steps):
+            t = work.tile([P, 4 * STEP, PACK], BF16, name="pg", tag="pg", bufs=4, align_bytes=ALIGN)
             for i, n in enumerate(steps):
                 scaled[n] = t[:, STEP * i : STEP * (i + 1), :]
             return t
 
-        def new_packed(steps=()):
-            return new_scaled(steps, "xg", 1)
+        packed = keep.tile([P, 2 * L, PACK], BF16, name="packed", align_bytes=ALIGN)
+
+        def new_packed(steps):
+            t = packed[:, L - P : 2 * L - P, :]
+            for i, n in enumerate(steps):
+                scaled[n] = t[:, STEP * i : STEP * (i + 1), :]
+            return t
+
+        def x_packed(c):
+            first = 0 if c % 2 == 0 else L - X_SPLIT[c]
+            return packed[:, first : first + L, :]
 
         def product_units(n, src, lo, hi):
             nc.vector.tensor_tensor(
@@ -255,11 +264,9 @@ def tile_stap_clutter_removal_s13_kernel(tc, x, g, p_bytes, p_scale, a, v_words,
         def interleave_gpsimd(dst, src, lo, hi):
             gpsimd_copy(dst[:, lo:hi, :], src[:, :, lo:hi].rearrange("p t l -> p l t"))
 
-        def quant_x(c, packed, lo=0, hi=L):
+        def quant_x(c):
             nc.vector.quantize_mx(
-                out=xq[:, c, lo:hi].bitcast(E4M3X4),
-                scales=xs[:, c, lo:hi],
-                in_=packed[:, lo:hi, :].rearrange("p l t -> p (l t)"),
+                out=xq[:, c, :].bitcast(E4M3X4), scales=xs[:, c, :], in_=x_packed(c).rearrange("p l t -> p (l t)")
             )
 
         def mm(n, lo=0, hi=2):
@@ -343,48 +350,47 @@ def tile_stap_clutter_removal_s13_kernel(tc, x, g, p_bytes, p_scale, a, v_words,
         nc.sync.dma_start(out=g_rows[0 : PACK * PLAIN, :], in_=g[0 : KP * PLAIN].rearrange("(i p) -> i p", p=P))
 
         def pack_x(c):
-            t = new_packed()
-            interleave_gpsimd(t, x_rows[c // 2][:, c % 2, :, :], 0, X_SPLIT[c])
-            return t
+            lo = L - X_SPLIT[c] if c % 2 == 0 else 0
+            interleave_gpsimd(x_packed(c), x_rows[c // 2][:, c % 2, :, :], lo, lo + X_SPLIT[c])
 
-        def pack_x_rest(c, t):
-            interleave(nc.scalar.copy, t, x_rows[c // 2][:, c % 2, :, :], X_SPLIT[c], L)
+        def pack_x_rest(c):
+            lo = 0 if c % 2 == 0 else X_SPLIT[c]
+            interleave(nc.scalar.copy, x_packed(c), x_rows[c // 2][:, c % 2, :, :], lo, lo + L - X_SPLIT[c])
 
         for k in range(PERIODS):
             n, c = FIRST * k, 2 * k
             last = k == PERIODS - 1
-            pg = new_scaled(range(n, n + FIRST - last))
-            xg = pack_x(c)
+            pg = new_scaled(range(n, n + 3))
+            pack_x(c)
+            pack_x_rest(c)
             if k == 0:
                 for j in range(2):
                     product_units(0, first_banks[j], j, j + 1)
                 turn(3)
-                pack_x_rest(c, xg)
             else:
                 interleave(nc.scalar.copy, scaled[n], planes[n], 0, STEP)
-                pack_x_rest(c, xg)
                 turn(n + 3)
                 mm(n - 2)
-            widen()
+            if not last:
+                widen()
+            pack_x_rest(c + 1)
             product(n + 1)
             turn(n + 4)
             if k > 0:
                 mm(n - 1)
             if last:
-                interleave(nc.scalar.copy, h_packed[1], x_rows[k][:, 1, :, :], X_SPLIT[c + 1], L)
                 product_planes(n + 4)
             product(n + 2)
             turn(n + 5)
             if k > 0:
                 mm(n - 3, 1, 2)
             quant_p(pg, both(n, n + 1))
-            quant_x(c, xg)
+            quant_x(c)
             quant_p(scaled[n + 2], both(n + 2))
             mm(n)
-            xg = pack_x(c + 1)
+            pack_x(c + 1)
+            pg = new_scaled(range(n + 3, n + 5 - last))
             widen()
-            if not last:
-                pack_x_rest(c + 1, xg)
             product(n + 3)
             mm(n + 1)
             turn(n + 6)
@@ -392,14 +398,15 @@ def tile_stap_clutter_removal_s13_kernel(tc, x, g, p_bytes, p_scale, a, v_words,
                 break
             widen()
             product_planes(n + 5)
+            if k == PERIODS - 2:
+                widen()
             product(n + 4)
             mm(n + 2, 0, 1)
             turn(n + 7)
-            quant_x(c + 1, xg)
-            quant_p(pg[:, 3 * STEP :, :], both(n + 3, n + 4))
-        quant_x(c + 1, h_packed[1], X_SPLIT[c + 1], L)
-        quant_x(c + 1, xg, 0, X_SPLIT[c + 1])
-        quant_p(scaled[n + 3], both(n + 3))
+            quant_x(c + 1)
+            quant_p(pg, both(n + 3, n + 4))
+        quant_x(c + 1)
+        quant_p(pg, both(n + 3))
         mm(n + 2, 0, 1)
         turn(n + 7)
         mm(n + 2, 1, 2)

@@ -64,7 +64,7 @@ def steps_in_order():
 
 
 UNITS = steps_in_order()
-WORD_STEPS = (6, 8, 9, 11, 13, 14, 16, 18)
+WORD_STEPS = (6, 8, 9, 11, 13, 14, 16, 18) + tuple(range(19, 32))
 
 
 def tile_stap_clutter_removal_s13_kernel(tc, x, g, p_bytes, p_scale, a, v_words, v_scales, out):
@@ -155,14 +155,17 @@ def tile_stap_clutter_removal_s13_kernel(tc, x, g, p_bytes, p_scale, a, v_words,
         wide, turned, scaled, planes, pq, sums, done = {}, {}, {}, {}, {}, {}, {}
         widened = []
 
-        def widen(copy=nc.scalar.copy):
+        def widen(copy=nc.scalar.copy, order="p n u q e"):
             t, units = pieces[len(widened)]
             widened.append(units)
             if len(units) > 2:
                 w = work.tile([P, 4 * KP], BF16, name="w", tag="w4", bufs=5, align_bytes=ALIGN)
             else:
                 w = work.tile([P, 2 * KP], BF16, name="w", tag="w2", bufs=4, align_bytes=ALIGN)
-            copy(out=w[:, 0 : KP * len(units)], in_=t[:].rearrange("p r k -> p (r k)").bitcast(E4M3))
+            copy(
+                out=w[:, 0 : KP * len(units)].rearrange("p (n u q e) -> " + order, u=2, q=P, e=2),
+                in_=t[:].rearrange("p r k -> p (r k)").bitcast(E4M3).rearrange("p (n q u e) -> " + order, u=2, q=P, e=2),
+            )
             for i, u in enumerate(units):
                 wide[u] = w[:, KP * i : KP * (i + 1)]
 
@@ -176,10 +179,10 @@ def tile_stap_clutter_removal_s13_kernel(tc, x, g, p_bytes, p_scale, a, v_words,
             if n in WORD_STEPS:
                 words = src.bitcast(F32)
                 for u in range(2):
-                    nc.tensor.transpose(dst[:, u, j, :], words[:, u : 2 * P : 2], ident[:])
+                    nc.tensor.transpose(dst[:, u, j, :], words[:, P * u : P * (u + 1)], ident[:])
             else:
                 for t in range(PACK):
-                    nc.tensor.matmul(dst[:, t, j, :], lhsT=src[:, t:KP:PACK], rhs=ident_bf[:], start=True, stop=True)
+                    nc.tensor.matmul(dst[:, t, j, :], lhsT=src[:, 2 * P * (t // 2) + t % 2 : 2 * P * (t // 2 + 1) : 2], rhs=ident_bf[:], start=True, stop=True)
 
         def turn(n, b=None):
             turned[n] = new_turned(n, FIRST + n % TURN_BANKS if b is None else b)
@@ -204,39 +207,29 @@ def tile_stap_clutter_removal_s13_kernel(tc, x, g, p_bytes, p_scale, a, v_words,
             first = 0 if c % 2 == 0 else L - X_SPLIT[c]
             return packed[:, first : first + L, :]
 
+        def values(n, src):
+            if n in WORD_STEPS:
+                return src[:].bitcast(BF16).rearrange("p u j (m e) -> p j m u e", e=2)
+            return src[:].rearrange("p (u e) j m -> p j m u e", e=2)
+
         def product_units(n, src, lo, hi):
+            c, passes = UNITS[n][lo][1], UNITS[n][hi - 1][1] - UNITS[n][lo][1] + 1
+            s = scales(c, passes).unsqueeze(2).to_broadcast([P, passes, P * (hi - lo) // passes, PACK])
             nc.vector.tensor_tensor(
-                out=scaled[n][:, P * lo : P * hi, :],
-                in0=src[:, :, lo:hi, :].rearrange("p t j m -> p (j m) t"),
-                in1=scales(UNITS[n][lo][1]).to_broadcast([P, P * (hi - lo), PACK]),
+                out=scaled[n][:, P * lo : P * hi, :].rearrange("p (c m) (u e) -> p c m u e", c=passes, e=2),
+                in0=values(n, src)[:, lo:hi].rearrange("p j m u e -> p (j m) u e").rearrange("p (c m) u e -> p c m u e", c=passes),
+                in1=s.rearrange("p c m (u e) -> p c m u e", e=2),
                 op=MULT,
             )
 
         def product(n):
-            c0, c1 = UNITS[n][0][1], UNITS[n][1][1]
-            if n in WORD_STEPS:
-                words = turned[n][:].rearrange("p u j m -> p (u j m)").bitcast(BF16)
-                nc.vector.tensor_tensor(
-                    out=scaled[n].rearrange("p m (u e) -> p m u e", u=2),
-                    in0=words.rearrange("p (u m e) -> p m u e", u=2, e=2),
-                    in1=scales(c0).to_broadcast([P, 2 * P, PACK]),
-                    op=MULT,
-                )
-            elif c0 == c1:
-                product_units(n, turned[n], 0, 2)
-            else:
-                nc.vector.tensor_tensor(
-                    out=scaled[n].rearrange("p (j m) t -> p j m t", j=2),
-                    in0=turned[n][:].rearrange("p t j m -> p j m t"),
-                    in1=scales(c0, 2).unsqueeze(2).to_broadcast([P, 2, P, PACK]),
-                    op=MULT,
-                )
+            product_units(n, turned[n], 0, 2)
 
         def product_planes(n):
             c = UNITS[n][0][1]
             planes[n] = work.tile([P, PACK, STEP], BF16, name="planes", tag="planes", bufs=2, align_bytes=ALIGN)
             for t in range(PACK):
-                src = turned[n][:, t, :, :].rearrange("p j m -> p (j m)")
+                src = values(n, turned[n])[:, :, :, t // 2, t % 2].rearrange("p j m -> p (j m)")
                 nc.scalar.activation(out=planes[n][:, t, :], in_=src, func=COPY, scale=scales(c)[:, 0, t : t + 1])
 
         def quant_p(src, units):
@@ -316,7 +309,7 @@ def tile_stap_clutter_removal_s13_kernel(tc, x, g, p_bytes, p_scale, a, v_words,
         for i in range(WARM_UPS):
             nc.tensor.matmul(warm[:], lhsT=g_rows[:], rhs=g_rows[:].unsqueeze(1).to_broadcast([P, PACK, P]), start=True, stop=True)
         first_banks = [new_turned(0, FIRST), new_turned(0, FIRST - 1)]
-        widen(nc.vector.tensor_copy)
+        widen(nc.vector.tensor_copy, "p n q u e")
         turn_unit(first_banks[0], 0, 0)
         widen()
         turn_unit(first_banks[1], 0, 1)

from contextlib import ExitStack

import concourse.mybir as mybir
from concourse.masks import make_identity

D, R, L = 4096, 1024, 512
FLOPS = 4 * D * R * L

F32 = mybir.dt.float32
BF16 = mybir.dt.bfloat16
I32 = mybir.dt.int32
U32 = mybir.dt.uint32
U16 = mybir.dt.uint16
U8 = mybir.dt.uint8
E4M3 = mybir.dt.float8_e4m3fn
E4M3X4 = mybir.dt.float8_e4m3fn_x4
E2M1X4 = mybir.dt.float4_e2m1fn_x4
MULT = mybir.AluOpType.mult
ADD = mybir.AluOpType.add
SUB = mybir.AluOpType.subtract
COPY = mybir.ActivationFunctionType.Copy

P = 128
PACK = 4
KP = P * PACK
NC = D // KP
NG = R // KP
BANKS = 8
HALF = L // 2
ALIGN = 64
MX_ALIGN = 256
STEP = 2 * P

FIRST = 5
TURN_BANKS = 3
PERIODS = NC // 2
SWEEP = FIRST * PERIODS
STEPS = 32
WARM_UPS = 3
X_SPLIT = (416, 352, 352, 352, 352, 352, 352, 128)
H_SPLIT = 352
PLAIN = 2
LEAD = 1
SHARED = (4, 9, 12, 20, 28)
EARLY = 2
PAIRED = (2, 3, 7)
OUT_BANKS = (0, 1, 7, 5, 6, 4, 2, 3)
SUM_BANK = (0, 1, 2, 3, 4, 4, 2, 3)


def steps_in_order():
    steps = []
    for k in range(PERIODS):
        c = 2 * k
        steps.extend([((0, c), (1, c)), ((2, c), (3, c)), ((4, c), (4, c + 1)), ((0, c + 1), (1, c + 1)), ((2, c + 1), (3, c + 1))])
    steps[-2], steps[-1] = steps[-1], steps[-2]
    pair = [((5, c), (6, c)) for c in range(NC)]
    last = [((7, c), (7, c + 1)) for c in range(0, NC, 2)]
    steps.extend([pair[0], pair[1]])
    steps.extend([pair[2], last[0], pair[3]])
    steps.extend([pair[4], last[1], pair[5], last[2]])
    steps.extend([pair[6], pair[7], last[3]])
    return steps


UNITS = steps_in_order()
WORD_STEPS = (6, 8, 9, 11, 13, 14, 16, 18) + tuple(range(19, 32))


def tile_stap_clutter_removal_s13_kernel(tc, x, g, p_bytes, p_scale, a, v_words, v_scales, out):
    nc = tc.nc
    with ExitStack() as ctx:
        keep = ctx.enter_context(tc.tile_pool(name="keep", bufs=1))
        work = ctx.enter_context(tc.tile_pool(name="work", bufs=3))
        psum = ctx.enter_context(tc.psum_pool(name="psum", bufs=1))
        ctx.enter_context(tc.manual_schedule())

        def bank(b, shape, dtype=F32):
            return psum.tile(shape, dtype, name="bank%d" % b, tag="bank%d" % b)

        ident_bf = keep.tile([P, P], BF16, name="ident_bf")
        make_identity(nc, ident_bf[:])
        g_rows = keep.tile([P, P], BF16, name="g_rows")
        nc.vector.memset(g_rows[:], 0.0)

        p_by = p_bytes.rearrange("(g m t) k -> g m t k", g=NG, t=PACK)
        pieces = []

        def load_p(r, tiles, c, passes):
            t = keep.tile([P, tiles, KP * passes], U8, name="pb_%d_%d" % (r, c), align_bytes=ALIGN)
            nc.sync.dma_start(out=t[:], in_=p_by[r // PACK][:, r % PACK : r % PACK + tiles, KP * c : KP * (c + passes)])
            pieces.append((t, [(r + i, c + j) for i in range(tiles) for j in range(passes)]))

        x_rows = {}

        def new_x(name):
            return work.tile([P, 2, PACK, L], BF16, name=name, tag="xr", bufs=PERIODS, align_bytes=ALIGN)

        def load_x(c):
            if c % 2 == 0:
                x_rows[c // 2] = new_x("xr_%d" % c)
            nc.sync.dma_start(
                out=x_rows[c // 2][:, c % 2, :, :], in_=x[KP * c : KP * (c + 1), :].rearrange("(p j) l -> p j l", j=PACK)
            )

        s_by = p_scale.rearrange("o (c p t) -> p (o c) t", p=P, t=PACK)
        s_first = keep.tile([P, 2, 8], F32, name="s_first")
        s_rest = keep.tile([P, NC - 2, 8], F32, name="s_rest")

        def scales(c, passes=1):
            if c < 2:
                return s_first[:, c : c + passes, 0:PACK]
            return s_rest[:, c - 2 : c - 2 + passes, 0:PACK]

        load_p(0, 1, 0, 1)
        load_p(1, 1, 0, 1)
        nc.scalar.dma_start(out=s_first[:, :, 0:PACK], in_=s_by[:, 0:2, :])
        vs_rows = keep.tile([P, 2 * KP], U8, name="vs_rows", align_bytes=ALIGN)
        nc.sync.dma_start(out=vs_rows[:], in_=v_scales.rearrange("g q (h n) -> (g q h) n", h=4))
        load_p(2, 2, 0, 1)
        load_p(4, 1, 0, 2)
        load_x(0)
        load_p(0, 2, 1, 1)
        load_p(2, 2, 1, 1)
        for k in range(1, PERIODS):
            load_p(0, 2, 2 * k, 2)
            if k == 1:
                load_x(1)
            load_p(2, 2, 2 * k, 2)
            if k == 1:
                nc.sync.dma_start(out=s_rest[:, :, 0:PACK], in_=s_by[:, 2:NC, :])
            load_p(4, 1, 2 * k, 2)
            load_x(2 * k)
            load_x(2 * k + 1)
        for r, k in ((5, 0), (5, 1), (7, 0), (5, 2), (7, 1), (7, 2), (5, 3), (7, 3)):
            load_p(r, 2 if r == 5 else 1, 2 * k, 2)
        a_bf = keep.tile([P, NG, 16], BF16, name="a_bf")
        nc.sync.dma_start(out=a_bf[:, :, 0:PACK], in_=a.rearrange("(g m t) -> m g t", g=NG, t=PACK))
        g_bf = keep.tile([P, NC - PLAIN, 16], BF16, name="g_bf")
        nc.sync.dma_start(
            out=g_bf[:, :, 0:PACK], in_=g[KP * PLAIN : D].rearrange("(c m j) -> m c j", m=P, j=PACK)
        )

        vs = keep.tile([P, NG, D], U8, name="vs", align_bytes=MX_ALIGN)
        vs_turned = keep.tile([P, 2 * KP], U8, name="vs_turned", align_bytes=ALIGN)
        xq = keep.tile([P, NC, L], U32, name="xq", align_bytes=MX_ALIGN)
        xs = keep.tile([P, NC, L], U8, name="xs", align_bytes=MX_ALIGN)
        hq = keep.tile([P, NG, L], U32, name="hq", align_bytes=MX_ALIGN)
        hs = keep.tile([P, NG, L], U8, name="hs", align_bytes=MX_ALIGN)
        h_planes = [keep.tile([P, PACK, L], BF16, name="hp%d" % gg, align_bytes=ALIGN) for gg in range(NG)]
        h_packed = [keep.tile([P, L, PACK], BF16, name="hg%d" % gg, align_bytes=ALIGN) for gg in range(NG)]
        a_f = keep.tile([P, NG, PACK], F32, name="a_f")
        g_f = keep.tile([P, NC, PACK], F32, name="g_f")

        wide, turned, scaled, planes, pq, sums, done = {}, {}, {}, {}, {}, {}, {}
        widened = []

        def widen(copy=nc.scalar.copy, order="p n u q e"):
            t, units = pieces[len(widened)]
            widened.append(units)
            if len(units) > 2:
                w = work.tile([P, 4 * KP], BF16, name="w", tag="w4", bufs=5, align_bytes=ALIGN)
            else:
                w = work.tile([P, 2 * KP], BF16, name="w", tag="w2", bufs=4, align_bytes=ALIGN)
            copy(
                out=w[:, 0 : KP * len(units)].rearrange("p (n u q e) -> " + order, u=2, q=P, e=2),
                in_=t[:].rearrange("p r k -> p (r k)").bitcast(E4M3).rearrange("p (n q u e) -> " + order, u=2, q=P, e=2),
            )
            for i, u in enumerate(units):
                wide[u] = w[:, KP * i : KP * (i + 1)]

        def new_turned(n, b):
            if n in WORD_STEPS:
                return bank(b, [P, 2, 2, P])
            return bank(b, [P, PACK, 2, P], BF16)

        def turn_unit(dst, n, j):
            src = wide[UNITS[n][j]]
            if n in WORD_STEPS:
                words = src.bitcast(F32)
                for u in range(2):
                    nc.tensor.transpose(dst[:, u, j, :], words[:, P * u : P * (u + 1)], ident[:])
            else:
                for t in range(PACK):
                    nc.tensor.matmul(dst[:, t, j, :], lhsT=src[:, 2 * P * (t // 2) + t % 2 : 2 * P * (t // 2 + 1) : 2], rhs=ident_bf[:], start=True, stop=True)

        def turn(n, b=None):
            turned[n] = new_turned(n, FIRST + n % TURN_BANKS if b is None else b)
            for j in range(2):
                turn_unit(turned[n], n, j)

        def new_scaled(steps):
            t = work.tile([P, 4 * STEP, PACK], BF16, name="pg", tag="pg", bufs=4, align_bytes=ALIGN)
            for i, n in enumerate(steps):
                scaled[n] = t[:, STEP * i : STEP * (i + 1), :]
            return t

        packed = keep.tile([P, 2 * L, PACK], BF16, name="packed", align_bytes=ALIGN)

        def new_packed(steps):
            t = packed[:, L - P : 2 * L - P, :]
            for i, n in enumerate(steps):
                scaled[n] = t[:, STEP * i : STEP * (i + 1), :]
            return t

        def x_packed(c):
            first = 0 if c % 2 == 0 else L - X_SPLIT[c]
            return packed[:, first : first + L, :]

        def values(n, src):
            if n in WORD_STEPS:
                return src[:].bitcast(BF16).rearrange("p u j (m e) -> p j m u e", e=2)
            return src[:].rearrange("p (u e) j m -> p j m u e", e=2)

        def product_units(n, src, lo, hi):
            c, passes = UNITS[n][lo][1], UNITS[n][hi - 1][1] - UNITS[n][lo][1] + 1
            s = scales(c, passes).unsqueeze(2).to_broadcast([P, passes, P * (hi - lo) // passes, PACK])
            nc.vector.tensor_tensor(
                out=scaled[n][:, P * lo : P * hi, :].rearrange("p (c m) (u e) -> p c m u e", c=passes, e=2),
                in0=values(n, src)[:, lo:hi].rearrange("p j m u e -> p (j m) u e").rearrange("p (c m) u e -> p c m u e", c=passes),
                in1=s.rearrange("p c m (u e) -> p c m u e", e=2),
                op=MULT,
            )

        def product(n):
            product_units(n, turned[n], 0, 2)

        def product_planes(n):
            c = UNITS[n][0][1]
            planes[n] = work.tile([P, PACK, STEP], BF16, name="planes", tag="planes", bufs=2, align_bytes=ALIGN)
            for t in range(PACK):
                src = values(n, turned[n])[:, :, :, t // 2, t % 2].rearrange("p j m -> p (j m)")
                nc.scalar.activation(out=planes[n][:, t, :], in_=src, func=COPY, scale=scales(c)[:, 0, t : t + 1])

        def quant_p(src, units):
            q = work.tile([P, 2 * STEP], U32, name="pq", tag="pq", bufs=6, align_bytes=MX_ALIGN)
            sc = work.tile([P, 2 * STEP], U8, name="ps", tag="ps", bufs=6, align_bytes=MX_ALIGN)
            w = P * len(units)
            nc.vector.quantize_mx(
                out=q[:, 0:w].bitcast(E4M3X4), scales=sc[:, 0:w], in_=src[:, 0:w, :].rearrange("p m t -> p (m t)")
            )
            for i, u in enumerate(units):
                pq[u] = (q[:, P * i : P * (i + 1)], sc[:, P * i : P * (i + 1)])

        def both(*steps):
            return [(n, j) for n in steps for j in range(2)]

        def interleave(engine_copy, dst, src, lo, hi):
            engine_copy(
                out=dst[:, lo:hi, :].rearrange("p (c i) t -> p c t i", i=4),
                in_=src[:, :, lo:hi].rearrange("p t (c i) -> p c t i", i=4),
            )

        def gpsimd_copy(dst, src):
            nc.gpsimd.tensor_scalar(out=dst, in0=src, scalar1=1.0, scalar2=0.0, op0=MULT, op1=ADD)

        def interleave_gpsimd(dst, src, lo, hi):
            gpsimd_copy(dst[:, lo:hi, :], src[:, :, lo:hi].rearrange("p t l -> p l t"))

        def quant_x(c):
            nc.vector.quantize_mx(
                out=xq[:, c, :].bitcast(E4M3X4), scales=xs[:, c, :], in_=x_packed(c).rearrange("p l t -> p (l t)")
            )

        def mm(n, lo=0, hi=2):
            for j in range(lo, hi):
                r, c = UNITS[n][j]
                done[r] = done.get(r, 0) + 1
                if done[r] == 1:
                    sums[r] = bank(SUM_BANK[r], [P, L])
                nc.tensor.matmul_mx(
                    out=sums[r][:],
                    lhsT=pq[(n, j)][0].bitcast(E4M3X4),
                    lhsT_scale=pq[(n, j)][1],
                    rhs=xq[:, c, :].bitcast(E4M3X4),
                    rhs_scale=xs[:, c, :],
                    start=(done[r] == 1),
                    stop=(done[r] == NC),
                )

        def quant_h(gg, lo, hi):
            nc.vector.quantize_mx(
                out=hq[:, gg, lo:hi].bitcast(E4M3X4),
                scales=hs[:, gg, lo:hi],
                in_=h_packed[gg][:, lo:hi, :].rearrange("p l t -> p (l t)"),
            )

        def h_scalar(r, lo, hi):
            gg, t = r // PACK, r % PACK
            nc.scalar.activation(
                out=h_planes[gg][:, t, lo:hi], in_=sums[r][:, lo:hi], func=COPY, scale=a_f[:, gg, t : t + 1]
            )

        def h_vector(r, lo, hi):
            gg, t = r // PACK, r % PACK
            nc.vector.tensor_scalar(
                out=h_planes[gg][:, t, lo:hi],
                in0=sums[r][:, lo:hi],
                scalar1=a_f[:, gg, t : t + 1],
                scalar2=None,
                op0=MULT,
            )

        ident = keep.tile([P, P], F32, name="ident")
        nc.scalar.activation(out=ident[:], in_=ident_bf[:], func=COPY)
        for gg in range(NG):
            nc.vector.memset(vs[:, gg, :].bitcast(I32), 0)
        warm = bank(0, [P, PACK, P])
        for i in range(WARM_UPS):
            nc.tensor.matmul(warm[:], lhsT=g_rows[:], rhs=g_rows[:].unsqueeze(1).to_broadcast([P, PACK, P]), start=True, stop=True)
        first_banks = [new_turned(0, FIRST), new_turned(0, FIRST - 1)]
        widen(nc.vector.tensor_copy, "p n q u e")
        turn_unit(first_banks[0], 0, 0)
        widen()
        turn_unit(first_banks[1], 0, 1)
        nc.vector.tensor_copy(
            out=vs_turned[:].rearrange("p (c j m) -> p c j m", c=2, j=PACK),
            in_=vs_rows[:].rearrange("p (c m j) -> p c j m", c=2, j=PACK),
        )
        widen()
        turn(1)
        widen()
        turn(2)
        widen()
        widen()

        for q in range(4):
            nc.sync.dma_start(
                out=vs[32 * q : 32 * q + 4, :, 0 : KP * PLAIN].bitcast(I32),
                in_=v_scales[:, 4 * q : 4 * q + 4, 0 : KP * PLAIN].rearrange("g q n -> q g n").bitcast(I32),
            )
        for gg in range(NG):
            for q in range(4):
                for h in range(PLAIN // 2, 4):
                    row = 64 * gg + 16 * q + h
                    nc.sync.dma_start(
                        out=vs[32 * q : 32 * q + 4, gg, 2 * KP * h : 2 * KP * (h + 1)].bitcast(I32),
                        in_=vs_turned[row : row + 13 : 4, :].bitcast(I32),
                    )
        vw = keep.tile([P, NG, 2 * D], U8, name="vw", align_bytes=MX_ALIGN)
        for gg in range(NG):
            nc.sync.dma_start(out=vw[:, gg, :].bitcast(I32), in_=v_words[gg].bitcast(I32))
        nc.sync.dma_start(out=g_rows[0 : PACK * PLAIN, :], in_=g[0 : KP * PLAIN].rearrange("(i p) -> i p", p=P))

        def pack_x(c):
            lo = L - X_SPLIT[c] if c % 2 == 0 else 0
            interleave_gpsimd(x_packed(c), x_rows[c // 2][:, c % 2, :, :], lo, lo + X_SPLIT[c])

        def pack_x_rest(c):
            lo = 0 if c % 2 == 0 else X_SPLIT[c]
            interleave(nc.scalar.copy, x_packed(c), x_rows[c // 2][:, c % 2, :, :], lo, lo + L - X_SPLIT[c])

        for k in range(PERIODS):
            n, c = FIRST * k, 2 * k
            last = k == PERIODS - 1
            pg = new_scaled(range(n, n + 3))
            pack_x(c)
            pack_x_rest(c)
            if k == 0:
                for j in range(2):
                    product_units(0, first_banks[j], j, j + 1)
                turn(3)
            else:
                interleave(nc.scalar.copy, scaled[n], planes[n], 0, STEP)
                turn(n + 3)
                mm(n - 2)
            if not last:
                widen()
            pack_x_rest(c + 1)
            product(n + 1)
            turn(n + 4)
            if k > 0:
                mm(n - 1)
            if last:
                product_planes(n + 4)
            product(n + 2)
            turn(n + 5)
            if k > 0:
                mm(n - 3, 1, 2)
            quant_p(pg, both(n, n + 1))
            quant_x(c)
            quant_p(scaled[n + 2], both(n + 2))
            mm(n)
            pack_x(c + 1)
            pg = new_scaled(range(n + 3, n + 5 - last))
            widen()
            product(n + 3)
            mm(n + 1)
            turn(n + 6)
            if last:
                break
            widen()
            product_planes(n + 5)
            if k == PERIODS - 2:
                widen()
            product(n + 4)
            mm(n + 2, 0, 1)
            turn(n + 7)
            quant_x(c + 1)
            quant_p(pg, both(n + 3, n + 4))
        quant_x(c + 1)
        quant_p(pg, both(n + 3))
        mm(n + 2, 0, 1)
        turn(n + 7)
        mm(n + 2, 1, 2)
        x_plain = new_x("xn")
        for j in range(PLAIN):
            nc.sync.dma_start(out=x_plain[:, j, :, :], in_=x[KP * j : KP * (j + 1), :].rearrange("(i p) l -> p i l", p=P))

        n = 19
        pg = new_scaled((n + 1, n + 2))
        xg = new_packed((n,))
        interleave_gpsimd(scaled[n], planes[n], 0, STEP)
        nc.scalar.activation(out=a_f[:], in_=a_bf[:, :, 0:PACK], func=COPY)
        widen()
        widen()
        product_planes(n + 3)
        product(n + 1)
        turn(n + 4)
        mm(n - 1)
        h_scalar(4, 0, L)
        h_scalar(2, 0, L)
        product(n + 2)
        turn(n + 5)
        quant_p(xg, both(n))
        quant_p(pg, both(n + 1, n + 2))
        mm(n)
        turn(n + 6)
        mm(n + 1)

        n = 22
        pg = new_scaled((n + 1, n + 2))
        xg = new_packed((n,))
        interleave_gpsimd(scaled[n], planes[n], 0, STEP)
        widen()
        widen()
        product_planes(n + 3)
        widen()
        h_scalar(3, 0, L)
        product(n + 1)
        turn(n + 4)
        mm(n - 1)
        product(n + 2)
        turn(n + 5)
        quant_p(xg, both(n))
        quant_p(pg, both(n + 1, n + 2))
        mm(n)
        turn(n + 6)

        n = 25
        pg = new_scaled((n + 1, n + 3))
        xg = new_packed((n, n + 2))
        interleave_gpsimd(scaled[n], planes[n], 0, STEP)
        widen()
        product(n + 1)
        turn(n + 4)
        mm(n - 1)
        mm(n - 2)
        product_planes(n + 4)
        h_scalar(0, 0, L)
        h_scalar(1, 0, L)
        product(n + 2)
        turn(n + 5)
        product(n + 3)
        turn(n + 6)
        quant_p(xg, both(n, n + 2))
        quant_p(pg, both(n + 1, n + 3))
        mm(n)
        mm(n + 2)

        n = 29
        pg = new_scaled((n + 1, n + 2))
        xg = new_packed((n,))
        interleave_gpsimd(scaled[n], planes[n], 0, STEP)
        interleave(nc.scalar.copy, h_packed[0], h_planes[0], 0, L)
        product(n + 1)
        mm(n - 3)
        mm(n - 1)
        g_turned = bank(OUT_BANKS[0], [P, PACK * PLAIN])
        nc.tensor.matmul(g_turned[:], lhsT=g_rows[:], rhs=ident_bf[:, 0 : PACK * PLAIN], start=True, stop=True)
        nc.scalar.copy(out=g_f[:, 0:PLAIN, :].rearrange("p c j -> p (c j)"), in_=g_turned[:])
        nc.scalar.activation(out=g_f[:, PLAIN:NC, :], in_=g_bf[:, :, 0:PACK], func=COPY)
        product_units(n + 2, turned[n + 2], 0, 1)
        quant_p(scaled[n + 1], both(n + 1))
        quant_p(xg, both(n))
        mm(n + 1)
        mm(n)
        product_units(n + 2, turned[n + 2], 1, 2)
        for j in range(2):
            quant_p(scaled[n + 2][:, P * j : P * (j + 1), :], [(n + 2, j)])
            mm(n + 2, j, j + 1)

        quant_h(0, 0, L)
        for lo in (0, HALF):
            h_scalar(5, lo, lo + HALF)
            h_scalar(6, lo, lo + HALF)
        h_vector(7, 0, HALF)
        h_vector(7, HALF, L)
        interleave(nc.vector.tensor_copy, h_packed[1], h_planes[1], 0, HALF)
        interleave(nc.scalar.copy, h_packed[1], h_planes[1], H_SPLIT, L)
        interleave(nc.vector.tensor_copy, h_packed[1], h_planes[1], HALF, H_SPLIT)
        quant_h(1, 0, HALF)
        quant_h(1, HALF, L)

        tiles = PACK * NC
        order = sorted(range(1, tiles), key=lambda i: i - EARLY - 0.5 if i in SHARED[:2] else i)
        jobs = [(0, 0, HALF), (0, HALF, L)] + [(i, 0, L) for i in order]
        y, gx, o, words = {}, {}, {}, {}
        vw16 = vw[:].bitcast(U16)

        def reorder(c):
            words[c] = work.tile([P, NG, 2 * KP], U8, name="vp", tag="vp", bufs=3, align_bytes=MX_ALIGN)
            nc.scalar.copy(
                out=words[c][:].bitcast(U16).rearrange("p g (j m) -> p g j m", j=PACK),
                in_=vw16[:, :, KP * c : KP * (c + 1)].rearrange("p g (m j) -> p g j m", j=PACK),
            )

        def x_tile(i):
            c, j = divmod(i, PACK)
            if c < PLAIN:
                return x_plain[:, c, j, :]
            return x_rows[c // 2][:, c % 2, j, :]

        def y_pass(k, gg):
            i, lo, hi = jobs[k]
            c, j = divmod(i, PACK)
            if gg == 0:
                y[k] = bank(OUT_BANKS[k % BANKS], [P, hi - lo])
            if c < PLAIN:
                w = vw[:, gg, 2 * P * i : 2 * P * (i + 1)]
            else:
                w = words[c][:, gg, 2 * P * j : 2 * P * (j + 1)]
            nc.tensor.matmul_mx(
                out=y[k][:],
                lhsT=w.bitcast(E2M1X4),
                lhsT_scale=vs[:, gg, P * i : P * (i + 1)],
                rhs=hq[:, gg, lo:hi].bitcast(E4M3X4),
                rhs_scale=hs[:, gg, lo:hi],
                start=(gg == 0),
                stop=(gg == NG - 1),
            )

        def gained(i):
            gx[i] = work.tile([P, L], F32, name="gx", tag="gx", bufs=2)
            nc.scalar.activation(out=gx[i][:], in_=x_tile(i), func=COPY, scale=g_f[:, i // PACK, i % PACK : i % PACK + 1])

        reorder(PLAIN)
        gained(SHARED[0])
        for k in range(BANKS):
            y_pass(k, 0)
        made, stored = [], [0]
        for k in range(len(jobs)):
            i, lo, hi = jobs[k]
            c, j = divmod(i, PACK)
            y_pass(k, 1)
            if BANKS <= k + LEAD < len(jobs):
                y_pass(k + LEAD, 0)
            if c not in o:
                o[c] = work.tile([P, PACK, L], F32, name="o", tag="pg", bufs=4, align_bytes=ALIGN)
            dst = o[c][:, j, lo:hi]
            if i in SHARED:
                ys = work.tile([P, L], F32, name="ys", tag="ys", bufs=2)
                nc.scalar.copy(out=ys[:], in_=y[k][:])
                if i != SHARED[-1]:
                    gained(SHARED[SHARED.index(i) + 1])
                nc.gpsimd.tensor_tensor(out=dst, in0=gx[i][:], in1=ys[:], op=SUB)
            else:
                nc.vector.scalar_tensor_tensor(
                    out=dst, in0=x_tile(i)[:, lo:hi], scalar=g_f[:, c, j : j + 1], in1=y[k][:], op0=MULT, op1=SUB
                )
            made.append(i)
            if j == 1 and PLAIN < c + 2 < NC:
                reorder(c + 2)
            while stored[0] < PACK * PLAIN and stored[0] in made and stored[0] <= max(e for e in made if e not in SHARED):
                e = stored[0]
                nc.sync.dma_start(out=out[P * e : P * (e + 1), lo:hi], in_=o[e // PACK][:, e % PACK, lo:hi])
                if hi < L:
                    break
                stored[0] = e + 1
            if c < PLAIN:
                continue
            rows = 2 if c in PAIRED else PACK
            j0 = j - j % rows
            if all(PACK * c + e in made for e in range(j0, j0 + rows)):
                nc.sync.dma_start(
                    out=out[KP * c : KP * (c + 1), :].rearrange("(m j) l -> m j l", j=PACK)[:, j0 : j0 + rows, :],
                    in_=o[c][:, j0 : j0 + rows, :],
                )
